import numpy as np, ml_dtypes
CORES = [9,25,41,57]
N = 4
import mx_ref
BF = ml_dtypes.bfloat16
def gentries(a):
    return np.ascontiguousarray(a.reshape(8, 16, -1).transpose(0, 2, 1)).reshape(8, -1)
def gtable(e):
    e = np.asarray(e); return np.ascontiguousarray(e.reshape(8, -1, 16).transpose(0, 2, 1)).reshape(128, -1).astype(np.int32)
def gcols(t, e):
    v = np.concatenate([t.reshape(8, 16, -1, 4), np.zeros((8, 16, 1, 4), BF)], axis=2)
    return np.ascontiguousarray(np.stack([v[g][:, e[g]] for g in range(8)])).reshape(128, -1)
def gpick(z, e):
    return np.concatenate([z[16 * g:16 * g + 16][:, e[g]] for g in range(8)])
def tile(rs):
    return np.stack(rs, axis=2).reshape(128, -1).astype(BF)
def pick(q, e):
    c = np.concatenate([q[0].reshape(128, -1, 4), np.zeros((128, 1, 4), np.uint8)], axis=1); s = np.concatenate([q[1], np.ones((16, 1), np.uint8)], axis=1)
    return (np.ascontiguousarray(c[:, e].reshape(128, -1)), np.ascontiguousarray(s[:, e]))
def join(*qs):
    return (np.concatenate([q[0] for q in qs], axis=1), np.concatenate([q[1] for q in qs], axis=1))
def put(q, e, v):
    c, s = q[0].reshape(128, -1, 4).copy(), q[1].copy(); c[:, e] = v[0].reshape(128, -1, 4); s[:, e] = v[1]
    return (c.reshape(128, -1), s)
def pk(c, s):
    return (np.ascontiguousarray(c), mx_ref.live(s))
def emit(q):
    return q[0], q[1]
def packed(v, rng):
    q = [mx_ref.quantize(np.ascontiguousarray(v[r])) for r in range(N)]
    return np.stack([a for a, b in q]), np.stack([mx_ref.plane(b, rng) for a, b in q])
def values_of_codes():
    e, c = np.zeros((128, 128, 4), np.float32), np.zeros((128, 2, 4), np.uint8)
    e[np.arange(128), np.arange(128), 0] = 1
    c[:127, :, 0] = np.arange(256).reshape(2, 128).T[:127]
    return mx_ref.matmul(mx_ref.quantize(e.reshape(128, 512).astype(BF)), (c.reshape(128, 8), np.full((16, 2), 127, np.uint8))).T.reshape(-1).astype(np.float64)
CODE_VALUE, SCALE_VALUE = values_of_codes(), 2.0 ** (np.arange(256) - 127.0)
def decode(q):
    return (CODE_VALUE[q[0]].reshape(16, 8, -1, 4) * SCALE_VALUE[q[1]][:, None, :, None] + 0.0).reshape(128, -1).astype(np.float32)
def f(rng, *shape):
    return mx_ref.flush((rng.standard_normal(shape, dtype=np.float32) * np.exp2(rng.integers(-2, 3, shape[:-1] + (1,)))).astype(BF))
def wide(rng, *shape, cols=0):
    v = rng.standard_normal(shape, dtype=np.float32) * np.exp2(rng.integers(-12, 13, shape)).astype(np.float32)
    if cols: v *= np.repeat(np.exp2(rng.integers(-cols, cols + 1, shape[:-2] + (1, shape[-1] // 4))) * (rng.random(shape[:-2] + (1, shape[-1] // 4)) > 0.0625), 4, axis=-1).astype(np.float32)
    return mx_ref.flush(v.astype(BF))
C = 448
STEP = [1, 2, 3]
def at(t, e):
    return np.take_along_axis(t, e, axis=1)
def ext(e):
    return np.concatenate([e, np.full((len(e), 1), C)], axis=1)
def numbers_of(rng):
    return {"x": np.array(f(rng, N, 128, 4 * C)), "u": np.array(f(rng, N, 128, 512)), "v": np.array(f(rng, N, 128, 512))}
def trees(rng, kind, o=None):
    n, kind = 8 * N, kind.reshape(-1)
    t = np.arange(n)
    if o is None: o = rng.permuted(np.tile(np.arange(C), (n, 1)), axis=1)
    free = np.tile(np.arange(C + 1), (n, 1))
    e = np.full((3, n, C), C)
    for i in range(1, C):
        k = rng.integers(0, i + 1, n)
        side = np.where(kind == 1, rng.integers(0, 2, n), kind - 3)
        slot = np.where(kind == 0, free[t, k], np.where(kind == 2, i - 1, 2 * i - 2 + side))
        free[t, k] = 2 * i
        free[:, i + 1] = 2 * i + 1
        a = o[t, slot // 2]
        e[0, t, o[:, i]] = a
        e[1 + slot % 2, t, a] = o[:, i]
    return e.reshape(3, N, 8, C)
def depths(p):
    h = ext(p.reshape(8 * N, C))
    d = (h < C).astype(np.int64)
    for k in range(9):
        d = d + at(d, h)
        h = at(h, h)
    return d[:, :C].reshape(N, 8, C)
def stored(e):
    return {k: np.stack([gtable(e[i, r]) for r in range(N)]) for i, k in enumerate(("up", "lf", "rt"))}
def lists(rng):
    return stored(trees(rng, np.zeros((N, 8), np.int64)))
def mixed(rng):
    return np.stack([rng.permutation([0, 0, 0, 1, 1, 2, 3, 4]) for r in range(N)])
def layers(rng, still=[]):
    w = np.array(f(rng, N, 128, 2048)).reshape(N, 8, 16, 4, 8, 16, 4)
    for i in still:
        w[:, :, i] = 0
        w[:, :, :, :, :, i] = 0
    return w
def weights(rng, w):
    c, p = packed(np.ascontiguousarray(w).reshape(N, 128, 2048), rng)
    return {"wc": c, "ws": p}
def setup_inputs(rng):
    return {**numbers_of(rng), **lists(rng), **weights(rng, layers(rng))}
def setup_inputs_ties(rng):
    d = numbers_of(rng)
    o = rng.permutation(N) % 4
    kind = mixed(rng)
    kind[o == 3] = 1
    e = trees(rng, kind)
    h = depths(e[0])
    k = rng.integers(0, 4, (N, 8, C))
    k[o == 0] = 5
    k[o == 1] = h[o == 1]
    k[o == 3] = h[o == 3] % 3 == 1
    x = d["x"].reshape(N, 8, 16, C, 4)
    x[:, :, :3] = 0
    u = d["u"].reshape(N, 128, 128, 4)
    u[:, :, ::16] = 0
    for i in range(3):
        x[:, :, i, :, 0] = (k // 8 ** i % 8).astype(np.float32).astype(BF)
        for c in range(0, 128, 16): u[:, c + i, c, 0] = 8.0 ** i
    return {"x": x.reshape(N, 128, 4 * C), "u": u.reshape(N, 128, 512), "v": d["v"], **stored(e), **weights(rng, layers(rng, [0, 1, 2]))}
def setup_inputs_near(rng):
    d = numbers_of(rng)
    x = d["x"].astype(np.float32).reshape(N, 8, 16, C, 4)
    x[:, :, 0] = 0
    x[:, :, 8:] = 0
    u = d["u"].reshape(N, 128, 128, 4)
    u[:, :, ::16] = 0
    o = (np.arange(N) + rng.integers(4)) % 4
    for r in range(N):
        c = np.where(rng.permutation(8)[:, None] < 4, rng.choice([-1.0, 1.0], (8, 1)), rng.choice([-1.0, 1.0], (8, C)))
        s = rng.integers(0, 16, (8, C))
        digits = ((s[:, :, None] >> np.arange(4)) & 1) * np.exp2(np.arange(4) - 23.0)
        if o[r] < 2:
            x[r, :, 0, :, 0] = c
            x[r, :, 8] = digits
            x[r, :, 11, :, 0] = c * 2.0 ** -10
        elif o[r] == 2: x[r, :, 8] = digits * rng.choice([-1.0, 1.0], (8, C, 1))
        else:
            a = rng.choice([-1.0, 1.0], (8, 1)) * 2.0 ** -30
            x[r, :, 8, :, 0] = np.where(s < 8, 1.25, 0.0) * a
            x[r, :, 9, :, 0] = np.where(s < 8, 0.0, 1.125) * a
            for g in rng.permutation(8)[:4]:
                e = rng.choice([-1.0, 1.0], C) * 2.0 ** -30
                x[r, g, 8, :, 0] = 1.25 * e
                x[r, g, 9, :, 0] = -1.125 * e
        if o[r] > 1: x[r, :, 12, :, 0] = rng.choice([1.0, 1.5], (8, C)) * 2.0 ** -30
        place = [0, C - 1, int(rng.integers(C)), int(rng.integers(C))]
        for g, j in zip(rng.permutation(8)[:4], place): x[r, g, 0, j, 0] = 2.0 ** 29 * rng.choice([-1.0, 1.0])
        k = 1.0 if o[r] == 0 else 2.0 ** -30
        for h in range(0, 128, 16):
            u[r, h, h, 0] = k if o[r] < 2 else 1.0
            if o[r] < 2: u[r, h + 11, h, 0] = k
            if o[r] < 3: u[r, h + 8, h] = k
            else:
                u[r, h + 8, h, 0] = k
                u[r, h + 9, h, 0] = 1.125 * k
                u[r, h + 10, h, 0] = k
    w = layers(rng, [0, 8, 9, 10, 11, 12, 13, 14, 15])
    for g in range(8): w[:, g, 12, 0, g, 10, 0] = 2.0 ** -8
    return {"x": x.reshape(N, 128, 4 * C).astype(BF), "u": u.reshape(N, 128, 512), "v": d["v"], **stored(trees(rng, mixed(rng))), **weights(rng, w)}
def setup_inputs_odd(rng):
    d = numbers_of(rng)
    o = rng.permutation(N) % 2
    x = (1.0 + (2 * rng.integers(0, 64, (N, 16, 8, C, 4)) + 1) * 2.0 ** -7) * np.exp2(-rng.integers(0, 7, (N, 16, 8, C, 4)).astype(np.float64)) * rng.choice([-1.0, 1.0], (N, 16, 8, C, 4))
    x[:, :, 0, :, 0] = rng.choice([1.96875, 1.875], (N, 16, C)) * 2.0 ** 8 * rng.choice([-1.0, 1.0], (N, 16, 1))
    u = d["u"].reshape(N, 16, 8, 128, 4)
    u[:, :, 0, ::16] = 0
    for r in range(N):
        if o[r]: continue
        for g, i in enumerate(rng.permutation(8) % 2):
            x[r, 2 * g, 1, :, 0] = (8 + rng.integers(0, 2, C)) * 2.0 ** (i - 8.0)
            u[r, :, :, 16 * g] = 0
            u[r, 2 * g, 1, 16 * g, 0] = 1.0
    return {"x": x.astype(np.float32).reshape(N, 128, 4 * C).astype(BF), "u": u.reshape(N, 128, 512), "v": d["v"], **lists(rng), **weights(rng, layers(rng, [0, 8]))}
def setup_inputs_ends(rng):
    d = numbers_of(rng)
    o = (np.arange(N) + rng.integers(4)) % 4
    big = (o < 2)[:, None, None, None]
    def sized(*n):
        return np.where(big, (0.955 + 0.02 * rng.random((N,) + n)) * 2.0 ** 30, (1.0 + 0.125 * rng.integers(0, 8, (N,) + n)) * 2.0 ** -30)
    s = rng.choice([-1.0, 1.0], (N, 128, C, 4))
    s[o == 1] = rng.choice([-1.0, 1.0], (N, 1, C, 1))[o == 1]
    s[o == 3] = rng.choice([-1.0, 1.0], (N, 128, 1, 4))[o == 3]
    s[o % 2 == 0] = -1
    x = s * sized(128, C, 4)
    h = np.stack([rng.permutation(8) for r in range(N)])
    u = d["u"].reshape(N, 128, 128, 4)
    u[:, :, ::16] = (np.where(h < 2, 0.0, h % 2 * 2.0 - 1.0)[:, None, :, None] * sized(128, 8, 4)).astype(np.float32).astype(BF)
    v = rng.choice([-1.0, 1.0], (N, 128, 128, 4)) * sized(128, 128, 4)
    w = np.zeros((N, 128, 4, 128, 4), np.float32)
    i = np.arange(128)
    for b in range(4): w[:, i, b, i, b] = np.array([-0.125, -0.125, -2.0 ** -8, 2.0 ** 4])[o][:, None]
    kind = np.stack([rng.permutation([0, 1, 2, 2, 3, 3, 4, 4]) for r in range(N)])
    fall = np.stack([rng.permutation(8) % 2 for r in range(N)]).reshape(-1, 1)
    k = np.tile(np.arange(C), (8 * N, 1))
    return {"x": x.astype(np.float32).reshape(N, 128, 4 * C).astype(BF), "u": u.reshape(N, 128, 512), "v": v.astype(np.float32).reshape(N, 128, 512).astype(BF), **stored(trees(rng, kind, np.where(fall == 0, k, C - 1 - k))), **weights(rng, w.astype(BF))}
def setup_inputs_spread(rng):
    d = setup_inputs(rng)
    d["x"] = wide(rng, N, 128, 4 * C, cols=6)
    return d
def check_inputs(d):
    b = []
    for k in ("x", "u", "v"):
        a = np.abs(d[k].astype(np.float32))
        if not (np.isfinite(a).all() and ((a == 0) | (a >= 2.0 ** -30) & (a <= 2.0 ** 30)).all()): b.append("a value of " + k)
    bad = [k for k in ("up", "lf", "rt") if not ((d[k] >= 0) & (d[k] <= C)).all()]
    b += ["an entry of " + k for k in bad]
    none, least, most = [emit(mx_ref.quantize(np.full((128, 16), k, np.float32).astype(BF)))[1][0, 0] for k in (0.0, 2.0 ** -8, 2.0 ** 8)]
    own = np.arange(C + 1)
    for r in range(N):
        if ((d["wc"][r] == 0x7F) | (d["wc"][r] == 0xFF)).any(): b.append("wc: a code that is no number")
        s = mx_ref.live(d["ws"][r])
        if ((s != none) & ((s < least) | (s > most))).any(): b.append("ws: a scale out of range")
        if bad: continue
        p, l, e = [ext(gentries(d[k][r])) for k in ("up", "lf", "rt")]
        ok = (np.sum(p[:, :C] == C, axis=1) == 1).all() and (np.sum(l < C, axis=1) + np.sum(e < C, axis=1) == C - 1).all()
        ok = ok and ((l == C) | (l != e)).all() and all(((k == C) | (at(p, k) == own)).all() for k in (l, e))
        for k in range(9): p = at(p, p)
        if not (ok and (p == C).all()): b.append("up, lf, rt: not a tree")
    return b
def rotated(s, p, l, r):
    own = np.tile(np.arange(C + 1), (8, 1))
    w = np.concatenate([s, np.zeros((8, 1), np.float32)], axis=1)
    gain = np.where(p < C, np.maximum(w - at(w, p), np.float32(0)), np.float32(0))
    def better(a, b):
        i, j = at(gain, a), at(gain, b)
        return np.where((i > j) | (i == j) & (a < b), a, b)
    child = better(l, r)
    best = better(better(own, child), better(at(child, l), at(child, r)))
    z = at(p, p)
    g, v = np.nonzero((gain > 0) & (best == own) & (at(best, p) == own) & ((z == C) | (at(best, z) == own)))
    y, z = p[g, v], z[g, v]
    left, high = l[g, y] == v, l[g, z] == y
    c = np.where(left, r[g, v], l[g, v])
    a, b, e = p.copy(), l.copy(), r.copy()
    a[g, c], a[g, y], a[g, v] = y, v, z
    b[g, y], e[g, y] = np.where(left, c, l[g, y]), np.where(left, r[g, y], c)
    b[g, v], e[g, v] = np.where(left, l[g, v], y), np.where(left, y, r[g, v])
    b[g, z], e[g, z] = np.where(high, v, l[g, z]), np.where(high, r[g, z], v)
    for k in (a, b, e): k[:, C] = C
    return a, b, e
def reference(x, u, v, up, lf, rt, wc, ws):
    qu = [mx_ref.quantize(u[r]) for r in range(N)]
    lay = [pk(wc[r], ws[r]) for r in range(N)]
    link = [[ext(gentries(k[r])) for k in (up, lf, rt)] for r in range(N)]
    now = [x[r] for r in range(N)]
    for step in STEP:
        t, par, z = [], [], []
        for r in range(N):
            q = mx_ref.quantize(now[r])
            link[r] = rotated(mx_ref.matmul(qu[r], q)[::16] + np.float32(0.0), *link[r])
            p = link[r][0][:, :C]
            a = np.where(p == C, np.arange(C), p)
            t.append(decode(q))
            par.append(a)
            m = t[r].astype(BF)
            z.append(mx_ref.quantize(((gcols(m, a).astype(np.float32) + gcols(m, at(a, a)).astype(np.float32)) * np.float32(0.5)).astype(BF)))
        for r in range(N):
            now[r] = tile([gpick(mx_ref.matmul(pick(lay[r], np.arange(128 * b, 128 * b + 128)), z[(r - step) % N]) * np.float32(0.03125), par[r]) + t[r][:, b::4] for b in range(4)])
    y, tr = np.zeros((N, 128, C), np.float32), np.zeros((N, 8, 3 * C), np.float32)
    oc, osc = np.zeros((N, 128, 4 * C), np.uint8), np.zeros((N, 16, C), np.uint8)
    for r in range(N):
        q = mx_ref.quantize(now[r])
        y[r] = mx_ref.matmul(mx_ref.quantize(v[r]), q)
        tr[r] = np.concatenate([k[:, :C] for k in link[r]], axis=1)
        oc[r], osc[r] = emit(q)
    return {"y": y, "tr": tr, "oc": oc, "osc": osc}

@@ -1,0 +1,527 @@
+from concourse.mybir import dt, AluOpType, ActivationFunctionType
+
+N = 4
+C = 448
+H = 224
+STEP = [1, 2, 3]
+BIGV = 3.0e29
+
+F32, BF, U16, I32, CODE, PLANE = "float32", "bfloat16", "uint16", "int32", "float8_e4m3fn_x4", "uint8"
+SCRATCH = {"ps": ("psum", [128, 4096], F32)}
+
+
+def _sbuf(names, n, dtype):
+    for k in names.split():
+        SCRATCH[k] = ("sbuf", [128, n], dtype)
+
+
+_sbuf("xt xn zt", 4 * C, BF)
+_sbuf("ut vt ones et0 et1 et2 et3", 512, BF)
+_sbuf("uq vq", 128, CODE)
+_sbuf("us vs", 128, PLANE)
+_sbuf("wq eq", 512, CODE)
+_sbuf("wp es", 512, PLANE)
+_sbuf("zq q0 q1 q2 q3 aq0 aq1 aq2", C, CODE)
+_sbuf("zs qs0 qs1 qs2 qs3 as0 as1 as2", C, PLANE)
+_sbuf("pidx", 2, I32)
+_sbuf("ti", 16, I32)
+_sbuf("c224", 8, F32)
+_sbuf("offm", 4, U16)
+_sbuf("upi lfi rti", 28, I32)
+_sbuf("al0 al1 al2", 28, U16)
+_sbuf("lup la0 la1 la2 la3", 32, U16)
+_sbuf("lb0 lb1", 64, U16)
+_sbuf("iot prow rrow ra qrow rrep", 464, BF)
+_sbuf("srow urow", 456, F32)
+_sbuf("nT lrow raa pT lT rT raT raaT pp ppT qa qaa qaaa ql qr qaT qaaT qaaaT qlT qrT repl repr_ replT reprT rp2", C, BF)
+_sbuf("sa sl sr sT saT slT srT ulT urT trf yt rr0 rr1 rr2 rr3", C, F32)
+_sbuf("wu", C, F32)
+_sbuf("wc_ wr zr", C, BF)
+_sbuf("ba0 ba1 bl0 bl1", C + 480, BF)
+_sbuf("rw rw2", 512, BF)
+_sbuf("m3 v3", 84, F32)
+_sbuf("cb", 28 * 80, F32)
+_sbuf("fo0 fo1 fo2 fo3 fp0 fp1 fp2 fp3", C, BF)
+_sbuf("fq kb", 4 * C, BF)
+
+SEMAPHORES = (["cv", "cs", "ct", "cg", "sent"] + ["ld_" + k for k in "x u v up lf rt wc ws z".split()]
+              + ["st_" + k for k in "y oc osc tr".split()] + ["cf%d" % k for k in range(4)] + ["arq%d" % k for k in range(3)] + ["arl%d" % k for k in range(3)])
+
+
+def rank_program(g, core, T, topo):
+    rank = T.rank_of(core)
+    if rank is None:
+        return
+    A = AluOpType
+    ACT = ActivationFunctionType
+    V, S = g.vector, g.scalar
+    queue = {"v": V, "s": S, "t": g.tensor, "g": g, "y": g.sync}
+
+    count = {}
+    seen = {k: {} for k in queue}
+    facts = {}
+    writer, readers = {}, {}
+
+    def wait(q, sem, val):
+        s = seen[q]
+        if s.get(sem, 0) >= val:
+            return
+        queue[q].wait_ge(T.sem[sem], val)
+        s[sem] = val
+        for k, n in facts.get((sem, val), {}).items():
+            if s.get(k, 0) < n:
+                s[k] = n
+
+    def prepare(q, reads, writes):
+        need = {}
+        for k in reads + writes:
+            if k in writer:
+                w, n, wq = writer[k]
+                need[w] = max(need.get(w, 0), n)
+        for k in writes:
+            for w, n, rq in readers.get(k, []):
+                if rq != q or w[0] != "c":
+                    need[w] = max(need.get(w, 0), n)
+        own = "c" + q
+        for w in sorted(need, key=lambda w: (w == own, w)):
+            wait(q, w, need[w])
+
+    def note(q, sem, val, reads, writes):
+        facts[(sem, val)] = dict(seen[q])
+        for k in writes:
+            writer[k] = (sem, val, q)
+            readers[k] = []
+        for k in reads:
+            readers.setdefault(k, []).append((sem, val, q))
+
+    def op(q, fn, reads, writes):
+        prepare(q, reads, writes)
+        sem = "c" + q
+        count[sem] = count.get(sem, 0) + 1
+        fn().then_inc(T.sem[sem], 1)
+        note(q, sem, count[sem], reads, writes)
+
+    def dma(q, sem, out, in_, reads, writes):
+        prepare(q, reads, writes)
+        count[sem] = count.get(sem, 0) + 16
+        queue[q].dma_start(out, in_).then_inc(T.sem[sem], 16)
+        note(q, sem, count[sem], reads, writes)
+
+    def send(dst, rsem, out, in_, reads):
+        prepare("g", reads, [])
+        rid, pid, se = topo.addr(dst)
+        g.remote_dma(out, in_, T.sem[rsem], T.sem["sent"], pid, rid, topo.mask(core, dst))
+        count["sent"] = count.get("sent", 0) + len(topo.engines(core, dst))
+
+    def ps(b, n=C):
+        return T.ps[:, 512 * b:512 * b + n]
+
+    slots = {}
+
+    def slot(name):
+        i = slots.setdefault(name, len(slots))
+        return T.cb[:, 28 * i:28 * i + 28], "cb." + name
+
+    def plane(buf, lane):
+        return T[buf][:, lane:C:16], buf
+
+    def sub(buf, lane):
+        return T[buf][:, lane:C:16], "%s.%d" % (buf, lane)
+
+    def tt(out, a, b, o):
+        op("v", lambda: V.tensor_tensor(out[0], a[0], b[0], o), [a[1], b[1]], [out[1]])
+        return out
+
+    def ts(out, a, s1, o1, s2=None, o2=None):
+        if o2 is None:
+            op("v", lambda: V.tensor_scalar(out[0], a[0], s1, None, o1), [a[1]], [out[1]])
+        else:
+            op("v", lambda: V.tensor_scalar(out[0], a[0], s1, s2, o1, o2), [a[1]], [out[1]])
+        return out
+
+    def turn(out, ok, in_, ik):
+        op("v", lambda: V.transpose(out, in_), ik, ok)
+
+    def turned(out, in_):
+        turn(T[out][:], [out], T[in_][:, 0:C], [in_])
+
+    def gather(q, out, win, wk, off, fk):
+        if q == "s":
+            op("s", lambda: S.activation(out[0], win.indirect(off), ACT.Copy), wk + [fk], [out[1]])
+        else:
+            op("v", lambda: V.tensor_copy(out[0], win.indirect(off)), wk + [fk], [out[1]])
+
+    def row(buf):
+        return T[buf][:], buf
+
+    def memset(ap, val, keys):
+        op("v", lambda: V.memset(ap, val), [], keys)
+
+    def mm(bank, l, ls, r, rs, keys, n=C):
+        op("t", lambda: g.tensor.matmul_mx(ps(bank, n), l, ls, r, rs, True, True), keys, ["ps%d" % bank])
+
+    def quantize(out, os, in_, reads, writes):
+        op("v", lambda: V.quantize_mx(out, os, in_), reads, writes)
+
+    def blk(buf, b):
+        return T[buf][:, 128 * b:128 * b + 128]
+
+    todo = []
+
+    def fill(n=1):
+        for _ in range(n):
+            if todo:
+                todo.pop(0)()
+
+    dma("y", "ld_up", T.upi[:], T.up[:], [], ["upi"])
+    dma("s", "ld_rt", T.rti[:], T.rt[:], [], ["rti"])
+    dma("s", "ld_lf", T.lfi[:], T.lf[:], [], ["lfi"])
+    dma("y", "ld_x", T.xt[:], T.x[:], [], ["xt"])
+    dma("y", "ld_u", T.ut[:], T.u[:], [], ["ut"])
+    dma("y", "ld_wc", T.wq[:, 0:512].bitcast(dt.uint8), T.wc[:], [], ["wq"])
+    dma("y", "ld_ws", T.wp[:, 0:512], T.ws[:], [], ["wp"])
+    dma("y", "ld_v", T.vt[:], T.v[:], [], ["vt"])
+
+    op("g", lambda: g.iota(T.pidx[:], [[0, 2]], 0, 1), [], ["pidx"])
+    memset(T.ones[:], 1.0, ["ones"])
+    op("g", lambda: g.iota(T.iot[:], [[1, 464]], -224, 0, allow_small_or_imprecise_dtypes=True), [], ["iot"])
+    op("g", lambda: g.affine_select(T.et0[:], T.ones[:], [[-1, 512]], A.is_equal, 0.0, 0, 4), ["ones"], ["et0"])
+    for b in range(1, 4):
+        memset(T["et%d" % b][:, 0:b], 0.0, ["et%d.0" % b])
+    op("s", lambda: S.activation(T.wu[:], T.iot[:, 0:C], ACT.Copy, scale=0.0), ["iot"], ["wu.0", "wu.1", "wu.i"])
+    op("s", lambda: S.activation(T.zr[:], T.iot[:, 0:C], ACT.Copy, scale=0.0), ["iot"], ["zr"])
+    for b in range(1, 4):
+        op("s", lambda: S.activation(T["et%d" % b][:, b:512], T.et0[:, 0:512 - b], ACT.Copy), ["et0"], ["et%d" % b])
+    memset(T.ba0[:, 0:C], 0.0, ["ba0.0", "ba0.i"])
+    memset(T.rw[:, 0:32], 0.0, ["rw.p0"])
+    memset(T.rw[:, 480:512], 0.0, ["rw.p1"])
+    for k in ("prow", "rrow", "ra"):
+        memset(T[k][:, C:464], 224.0, [k + ".n"])
+    memset(T.srow[:, C:456], -BIGV, ["srow.n"])
+    memset(T.urow[:, C:456], BIGV, ["urow.n"])
+    memset(T.qrow[:, C:464], 600.0, ["qrow.n"])
+    memset(T.c224[:, 0:4], 224.0, ["c224"])
+    memset(T.c224[:, 4:8], -256.0, ["cm256"])
+
+    def tiv(i):
+        return T.ti[:, i:i + 1], "ti%d" % i
+    pd = (T.pidx[:, 0:1], "pidx")
+    ts(tiv(0), pd, 1, A.logical_shift_right, 7, A.bitwise_and)
+    ts(tiv(1), pd, 1, A.bitwise_and)
+    ts(tiv(2), pd, 4, A.logical_shift_right, 1, A.bitwise_and)
+    ts(tiv(4), tiv(0), 32, A.mult)
+    tt(tiv(3), tiv(1), tiv(2), A.mult)
+    ts(tiv(5), tiv(1), 480, A.mult)
+    ts(tiv(6), tiv(2), 464, A.mult)
+    ts(tiv(7), tiv(3), -928, A.mult)
+
+    def turned_back(big, rw, lanes, between=None):
+        turn(T[rw][:, 32:480], [rw], T[big][:, 0:C], ["%s.%s" % (big, k) for k in lanes] + [big + ".i"])
+        if between:
+            between()
+        turn(T[big][:, C:928], [big + ".s"], T[rw][:, 16:496], [rw, rw + ".p0", rw + ".p1"])
+
+    def make_list(out, big, lanes):
+        op("v", lambda: V.tensor_scalar(T[out][:], T[big][:, 0:928].indirect(T.offm[:, 0:2 * len(lanes)]), 224.0, None, A.add),
+           ["%s.%d" % (big, i) for i in lanes] + [big + ".i", big + ".s"] + ["offm%d" % i for i in lanes], [out])
+
+    op("v", lambda: V.tensor_copy(T.lup[:, 0:28], T.upi[:]), ["upi"], ["lup"])
+    op("v", lambda: V.tensor_copy(T.lb0[:, 32:60], T.rti[:]), ["rti"], ["lb0.r"])
+    op("v", lambda: V.tensor_copy(T.lb0[:, 0:28], T.lfi[:]), ["lfi"], ["lb0.l"])
+    lup = T.lup[:, 0:28]
+    gather("v", (T.prow[:, 0:C], "prow"), T.iot[:], ["iot"], lup, "lup")
+    gather("s", (T.rrow[:, 0:C], "rrow"), T.iot[:], ["iot"], T.lb0[:, 32:60], "lb0.r")
+    gather("s", row("lrow"), T.iot[:], ["iot"], T.lb0[:, 0:28], "lb0.l")
+    gather("s", (T.ra[:, 0:C], "ra"), T.rrow[:], ["rrow", "rrow.n"], lup, "lup")
+    tt(tiv(8), tiv(4), tiv(5), A.add)
+    tt(tiv(9), tiv(6), tiv(7), A.add)
+    turned("pT", "prow")
+    tt(tiv(10), tiv(8), tiv(9), A.add)
+    nv = plane("nT", 0)
+    turned("nT", "iot")
+    pT = plane("pT", 0)
+    e = ts(slot("i0"), pT, 224.0, A.is_equal)
+    f_ = tt(slot("i1"), nv, pT, A.subtract)
+    ts((T.offm[:, 0:1], "offm0"), tiv(10), 0, A.add, 927, A.min)
+    f_ = tt(slot("i2"), e, f_, A.mult)
+    ts((T.offm[:, 1:2], "offm0"), tiv(10), 256, A.add, 927, A.min)
+    tt(sub("ba0", 0), pT, f_, A.add)
+
+    def quantize_constants(b):
+        quantize(blk("eq", b), blk("es", b), T["et%d" % b][:], ["et%d" % b] + (["et%d.0" % b] if b else []), ["eq%d" % b])
+    ts((T.offm[:, 2:3], "offm1"), tiv(10), 1, A.add, 927, A.min)
+    turned_back("ba0", "rw", [0], lambda: ts((T.offm[:, 3:4], "offm1"), tiv(10), 257, A.add, 927, A.min))
+    quantize_constants(0)
+    make_list("la0", "ba0", [0])
+    for b in range(1, 4):
+        quantize_constants(b)
+    quantize(T.uq[:], T.us[:], T.ut[:], ["ut"], ["uq"])
+    zeros = {"wc_": ["wc_.0", "wc_.i"], "ba1": ["ba1.0", "ba1.i"], "wr": ["wr.0", "wr.i"],
+             "bl1": ["bl1.0", "bl1.1", "bl1.2", "bl1.i"], "bl0": ["bl0.0", "bl0.1", "bl0.2", "bl0.i"]}
+    for k in zeros:
+        dma("y", "ld_z", T[k][:, 0:C], T.zr[:], ["zr"], [])
+    for k in zeros:
+        for key in zeros[k]:
+            writer[key] = ("ld_z", count["ld_z"], "y")
+    facts[("ld_z", count["ld_z"])] = {}
+    quantize(T.q0[:], T.qs0[:], T.xt[:], ["xt"], ["q0"])
+    turned("rT", "rrow")
+    turned("lT", "lrow")
+    lv, rv = plane("lT", 0), plane("rT", 0)
+
+    def m3(i):
+        return T.m3[:, 28 * i:28 * i + 28], "m3.%d" % i
+
+    def v3(i):
+        return T.v3[:, 28 * i:28 * i + 28], "v3.%d" % i
+    ts(m3(0), nv, -256.0, A.add)
+    ts(m3(1), lv, -256.0, A.add)
+    ts(m3(2), rv, -256.0, A.add)
+
+    def late_constants():
+        memset(T.rrep[:, C:464], 224.0, ["rrep.n"])
+        memset(T.rw2[:, 0:32], 0.0, ["rw2.p0"])
+        memset(T.rw2[:, 480:512], 0.0, ["rw2.p1"])
+
+    def derive(k, pv, sv, lv, rv):
+        def add(f, *a):
+            todo.append(lambda: f(*a))
+        spv = slot("sp")
+        if k == 0:
+            ppv = plane("ppT", 0)
+            for n in ("raT raaT ppT").split():
+                add(turned, n, n[:-1])
+            add(tt, sv, plane("raT", 0), nv, A.is_equal)
+            add(tt, spv, plane("raaT", 0), pv, A.is_equal)
+            add(ts, slot("d0"), ppv, 224.0, A.is_equal)
+        else:
+            ppv = plane("ppT", 2)
+            add(turned, "ppT", "pp")
+            add(tt, sv, plane("ppT", 0), nv, A.not_equal)
+            add(tt, slot("d0"), ppv, pv, A.is_equal)
+            add(turned, "raaT", "raa")
+            add(tt, spv, plane("raaT", 0), pv, A.not_equal)
+        add(tt, slot("d1"), nv, ppv, A.subtract)
+        add(tt, slot("d2"), sv, spv, A.is_equal)
+        add(tt, slot("d3"), lv, rv, A.subtract)
+        add(tt, slot("d4"), slot("d0"), slot("d1"), A.mult)
+        add(ts, slot("d5"), slot("d2"), 2048.0, A.mult)
+        add(tt, slot("d6"), sv, slot("d3"), A.mult)
+        add(tt, slot("d7"), ppv, slot("d4"), A.add)
+        add(tt, slot("pin"), slot("d5"), pv, A.add)
+        add(tt, slot("d8"), rv, slot("d6"), A.add)
+        add(tt, slot("dz"), slot("d7"), pv, A.subtract)
+        add(tt, slot("cn"), slot("d8"), nv, A.subtract)
+
+    pv, sv = sub("ba0", 0), slot("side")
+    for k in range(3):
+        par, nxt = k % 2, 1 - k % 2
+        last = k == 2
+        q, qs, qk = T["q%d" % k], T["qs%d" % k], "q%d" % k
+        dst = T.cores[(rank + STEP[k]) % N]
+        la, lak = T["la%d" % k][:, 0:28], "la%d" % k
+        ll, llk = T["lb%d" % par][:, 0:28], ["lb%d" % par, "lb0.l"][k == 0]
+        lr, lrk = T["lb%d" % par][:, 32:60], ["lb%d" % par, "lb0.r"][k == 0]
+        lak2 = "la%d" % (k + 1)
+        la2 = T[lak2][:, 0:28]
+        send(dst, "arq%d" % k, T["aq%d" % k][:, 0:C].bitcast(dt.uint8), q[:, 0:C].bitcast(dt.uint8), [qk])
+        send(dst, "arq%d" % k, T["as%d" % k][:, 0:C], qs[:, 0:C], [qk])
+        mm(0, T.uq[:], T.us[:], q[:, 0:H], qs[:, 0:H], ["uq", qk], H)
+        mm(7, T.uq[:], T.us[:], q[:, H:C], qs[:, H:C], ["uq", qk], H)
+        for b in range(4):
+            mm(1 + b, blk("eq", b), blk("es", b), q[:], qs[:], ["eq%d" % b, qk])
+        if k:
+            derive(k, pv, sv, lv, rv)
+            fill(3)
+        op("v", lambda: V.tensor_copy(T.srow[:, 0:H], ps(0, H)), ["ps0"], ["srow.a"])
+        op("s", lambda: S.activation(T.srow[:, H:C], ps(7, H), ACT.Copy), ["ps7"], ["srow.b"])
+        sk = ["srow.a", "srow.b", "srow.n"]
+        gather("s", row("sl"), T.srow[:, 0:456], sk, ll, llk)
+        gather("s", row("sr"), T.srow[:, 0:456], sk, lr, lrk)
+        if k:
+            for i, w in ((1, lv), (2, rv)):
+                op("s", lambda: S.activation(m3(i)[0], w[0], ACT.Identity, bias=T.c224[:, 4:5]), [w[1], "cm256"], [m3(i)[1]])
+        else:
+            gather("s", row("raa"), T.ra[:], ["ra", "ra.n"], lup, "lup")
+            gather("s", row("pp"), T.prow[:], ["prow", "prow.n"], lup, "lup")
+        for b in range(3):
+            op("s", lambda: S.activation(T["fo%d" % b][:], ps(1 + b), ACT.Copy), ["ps%d" % (1 + b)], ["fo%d" % b])
+        if k:
+            fill(2)
+        else:
+            derive(k, pv, sv, lv, rv)
+        gather("v", row("sa"), T.srow[:, 0:456], sk, la, lak)
+        turn(T.sT[:], ["sT"], T.srow[:, 0:C], sk)
+        turned("saT", "sa")
+        s0, sav, slv, srv = plane("sT", 0), plane("saT", 0), plane("slT", 0), plane("srT", 0)
+        turned("slT", "sl")
+        tt(v3(0), sav, s0, A.subtract)
+        turned("srT", "sr")
+        tt(v3(1), s0, slv, A.subtract)
+        tt(v3(2), s0, srv, A.subtract)
+        tt(slot("m"), v3(0), v3(1), A.min)
+        ts(slot("v0c"), v3(0), -1.0e-30, A.min)
+        u0, u1 = sub("wu", 0), sub("wu", 1)
+        tt(u0, slot("m"), v3(2), A.min)
+        fill()
+        for i in range(3):
+            tt(slot("e%d" % i), v3(i), u0, A.is_equal)
+        for i in range(3):
+            tt(slot("t%d" % i), slot("e%d" % i), m3(i), A.mult)
+        tt(slot("t3"), slot("t0"), slot("t1"), A.min)
+        fill()
+        tt(u1, slot("t3"), slot("t2"), A.min)
+        fill()
+        turn(T.urow[:, 0:C], ["urow"], T.wu[:], ["wu.0", "wu.1", "wu.i"])
+        uk = ["urow", "urow.n"]
+        gather("s", row("sl"), T.urow[:, 0:456], uk, ll, llk)
+        fill()
+        gather("v", row("sr"), T.urow[:, 0:456], uk, lr, lrk)
+        if k == 0:
+            late_constants()
+        turned("ulT", "sl")
+        turned("urT", "sr")
+        tt(slot("m"), slot("v0c"), plane("ulT", 0), A.min)
+        fill()
+        m = tt(slot("mm"), slot("m"), plane("urT", 0), A.min)
+        fill()
+        tt(slot("e0"), v3(0), m, A.is_equal)
+        tt(slot("e1"), plane("ulT", 0), m, A.is_equal)
+        tt(slot("e2"), plane("urT", 0), m, A.is_equal)
+        tt(slot("t0"), slot("e0"), m3(0), A.mult)
+        tt(slot("t1"), slot("e1"), plane("ulT", 1), A.mult)
+        tt(slot("t2"), slot("e2"), plane("urT", 1), A.mult)
+        tt(slot("t3"), slot("t0"), slot("t1"), A.min)
+        fill()
+        tt(slot("t4"), slot("t2"), slot("t3"), A.min)
+        fill()
+        Q0 = ts(sub("wc_", 0), slot("t4"), 256.0, A.add)
+        fill()
+        turn(T.qrow[:, 0:C], ["qrow"], T.wc_[:], ["wc_.0", "wc_.i"])
+        gather("s", row("qa"), T.qrow[:, 0:C], ["qrow"], la, lak)
+        gather("s", row("qaa"), T.qa[:], ["qa"], la, lak)
+        fill()
+        gather("v", row("ql"), T.qrow[:], ["qrow", "qrow.n"], ll, llk)
+        gather("s", row("qr"), T.qrow[:], ["qrow", "qrow.n"], lr, lrk)
+        gather("s", row("qaaa"), T.qaa[:], ["qaa"], la, lak)
+        fill(len(todo))
+        turned("qaT", "qa")
+        turned("qlT", "ql")
+        Qa, Qaa, Qaaa, Ql, Qr = plane("qaT", 0), plane("qaaT", 0), plane("qaaaT", 0), plane("qlT", 0), plane("qrT", 0)
+        eA = tt(slot("eA"), Q0, Qa, A.is_equal)
+        xn = tt(slot("xn"), Qa, nv, A.is_equal)
+        xl = tt(slot("xl"), Qa, lv, A.is_equal)
+        xp = tt(slot("xp"), Qa, slot("pin"), A.is_equal)
+        xr = tt(slot("xr"), Qa, rv, A.is_equal)
+        eL = tt(slot("eL"), Ql, Qa, A.is_equal)
+        rn = tt(slot("rn"), xn, eA, A.mult)
+        yq = tt(slot("yq"), Qa, pv, A.subtract)
+        yl = tt(slot("yl"), xl, eL, A.mult)
+        turned("qaaT", "qaa")
+        t = tt(slot("r0"), Qa, nv, A.subtract)
+        eB = tt(slot("eB"), Qaa, Qa, A.is_equal)
+        rot = tt(slot("rot"), rn, eB, A.mult)
+        xb = tt(slot("xb"), xp, eB, A.mult)
+        turned("qrT", "qr")
+        rd = tt(slot("rd"), rot, slot("dz"), A.mult)
+        eR = tt(slot("eR"), Qr, Qa, A.is_equal)
+        xbd = tt(slot("xbd"), xb, slot("dz"), A.mult)
+        yr = tt(slot("yr"), xr, eR, A.mult)
+        rd = tt(slot("rd2"), rd, pv, A.add)
+        yy = tt(slot("yy"), yl, yr, A.add)
+        fr = tt(slot("r1"), rot, slot("cn"), A.mult)
+        Y = tt(slot("Y"), yy, eA, A.mult)
+        rs1 = tt(slot("rs1"), rot, sv, A.mult)
+        yd = tt(slot("yd"), Y, yq, A.mult)
+        turned("qaaaT", "qaaa")
+        base = tt(slot("base"), rd, yd, A.add)
+        eC = tt(slot("eC"), Qaaa, Qa, A.is_equal)
+        t = tt(slot("r2"), Y, t, A.mult)
+        cd = tt(slot("cd"), xbd, eC, A.mult)
+        fr = tt(slot("r3"), fr, nv, A.add)
+        pn = tt(sub("ba%d" % nxt, 0), base, cd, A.add)
+        rs0 = tt(slot("rs0"), rot, rs1, A.subtract)
+        turned_back("ba%d" % nxt, "rw", [0], lambda: tt(sub("wr", 0), fr, t, A.add))
+        make_list(lak2, "ba%d" % nxt, [0])
+        send(dst, "arl%d" % k, T["al%d" % k][:], la2, [lak2])
+        wait("t", "arq%d" % k, 2 * len(topo.engines(core, dst)))
+        fbank = [5, 6, 7, 0]
+        for b in range(4):
+            mm(fbank[b], blk("eq", b), blk("es", b), T["aq%d" % k][:], T["as%d" % k][:], ["eq%d" % b])
+        for b in range(4):
+            op("s", lambda: S.activation(T["fp%d" % b][:], ps(fbank[b]), ACT.Copy), ["ps%d" % fbank[b]], ["fp%d" % b])
+            dma("y", "cf%d" % b, T.fq[:, C * b:C * b + C], T["fp%d" % b][:], ["fp%d" % b], ["fq%d" % b])
+        turn(T.rrep[:, 0:C], ["rrep"], T.wr[:], ["wr.0", "wr.i"])
+        rk = ["rrep", "rrep.n"]
+        gather("s", row("repl"), T.rrep[:], rk, ll, llk)
+        gather("v", row("repr_"), T.rrep[:], rk, lr, lrk)
+        if not last:
+            bl2 = sub("bl%d" % nxt, 2)
+            op("s", lambda: S.activation(bl2[0], pn[0], ACT.Copy), [pn[1]], [bl2[1]])
+        turned("replT", "repl")
+        turned("reprT", "repr_")
+        Rl, Rr = plane("replT", 0), plane("reprT", 0)
+        lnew, rnew = sub("bl%d" % nxt, 0), sub("bl%d" % nxt, 1)
+        t1 = tt(slot("l0"), pv, Rl, A.subtract)
+        t2 = tt(slot("l1"), pv, Rr, A.subtract)
+        t1 = tt(slot("l2"), rs1, t1, A.mult)
+        t2 = tt(slot("l3"), rs0, t2, A.mult)
+        tt(lnew, Rl, t1, A.add)
+        tt(rnew, Rr, t2, A.add)
+        if last:
+            quantize(T.vq[:], T.vs[:], T.vt[:], ["vt"], ["vq"])
+        wait("v", "arl%d" % k, len(topo.engines(core, dst)))
+        wait("s", "arl%d" % k, len(topo.engines(core, dst)))
+        al = T["al%d" % k]
+        for b in range(4):
+            fp, fq, kb = T["fp%d" % b], T.fq[:, C * b:C * b + C], T.kb[:, C * b:C * b + C]
+            op("v", lambda: V.tensor_tensor(kb, fp[:].indirect(al[:]), fq, A.add), ["fp%d" % b, "fq%d" % b], ["kb%d" % b])
+            if b < 3:
+                op("s", lambda: S.activation(T.zt[:, b:4 * C:4], kb.indirect(al[:]), ACT.Copy, scale=0.5), ["kb%d" % b], ["zt%d" % b])
+        op("s", lambda: S.activation(T.zt[:, 4 * H + 3:4 * C:4], kb.indirect(al[:, 14:28]), ACT.Copy, scale=0.5), ["kb3"], ["zt4"])
+        op("v", lambda: V.tensor_scalar(T.zt[:, 3:4 * H:4], kb.indirect(al[:, 0:14]), 0.5, None, A.mult), ["kb3"], ["zt3"])
+        quantize(T.zq[:], T.zs[:], T.zt[:], ["zt%d" % b for b in range(5)], ["zq"])
+        mm(1, blk("wq", 0), blk("wp", 0), T.zq[:, 0:H], T.zs[:, 0:H], ["wq", "wp", "zq"], H)
+        mm(5, blk("wq", 0), blk("wp", 0), T.zq[:, H:C], T.zs[:, H:C], ["wq", "wp", "zq"], H)
+        wbank = [1, 2, 3, 6]
+        for b in range(1, 4):
+            mm(wbank[b], blk("wq", b), blk("wp", b), T.zq[:], T.zs[:], ["wq", "wp", "zq"])
+        op("s", lambda: S.activation(T.rr0[:, 0:H], ps(1, H), ACT.Copy, scale=0.03125), ["ps1"], ["rr0.a"])
+        op("s", lambda: S.activation(T.rr0[:, H:C], ps(5, H), ACT.Copy, scale=0.03125), ["ps5"], ["rr0.b"])
+        for b in range(1, 4):
+            op("s", lambda: S.activation(T["rr%d" % b][:], ps(wbank[b]), ACT.Copy, scale=0.03125), ["ps%d" % wbank[b]], ["rr%d" % b])
+        gather("s", row("sa"), T.rr3[:], ["rr3"], la2, lak2)
+        if not last:
+            turned_back("bl%d" % nxt, "rw2", [0, 1, 2])
+            make_list("lb%d" % nxt, "bl%d" % nxt, [0, 1])
+            gather("s", row("pp"), T.rw2[:, 32:480], ["rw2"], la2, lak2)
+            gather("s", row("raa"), T.pp[:], ["pp"], la2, lak2)
+        else:
+            e = tt(slot("f0"), pn, nv, A.is_equal)
+            h = ts(slot("f1"), nv, -1.0, A.mult, 224.0, A.add)
+            e = tt(slot("f2"), e, h, A.mult)
+            tt(sub("bl1", 2), pn, e, A.add)
+            turn(T.rp2[:], ["rp2"], T.bl1[:, 0:C], ["bl1.0", "bl1.1", "bl1.2", "bl1.i"])
+            op("s", lambda: S.activation(T.trf[:], T.rp2[:], ACT.Identity, bias=T.c224[:, 0:1]), ["rp2", "c224"], ["trf"])
+            for i in range(3):
+                lane = (i + 2) % 3
+                dma("y", "st_tr", T.tr[:, C * i:C * i + C], T.trf[lane:128:16, :], ["trf"], ["tr%d" % i])
+        for b in range(3):
+            rks = ["rr0.a", "rr0.b"] if b == 0 else ["rr%d" % b]
+            op("v", lambda: V.tensor_tensor(T.xn[:, b:4 * C:4], T["rr%d" % b][:].indirect(la2), T["fo%d" % b][:], A.add),
+               rks + ["fo%d" % b, lak2], ["xn%d" % b])
+        tt((T.xn[:, 3:4 * C:4], "xn3"), row("sa"), (ps(4), "ps4"), A.add)
+        quantize(T["q%d" % (k + 1)][:], T["qs%d" % (k + 1)][:], T.xn[:], ["xn%d" % b for b in range(4)], ["q%d" % (k + 1)])
+        if not last:
+            pv, lv, rv = pn, lnew, rnew
+
+    mm(5, T.vq[:], T.vs[:], T.q3[:, 0:H], T.qs3[:, 0:H], ["vq", "q3"], H)
+    mm(6, T.vq[:], T.vs[:], T.q3[:, H:C], T.qs3[:, H:C], ["vq", "q3"], H)
+    dma("y", "st_oc", T.oc[:, 0:4 * C], T.q3[:, 0:C].bitcast(dt.uint8), ["q3"], ["oc"])
+    for i in range(4):
+        dma("y", "st_osc", T.osc[4 * i:4 * i + 4, :], T.qs3[32 * i:32 * i + 4, 0:C], ["q3"], ["osc%d" % i])
+    op("v", lambda: V.tensor_copy(T.yt[:, 0:H], ps(5, H)), ["ps5"], ["yt.a"])
+    op("s", lambda: S.activation(T.yt[:, H:C], ps(6, H), ACT.Copy), ["ps6"], ["yt.b"])
+    dma("s", "st_y", T.y[:], T.yt[:], ["yt.a", "yt.b"], ["yo"])
+    for sem in sorted(count):
+        wait("g", sem, count[sem])

@@ -3,6 +3,8 @@ from concourse.mybir import dt, AluOpType, ActivationFunctionType
 N = 4
 C = 448
 H = 224
+CUT = [0, 256, C]
+THREE = [0, 128, 288, C]
 STEP = [1, 2, 3]
 BIGV = 3.0e29
 
@@ -15,7 +17,7 @@ def _sbuf(names, n, dtype):
         SCRATCH[k] = ("sbuf", [128, n], dtype)
 
 
-_sbuf("xt xn zt", 4 * C, BF)
+_sbuf("xt xn zt fq kb", 4 * C, BF)
 _sbuf("ut vt ones et0 et1 et2 et3", 512, BF)
 _sbuf("uq vq", 128, CODE)
 _sbuf("us vs", 128, PLANE)
@@ -23,29 +25,32 @@ _sbuf("wq eq", 512, CODE)
 _sbuf("wp es", 512, PLANE)
 _sbuf("zq q0 q1 q2 q3 aq0 aq1 aq2", C, CODE)
 _sbuf("zs qs0 qs1 qs2 qs3 as0 as1 as2", C, PLANE)
-_sbuf("pidx", 2, I32)
-_sbuf("ti", 16, I32)
-_sbuf("c224", 8, F32)
-_sbuf("offm", 4, U16)
-_sbuf("upi lfi rti", 28, I32)
+_sbuf("pidx", 8, I32)
+_sbuf("col", 16, F32)
+_sbuf("i16 i32 jt nn", 28, F32)
+_sbuf("offm", 6, U16)
+_sbuf("ti", 96, I32)
 _sbuf("al0 al1 al2", 28, U16)
-_sbuf("lup la0 la1 la2 la3", 32, U16)
-_sbuf("lb0 lb1", 64, U16)
-_sbuf("iot prow rrow ra qrow rrep", 464, BF)
+_sbuf("la0 la1 la2 la3", 32, U16)
+_sbuf("lb", 64, U16)
+_sbuf("di dt", 256, BF)
+_sbuf("da", 288, BF)
+_sbuf("offa", 2, U16)
+_sbuf("eb", 160, BF)
+_sbuf("kg", C, BF)
+_sbuf("dd", 64, F32)
+_sbuf("qrow rrep", 464, BF)
 _sbuf("srow urow", 456, F32)
-_sbuf("nT lrow raa pT lT rT raT raaT pp ppT qa qaa qaaa ql qr qaT qaaT qaaaT qlT qrT repl repr_ replT reprT rp2", C, BF)
-_sbuf("sa sl sr sT saT slT srT ulT urT trf yt rr0 rr1 rr2 rr3", C, F32)
-_sbuf("wu", C, F32)
-_sbuf("wc_ wr zr", C, BF)
-_sbuf("ba0 ba1 bl0 bl1", C + 480, BF)
-_sbuf("rw rw2", 512, BF)
-_sbuf("m3 v3", 84, F32)
-_sbuf("cb", 28 * 80, F32)
-_sbuf("fo0 fo1 fo2 fo3 fp0 fp1 fp2 fp3", C, BF)
-_sbuf("fq kb", 4 * C, BF)
+_sbuf("lanes trow pp ppT qa qaa qaaa ql qr qaT qaaT qaaaT qlT qrT repl repr_", C, BF)
+_sbuf("repT", 512 + C, BF)
+_sbuf("sa sl sr ul ur xg sT saT slT srT ulT urT trf yt rr0 rr1 rr2 rr3 wu", C, F32)
+_sbuf("sc", 1024, F32)
+_sbuf("so", 3 * 112, F32)
+_sbuf("cb", 28 * 40, F32)
+_sbuf("fo0 fo1 fo2 fp0 fp1 fp2 fp3", C, BF)
 
-SEMAPHORES = (["cv", "cs", "ct", "cg", "sent"] + ["ld_" + k for k in "x u v up lf rt wc ws z".split()]
-              + ["st_" + k for k in "y oc osc tr".split()] + ["cf%d" % k for k in range(4)] + ["arq%d" % k for k in range(3)] + ["arl%d" % k for k in range(3)])
+SEMAPHORES = (["cv", "cs", "ct", "cg", "sent"] + ["ld_" + k for k in "x0 x1 u v t w".split()]
+              + ["st_" + k for k in "y oc tr".split()] + ["cf%d" % k for k in range(4)] + ["arq%d" % k for k in range(3)] + ["arl%d" % k for k in range(3)])
 
 
 def rank_program(g, core, T, topo):
@@ -60,7 +65,18 @@ def rank_program(g, core, T, topo):
     count = {}
     seen = {k: {} for k in queue}
     facts = {}
-    writer, readers = {}, {}
+    uses = {}
+    masks = {}
+
+    def ap(v):
+        return T[v[0]][:, v[1]:v[2]:v[3]] if v[3] > 1 else T[v[0]][:, v[1]:v[2]]
+
+    def columns(v):
+        if v[0] == "ps":
+            return 1 << (v[1] // 512)
+        if v[1:] not in masks:
+            masks[v[1:]] = sum(1 << c for c in range(v[1], v[2], v[3]))
+        return masks[v[1:]]
 
     def wait(q, sem, val):
         s = seen[q]
@@ -74,25 +90,21 @@ def rank_program(g, core, T, topo):
 
     def prepare(q, reads, writes):
         need = {}
-        for k in reads + writes:
-            if k in writer:
-                w, n, wq = writer[k]
-                need[w] = max(need.get(w, 0), n)
-        for k in writes:
-            for w, n, rq in readers.get(k, []):
-                if rq != q or w[0] != "c":
-                    need[w] = max(need.get(w, 0), n)
-        own = "c" + q
-        for w in sorted(need, key=lambda w: (w == own, w)):
-            wait(q, w, need[w])
+        for v, w in [(v, False) for v in reads] + [(v, True) for v in writes]:
+            m = columns(v)
+            for cols, sem, val, uq, wrote in uses.get(v[0], []):
+                if cols & m and (wrote or ((w or v[0] == "ps") and not (uq == q and sem == "c" + q))):
+                    need[sem] = max(need.get(sem, 0), val)
+        for sem in sorted(need, key=lambda s: (s == "c" + q, s)):
+            wait(q, sem, need[sem])
 
     def note(q, sem, val, reads, writes):
         facts[(sem, val)] = dict(seen[q])
-        for k in writes:
-            writer[k] = (sem, val, q)
-            readers[k] = []
-        for k in reads:
-            readers.setdefault(k, []).append((sem, val, q))
+        for v in writes:
+            m = columns(v)
+            uses[v[0]] = [[u[0] & ~m] + u[1:] for u in uses.get(v[0], []) if u[0] & ~m] + [[m, sem, val, q, True]]
+        for v in reads:
+            uses.setdefault(v[0], []).append([columns(v), sem, val, q, False])
 
     def op(q, fn, reads, writes):
         prepare(q, reads, writes)
@@ -101,11 +113,13 @@ def rank_program(g, core, T, topo):
         fn().then_inc(T.sem[sem], 1)
         note(q, sem, count[sem], reads, writes)
 
-    def dma(q, sem, out, in_, reads, writes):
-        prepare(q, reads, writes)
-        count[sem] = count.get(sem, 0) + 16
-        queue[q].dma_start(out, in_).then_inc(T.sem[sem], 16)
-        note(q, sem, count[sem], reads, writes)
+    def dmas(q, sem, moves):
+        for out, in_, reads, writes in moves:
+            prepare(q, reads, writes)
+            queue[q].dma_start(out, in_).then_inc(T.sem[sem], 16)
+        count[sem] = count.get(sem, 0) + 16 * len(moves)
+        for out, in_, reads, writes in moves:
+            note(q, sem, count[sem], reads, writes)
 
     def send(dst, rsem, out, in_, reads):
         prepare("g", reads, [])
@@ -113,415 +127,414 @@ def rank_program(g, core, T, topo):
         g.remote_dma(out, in_, T.sem[rsem], T.sem["sent"], pid, rid, topo.mask(core, dst))
         count["sent"] = count.get("sent", 0) + len(topo.engines(core, dst))
 
+    def cols(buf, a=0, b=C):
+        return buf, a, b, 1
+
+    def half(buf, h, w=1):
+        return buf, w * H * h, w * H * (h + 1), 1
+
+    def piece(buf, h, b=None):
+        a, z = CUT[h], CUT[h + 1]
+        return (buf, a, z, 1) if b is None else (buf, 4 * a + b, 4 * z, 4)
+
     def ps(b, n=C):
-        return T.ps[:, 512 * b:512 * b + n]
+        return "ps", 512 * b, 512 * b + n, 1
+
+    def plane(buf, lane, at=0):
+        return buf, at + lane, at + C, 16
+
+    def dense(buf, w):
+        return buf, 32 * w, 32 * w + 28, 1
+
+    def col(i):
+        return "col", i, i + 1, 1
 
     slots = {}
 
-    def slot(name):
+    def val(name):
         i = slots.setdefault(name, len(slots))
-        return T.cb[:, 28 * i:28 * i + 28], "cb." + name
+        return "cb", 28 * i, 28 * i + 28, 1
 
-    def plane(buf, lane):
-        return T[buf][:, lane:C:16], buf
+    def slot(i, j, buf="sc"):
+        return buf, 112 * i + j, 112 * i + 112, 4
 
-    def sub(buf, lane):
-        return T[buf][:, lane:C:16], "%s.%d" % (buf, lane)
+    def four(i, buf="sc"):
+        return buf, 112 * i, 112 * i + 112, 1
 
     def tt(out, a, b, o):
-        op("v", lambda: V.tensor_tensor(out[0], a[0], b[0], o), [a[1], b[1]], [out[1]])
+        op("v", lambda: V.tensor_tensor(ap(out), ap(a), ap(b), o), [a, b], [out])
         return out
 
     def ts(out, a, s1, o1, s2=None, o2=None):
+        more = [s for s in (s1, s2) if isinstance(s, tuple)]
+        s1, s2 = [ap(s) if isinstance(s, tuple) else s for s in (s1, s2)]
         if o2 is None:
-            op("v", lambda: V.tensor_scalar(out[0], a[0], s1, None, o1), [a[1]], [out[1]])
+            op("v", lambda: V.tensor_scalar(ap(out), ap(a), s1, None, o1), [a] + more, [out])
         else:
-            op("v", lambda: V.tensor_scalar(out[0], a[0], s1, s2, o1, o2), [a[1]], [out[1]])
+            op("v", lambda: V.tensor_scalar(ap(out), ap(a), s1, s2, o1, o2), [a] + more, [out])
         return out
 
-    def turn(out, ok, in_, ik):
-        op("v", lambda: V.transpose(out, in_), ik, ok)
+    def scan(out, d0, d1, o1=A.add):
+        op("v", lambda: V.tensor_tensor_scan(ap(out), ap(d0), ap(d1), 0.0, A.mult, o1), [d0, d1], [out])
 
-    def turned(out, in_):
-        turn(T[out][:], [out], T[in_][:, 0:C], [in_])
+    def turn(out, in_):
+        op("v", lambda: V.transpose(ap(out), ap(in_)), [in_], [out])
 
-    def gather(q, out, win, wk, off, fk):
-        if q == "s":
-            op("s", lambda: S.activation(out[0], win.indirect(off), ACT.Copy), wk + [fk], [out[1]])
+    def turned(name):
+        turn(cols(name + "T"), cols(name))
+
+    def copy(q, out, in_, scale=1.0, bias=None):
+        if q == "v":
+            if scale == 1.0:
+                op("v", lambda: V.tensor_copy(ap(out), ap(in_)), [in_], [out])
+            else:
+                ts(out, in_, scale, A.mult)
+        elif bias is None:
+            op("s", lambda: S.activation(ap(out), ap(in_), ACT.Copy, scale=scale), [in_], [out])
         else:
-            op("v", lambda: V.tensor_copy(out[0], win.indirect(off)), wk + [fk], [out[1]])
+            op("s", lambda: S.activation(ap(out), ap(in_), ACT.Identity, bias=ap(bias)), [in_, bias], [out])
 
-    def row(buf):
-        return T[buf][:], buf
+    def gather(q, out, win, off, scale=1.0):
+        if q == "s":
+            op("s", lambda: S.activation(ap(out), ap(win).indirect(ap(off)), ACT.Copy, scale=scale), [win, off], [out])
+        elif scale == 1.0:
+            op("v", lambda: V.tensor_copy(ap(out), ap(win).indirect(ap(off))), [win, off], [out])
+        else:
+            op("v", lambda: V.tensor_scalar(ap(out), ap(win).indirect(ap(off)), scale, None, A.mult), [win, off], [out])
 
-    def memset(ap, val, keys):
-        op("v", lambda: V.memset(ap, val), [], keys)
+    def gather_add(out, win, off, other):
+        op("v", lambda: V.tensor_tensor(ap(out), ap(win).indirect(ap(off)), ap(other), A.add), [win, off, other], [out])
 
-    def mm(bank, l, ls, r, rs, keys, n=C):
-        op("t", lambda: g.tensor.matmul_mx(ps(bank, n), l, ls, r, rs, True, True), keys, ["ps%d" % bank])
+    def part(off, h, cut=(0, H, C)):
+        return off[0], off[1] + cut[h] // 16, off[1] + cut[h + 1] // 16, 1
 
-    def quantize(out, os, in_, reads, writes):
-        op("v", lambda: V.quantize_mx(out, os, in_), reads, writes)
+    def memset(v, x):
+        op("v", lambda: V.memset(ap(v), x), [], [v])
 
-    def blk(buf, b):
-        return T[buf][:, 128 * b:128 * b + 128]
+    def mm(bank, l, ls, b, r, rs, a=0, n=C):
+        l, ls, r, rs = cols(l, 128 * b, 128 * b + 128), cols(ls, 128 * b, 128 * b + 128), cols(r, a, a + n), cols(rs, a, a + n)
+        op("t", lambda: g.tensor.matmul_mx(ap(ps(bank, n)), ap(l), ap(ls), ap(r), ap(rs), True, True), [l, ls, r, rs], [ps(bank)])
+
+    def quantize(out, scales, in_, a, n):
+        o, s, i = cols(out, a, a + n), cols(scales, a, a + n), cols(in_, 4 * a, 4 * (a + n))
+        op("v", lambda: V.quantize_mx(ap(o), ap(s), ap(i)), [i], [o, s])
+
+    def swapped(buf, w, n):
+        turn(cols("eb", 16 + 32 * w, 16 + 32 * (w + n)), cols(buf, 32 * w, 32 * (w + n)))
+        turn(cols(buf, 128 + 32 * w, 160 + 32 * (w + n)), cols("eb", 32 * w, 32 + 32 * (w + n)))
+
+    def make_list(out, win, off):
+        op("v", lambda: V.tensor_scalar(ap(out), ap(win).indirect(ap(off)), 224.0, None, A.add), [win, off], [out])
 
     todo = []
+
+    def later(f, *a):
+        todo.append(lambda: f(*a))
 
     def fill(n=1):
         for _ in range(n):
             if todo:
                 todo.pop(0)()
 
-    dma("y", "ld_up", T.upi[:], T.up[:], [], ["upi"])
-    dma("s", "ld_rt", T.rti[:], T.rt[:], [], ["rti"])
-    dma("s", "ld_lf", T.lfi[:], T.lf[:], [], ["lfi"])
-    dma("y", "ld_x", T.xt[:], T.x[:], [], ["xt"])
-    dma("y", "ld_u", T.ut[:], T.u[:], [], ["ut"])
-    dma("y", "ld_wc", T.wq[:, 0:512].bitcast(dt.uint8), T.wc[:], [], ["wq"])
-    dma("y", "ld_ws", T.wp[:, 0:512], T.ws[:], [], ["wp"])
-    dma("y", "ld_v", T.vt[:], T.v[:], [], ["vt"])
+    dmas("s", "ld_t", [(T.ti[:, 32 * i:32 * i + 28], T[k][:], [], [dense("ti", i)]) for i, k in enumerate(("up", "lf", "rt"))])
+    dmas("y", "ld_u", [(T.ut[:], T.u[:], [], [cols("ut", 0, 512)])])
+    for h in range(2):
+        v = cols("xt", 4 * CUT[h], 4 * CUT[h + 1])
+        dmas("y", "ld_x%d" % h, [(ap(v), T.x[:, v[1]:v[2]], [], [v])])
+    wait("y", "ld_x1", 16)
+    dmas("y", "ld_w", [(T.wq[:, 0:512].bitcast(dt.uint8), T.wc[:], [], [cols("wq", 0, 512)]), (T.wp[:, 0:512], T.ws[:], [], [cols("wp", 0, 512)])])
+    dmas("y", "ld_v", [(T.vt[:], T.v[:], [], [cols("vt", 0, 512)])])
 
-    op("g", lambda: g.iota(T.pidx[:], [[0, 2]], 0, 1), [], ["pidx"])
-    memset(T.ones[:], 1.0, ["ones"])
-    op("g", lambda: g.iota(T.iot[:], [[1, 464]], -224, 0, allow_small_or_imprecise_dtypes=True), [], ["iot"])
-    op("g", lambda: g.affine_select(T.et0[:], T.ones[:], [[-1, 512]], A.is_equal, 0.0, 0, 4), ["ones"], ["et0"])
+    ones = cols("ones", 0, 512)
+    memset(ones, 1.0)
+    op("g", lambda: g.iota(T.pidx[:, 0:2], [[0, 2]], 0, 1), [], [cols("pidx", 0, 2)])
+    op("g", lambda: g.iota(T.i16[:], [[16, 28]], 0, 0, allow_small_or_imprecise_dtypes=True), [], [cols("i16", 0, 28)])
+    op("g", lambda: g.iota(T.i32[:], [[32, 14], [0, 2]], -224, 0, allow_small_or_imprecise_dtypes=True), [], [cols("i32", 0, 28)])
+    op("g", lambda: g.affine_select(T.et0[:], T.ones[:], [[-1, 512]], A.is_equal, 0.0, 0, 4), [ones], [cols("et0", 0, 512)])
+    for h in range(2):
+        copy("s", cols("sc", 512 * h, 512 * h + 512), ones, scale=0.0)
+    copy("s", cols("lanes"), cols("ones"), scale=0.0)
+    copy("s", cols("wu"), cols("ones"), scale=0.0)
     for b in range(1, 4):
-        memset(T["et%d" % b][:, 0:b], 0.0, ["et%d.0" % b])
-    op("s", lambda: S.activation(T.wu[:], T.iot[:, 0:C], ACT.Copy, scale=0.0), ["iot"], ["wu.0", "wu.1", "wu.i"])
-    op("s", lambda: S.activation(T.zr[:], T.iot[:, 0:C], ACT.Copy, scale=0.0), ["iot"], ["zr"])
+        memset(cols("et%d" % b, 0, b), 0.0)
     for b in range(1, 4):
-        op("s", lambda: S.activation(T["et%d" % b][:, b:512], T.et0[:, 0:512 - b], ACT.Copy), ["et0"], ["et%d" % b])
-    memset(T.ba0[:, 0:C], 0.0, ["ba0.0", "ba0.i"])
-    memset(T.rw[:, 0:32], 0.0, ["rw.p0"])
-    memset(T.rw[:, 480:512], 0.0, ["rw.p1"])
-    for k in ("prow", "rrow", "ra"):
-        memset(T[k][:, C:464], 224.0, [k + ".n"])
-    memset(T.srow[:, C:456], -BIGV, ["srow.n"])
-    memset(T.urow[:, C:456], BIGV, ["urow.n"])
-    memset(T.qrow[:, C:464], 600.0, ["qrow.n"])
-    memset(T.c224[:, 0:4], 224.0, ["c224"])
-    memset(T.c224[:, 4:8], -256.0, ["cm256"])
-
-    def tiv(i):
-        return T.ti[:, i:i + 1], "ti%d" % i
-    pd = (T.pidx[:, 0:1], "pidx")
-    ts(tiv(0), pd, 1, A.logical_shift_right, 7, A.bitwise_and)
-    ts(tiv(1), pd, 1, A.bitwise_and)
-    ts(tiv(2), pd, 4, A.logical_shift_right, 1, A.bitwise_and)
-    ts(tiv(4), tiv(0), 32, A.mult)
-    tt(tiv(3), tiv(1), tiv(2), A.mult)
-    ts(tiv(5), tiv(1), 480, A.mult)
-    ts(tiv(6), tiv(2), 464, A.mult)
-    ts(tiv(7), tiv(3), -928, A.mult)
-
-    def turned_back(big, rw, lanes, between=None):
-        turn(T[rw][:, 32:480], [rw], T[big][:, 0:C], ["%s.%s" % (big, k) for k in lanes] + [big + ".i"])
-        if between:
-            between()
-        turn(T[big][:, C:928], [big + ".s"], T[rw][:, 16:496], [rw, rw + ".p0", rw + ".p1"])
-
-    def make_list(out, big, lanes):
-        op("v", lambda: V.tensor_scalar(T[out][:], T[big][:, 0:928].indirect(T.offm[:, 0:2 * len(lanes)]), 224.0, None, A.add),
-           ["%s.%d" % (big, i) for i in lanes] + [big + ".i", big + ".s"] + ["offm%d" % i for i in lanes], [out])
-
-    op("v", lambda: V.tensor_copy(T.lup[:, 0:28], T.upi[:]), ["upi"], ["lup"])
-    op("v", lambda: V.tensor_copy(T.lb0[:, 32:60], T.rti[:]), ["rti"], ["lb0.r"])
-    op("v", lambda: V.tensor_copy(T.lb0[:, 0:28], T.lfi[:]), ["lfi"], ["lb0.l"])
-    lup = T.lup[:, 0:28]
-    gather("v", (T.prow[:, 0:C], "prow"), T.iot[:], ["iot"], lup, "lup")
-    gather("s", (T.rrow[:, 0:C], "rrow"), T.iot[:], ["iot"], T.lb0[:, 32:60], "lb0.r")
-    gather("s", row("lrow"), T.iot[:], ["iot"], T.lb0[:, 0:28], "lb0.l")
-    gather("s", (T.ra[:, 0:C], "ra"), T.rrow[:], ["rrow", "rrow.n"], lup, "lup")
-    tt(tiv(8), tiv(4), tiv(5), A.add)
-    tt(tiv(9), tiv(6), tiv(7), A.add)
-    turned("pT", "prow")
-    tt(tiv(10), tiv(8), tiv(9), A.add)
-    nv = plane("nT", 0)
-    turned("nT", "iot")
-    pT = plane("pT", 0)
-    e = ts(slot("i0"), pT, 224.0, A.is_equal)
-    f_ = tt(slot("i1"), nv, pT, A.subtract)
-    ts((T.offm[:, 0:1], "offm0"), tiv(10), 0, A.add, 927, A.min)
-    f_ = tt(slot("i2"), e, f_, A.mult)
-    ts((T.offm[:, 1:2], "offm0"), tiv(10), 256, A.add, 927, A.min)
-    tt(sub("ba0", 0), pT, f_, A.add)
+        copy("s", cols("et%d" % b, b, 512), cols("et0", 0, 512 - b))
+    pd = cols("pidx", 0, 1)
+    for i, (sh, m) in enumerate(((0, 1), (4, 1), (0, 15), (0, 31))):
+        ts(cols("pidx", 2 + i, 3 + i), pd, sh, A.logical_shift_right, m, A.bitwise_and)
+    memset(("ti", 28, 32, 1), 0)
+    memset(("ti", 60, 64, 1), 0)
+    memset(("ti", 92, 96, 1), 0)
+    copy("v", cols("col", 0, 4), cols("pidx", 2, 6))
+    memset(cols("dt", 0, 256), 0.0)
+    memset(cols("di", 96, 128), 0.0)
+    tt(col(4), col(0), col(1), A.not_equal)
+    ts(col(5), col(1), -30.0, A.mult, 159.0, A.add)
+    ts(col(10), col(1), -24.0, A.mult, 156.0, A.add)
+    ts(col(11), col(2), 4.0, A.mult, 3.0, A.add)
+    jt = ts(cols("jt", 0, 28), cols("i16", 0, 28), col(2), A.add, -448.0, A.add)
+    nv = ts(cols("nn", 0, 28), cols("i32", 0, 28), col(3), A.add)
+    ts(col(7), col(4), col(5), A.mult, col(2), A.add)
+    ts(col(12), col(4), col(10), A.mult, col(11), A.add)
+    memset(cols("eb", 0, 160), 0.0)
+    memset(cols("da", 0, 288), 0.0)
+    memset(col(8), 224.0)
+    memset(col(9), -256.0)
+    ts(cols("offm", 0, 6), cols("i16", 0, 6), col(7), A.add)
+    ts(cols("offa", 0, 2), cols("i16", 0, 2), 4.0, A.mult, col(12), A.add)
+    memset(cols("srow", C, 456), -BIGV)
+    memset(cols("urow", C, 456), BIGV)
+    memset(cols("qrow", C, 464), 600.0)
+    memset(cols("rrep", C, 464), 224.0)
+    memset(cols("repT", C, 512), 0.0)
+    memset(cols("dd", 28, 32), 0.0)
+    n2 = ts(slot(3, 0), nv, -256.0, A.add)
+    memset(slot(2, 2), 1.0)
+    memset(slot(2, 3), 1.0)
+    memset(slot(6, 1), 1.0)
 
     def quantize_constants(b):
-        quantize(blk("eq", b), blk("es", b), T["et%d" % b][:], ["et%d" % b] + (["et%d.0" % b] if b else []), ["eq%d" % b])
-    ts((T.offm[:, 2:3], "offm1"), tiv(10), 1, A.add, 927, A.min)
-    turned_back("ba0", "rw", [0], lambda: ts((T.offm[:, 3:4], "offm1"), tiv(10), 257, A.add, 927, A.min))
+        o, s, i = cols("eq", 128 * b, 128 * b + 128), cols("es", 128 * b, 128 * b + 128), cols("et%d" % b, 0, 512)
+        op("v", lambda: V.quantize_mx(ap(o), ap(s), ap(i)), [i], [o, s])
+
+    ts(cols("di", 0, 96), cols("ti", 0, 96), -224.0, A.add)
+    copy("v", cols("lb", 0, 64), cols("ti", 32, 96))
+    e = ts(val("i0"), dense("di", 0), 224.0, A.is_equal)
+    quantize("uq", "us", "ut", 0, 128)
+    e = tt(val("i1"), e, jt, A.mult)
     quantize_constants(0)
-    make_list("la0", "ba0", [0])
-    for b in range(1, 4):
-        quantize_constants(b)
-    quantize(T.uq[:], T.us[:], T.ut[:], ["ut"], ["uq"])
-    zeros = {"wc_": ["wc_.0", "wc_.i"], "ba1": ["ba1.0", "ba1.i"], "wr": ["wr.0", "wr.i"],
-             "bl1": ["bl1.0", "bl1.1", "bl1.2", "bl1.i"], "bl0": ["bl0.0", "bl0.1", "bl0.2", "bl0.i"]}
-    for k in zeros:
-        dma("y", "ld_z", T[k][:, 0:C], T.zr[:], ["zr"], [])
-    for k in zeros:
-        for key in zeros[k]:
-            writer[key] = ("ld_z", count["ld_z"], "y")
-    facts[("ld_z", count["ld_z"])] = {}
-    quantize(T.q0[:], T.qs0[:], T.xt[:], ["xt"], ["q0"])
-    turned("rT", "rrow")
-    turned("lT", "lrow")
-    lv, rv = plane("lT", 0), plane("rT", 0)
+    tt(dense("di", 0), dense("di", 0), e, A.add)
+    quantize_constants(1)
+    pv, lv, rv = ("da", 3, 112, 4), dense("dt", 1), dense("dt", 2)
+    turn(cols("eb", 16, 112), cols("di", 0, 96))
+    ts(cols("la0", 0, 32), cols("di", 0, 32), 224.0, A.add)
+    turn(cols("di", 128, 256), cols("eb", 0, 128))
+    quantize("q0", "qs0", "xt", 0, CUT[1])
+    gather("v", cols("dt", 32, 96), cols("di", 0, 256), cols("offm", 2, 6))
+    gather("v", ("da", 3, 128, 4), cols("di", 0, 256), cols("offm", 0, 2))
+    quantize("q0", "qs0", "xt", CUT[1], C - CUT[1])
 
-    def m3(i):
-        return T.m3[:, 28 * i:28 * i + 28], "m3.%d" % i
+    LB, LX, LC, LR, LP, LL, LE = range(7)
 
-    def v3(i):
-        return T.v3[:, 28 * i:28 * i + 28], "v3.%d" % i
-    ts(m3(0), nv, -256.0, A.add)
-    ts(m3(1), lv, -256.0, A.add)
-    ts(m3(2), rv, -256.0, A.add)
+    def tree_lanes():
+        copy("s", slot(1, 2), lv, bias=col(9))
+        copy("s", plane("lanes", LL), lv)
+        copy("s", plane("lanes", LP), pv)
 
-    def late_constants():
-        memset(T.rrep[:, C:464], 224.0, ["rrep.n"])
-        memset(T.rw2[:, 0:32], 0.0, ["rw2.p0"])
-        memset(T.rw2[:, 480:512], 0.0, ["rw2.p1"])
+    def tree_facts():
+        side, ppv = val("side"), plane("ppT", LP)
+        later(turned, "pp")
+        later(tt, side, plane("ppT", LL), nv, A.not_equal)
+        later(tt, ("sc", 953, 1008, 2), ppv, pv, A.subtract)
+        later(tt, ("sc", 897, 952, 2), nv, pv, A.subtract)
+        later(tt, val("d6"), side, slot(0, 2), A.mult)
+        later(ts, ("sc", 952, 1008, 2), ("sc", 953, 1008, 2), 0.0, A.is_equal)
+        later(tt, plane("lanes", LC), rv, val("d6"), A.subtract)
+        later(scan, ("sc", 449, 560, 2), cols("sc", 896, 952), cols("sc", 952, 1008))
+        later(tt, val("cn"), plane("lanes", LC), nv, A.subtract)
+        later(tt, val("pc"), pv, plane("lanes", LC), A.subtract)
 
-    def derive(k, pv, sv, lv, rv):
-        def add(f, *a):
-            todo.append(lambda: f(*a))
-        spv = slot("sp")
-        if k == 0:
-            ppv = plane("ppT", 0)
-            for n in ("raT raaT ppT").split():
-                add(turned, n, n[:-1])
-            add(tt, sv, plane("raT", 0), nv, A.is_equal)
-            add(tt, spv, plane("raaT", 0), pv, A.is_equal)
-            add(ts, slot("d0"), ppv, 224.0, A.is_equal)
-        else:
-            ppv = plane("ppT", 2)
-            add(turned, "ppT", "pp")
-            add(tt, sv, plane("ppT", 0), nv, A.not_equal)
-            add(tt, slot("d0"), ppv, pv, A.is_equal)
-            add(turned, "raaT", "raa")
-            add(tt, spv, plane("raaT", 0), pv, A.not_equal)
-        add(tt, slot("d1"), nv, ppv, A.subtract)
-        add(tt, slot("d2"), sv, spv, A.is_equal)
-        add(tt, slot("d3"), lv, rv, A.subtract)
-        add(tt, slot("d4"), slot("d0"), slot("d1"), A.mult)
-        add(ts, slot("d5"), slot("d2"), 2048.0, A.mult)
-        add(tt, slot("d6"), sv, slot("d3"), A.mult)
-        add(tt, slot("d7"), ppv, slot("d4"), A.add)
-        add(tt, slot("pin"), slot("d5"), pv, A.add)
-        add(tt, slot("d8"), rv, slot("d6"), A.add)
-        add(tt, slot("dz"), slot("d7"), pv, A.subtract)
-        add(tt, slot("cn"), slot("d8"), nv, A.subtract)
+    def child_order():
+        tt(slot(0, 2), rv, lv, A.subtract)
+        tt(slot(0, 1), lv, rv, A.is_gt)
 
-    pv, sv = sub("ba0", 0), slot("side")
+    tree_lanes()
+    ll, lr = cols("lb", 0, 28), cols("lb", 32, 60)
     for k in range(3):
-        par, nxt = k % 2, 1 - k % 2
         last = k == 2
-        q, qs, qk = T["q%d" % k], T["qs%d" % k], "q%d" % k
+        q, qs = "q%d" % k, "qs%d" % k
         dst = T.cores[(rank + STEP[k]) % N]
-        la, lak = T["la%d" % k][:, 0:28], "la%d" % k
-        ll, llk = T["lb%d" % par][:, 0:28], ["lb%d" % par, "lb0.l"][k == 0]
-        lr, lrk = T["lb%d" % par][:, 32:60], ["lb%d" % par, "lb0.r"][k == 0]
-        lak2 = "la%d" % (k + 1)
-        la2 = T[lak2][:, 0:28]
-        send(dst, "arq%d" % k, T["aq%d" % k][:, 0:C].bitcast(dt.uint8), q[:, 0:C].bitcast(dt.uint8), [qk])
-        send(dst, "arq%d" % k, T["as%d" % k][:, 0:C], qs[:, 0:C], [qk])
-        mm(0, T.uq[:], T.us[:], q[:, 0:H], qs[:, 0:H], ["uq", qk], H)
-        mm(7, T.uq[:], T.us[:], q[:, H:C], qs[:, H:C], ["uq", qk], H)
-        for b in range(4):
-            mm(1 + b, blk("eq", b), blk("es", b), q[:], qs[:], ["eq%d" % b, qk])
-        if k:
-            derive(k, pv, sv, lv, rv)
-            fill(3)
-        op("v", lambda: V.tensor_copy(T.srow[:, 0:H], ps(0, H)), ["ps0"], ["srow.a"])
-        op("s", lambda: S.activation(T.srow[:, H:C], ps(7, H), ACT.Copy), ["ps7"], ["srow.b"])
-        sk = ["srow.a", "srow.b", "srow.n"]
-        gather("s", row("sl"), T.srow[:, 0:456], sk, ll, llk)
-        gather("s", row("sr"), T.srow[:, 0:456], sk, lr, lrk)
-        if k:
-            for i, w in ((1, lv), (2, rv)):
-                op("s", lambda: S.activation(m3(i)[0], w[0], ACT.Identity, bias=T.c224[:, 4:5]), [w[1], "cm256"], [m3(i)[1]])
-        else:
-            gather("s", row("raa"), T.ra[:], ["ra", "ra.n"], lup, "lup")
-            gather("s", row("pp"), T.prow[:], ["prow", "prow.n"], lup, "lup")
-        for b in range(3):
-            op("s", lambda: S.activation(T["fo%d" % b][:], ps(1 + b), ACT.Copy), ["ps%d" % (1 + b)], ["fo%d" % b])
-        if k:
-            fill(2)
-        else:
-            derive(k, pv, sv, lv, rv)
-        gather("v", row("sa"), T.srow[:, 0:456], sk, la, lak)
-        turn(T.sT[:], ["sT"], T.srow[:, 0:C], sk)
-        turned("saT", "sa")
-        s0, sav, slv, srv = plane("sT", 0), plane("saT", 0), plane("slT", 0), plane("srT", 0)
-        turned("slT", "sl")
-        tt(v3(0), sav, s0, A.subtract)
-        turned("srT", "sr")
-        tt(v3(1), s0, slv, A.subtract)
-        tt(v3(2), s0, srv, A.subtract)
-        tt(slot("m"), v3(0), v3(1), A.min)
-        ts(slot("v0c"), v3(0), -1.0e-30, A.min)
-        u0, u1 = sub("wu", 0), sub("wu", 1)
-        tt(u0, slot("m"), v3(2), A.min)
-        fill()
-        for i in range(3):
-            tt(slot("e%d" % i), v3(i), u0, A.is_equal)
-        for i in range(3):
-            tt(slot("t%d" % i), slot("e%d" % i), m3(i), A.mult)
-        tt(slot("t3"), slot("t0"), slot("t1"), A.min)
-        fill()
-        tt(u1, slot("t3"), slot("t2"), A.min)
-        fill()
-        turn(T.urow[:, 0:C], ["urow"], T.wu[:], ["wu.0", "wu.1", "wu.i"])
-        uk = ["urow", "urow.n"]
-        gather("s", row("sl"), T.urow[:, 0:456], uk, ll, llk)
-        fill()
-        gather("v", row("sr"), T.urow[:, 0:456], uk, lr, lrk)
+        arrivals = len(topo.engines(core, dst))
+        la, la2 = cols("la%d" % k, 0, 28), cols("la%d" % (k + 1), 0, 28)
+        send(dst, "arq%d" % k, T["aq%d" % k][:, 0:C].bitcast(dt.uint8), T[q][:, 0:C].bitcast(dt.uint8), [cols(q)])
+        send(dst, "arq%d" % k, T["as%d" % k][:, 0:C], T[qs][:, 0:C], [cols(qs)])
+        mm(0, "uq", "us", 0, q, qs, 0, CUT[1])
+        mm(7, "uq", "us", 0, q, qs, CUT[1], C - CUT[1])
         if k == 0:
-            late_constants()
-        turned("ulT", "sl")
-        turned("urT", "sr")
-        tt(slot("m"), slot("v0c"), plane("ulT", 0), A.min)
+            child_order()
+            quantize_constants(2)
+            quantize_constants(3)
+        else:
+            fill(2)
+        for b in range(4):
+            mm(1 + b, "eq", "es", b, q, qs)
+        srow, urow, qrow, rrep = cols("srow", 0, 456), cols("urow", 0, 456), cols("qrow", 0, 464), cols("rrep", 0, 464)
+        copy("s", piece("srow", 0), ps(0, CUT[1]))
+        copy("v", piece("srow", 1), ps(7, C - CUT[1]))
+        gather("s", cols("sl"), srow, ll)
+        gather("s", half("sr", 1), srow, part(lr, 1))
+        if k == 0:
+            turn(cols("trow"), cols("lanes"))
+        else:
+            fill()
+        gather("v", half("sr", 0), srow, part(lr, 0))
+        gather("s", cols("sa"), srow, la)
+        if k == 0:
+            gather("s", cols("pp"), cols("trow"), la)
+        turn(cols("sT"), cols("srow"))
+        turned("sl")
+        s0 = plane("sT", 0)
+        turned("sr")
+        vl = tt(val("vl"), s0, plane("slT", 0), A.subtract)
         fill()
-        m = tt(slot("mm"), slot("m"), plane("urT", 0), A.min)
+        vr = tt(val("vr"), s0, plane("srT", 0), A.subtract)
+        fill(2)
+        tt(slot(1, 0), vl, vr, A.is_equal)
+        tt(slot(1, 1), vl, vr, A.is_gt)
+        cv, cn = tt(plane("wu", 0), vl, vr, A.min), plane("wu", 9)
         fill()
-        tt(slot("e0"), v3(0), m, A.is_equal)
-        tt(slot("e1"), plane("ulT", 0), m, A.is_equal)
-        tt(slot("e2"), plane("urT", 0), m, A.is_equal)
-        tt(slot("t0"), slot("e0"), m3(0), A.mult)
-        tt(slot("t1"), slot("e1"), plane("ulT", 1), A.mult)
-        tt(slot("t2"), slot("e2"), plane("urT", 1), A.mult)
-        tt(slot("t3"), slot("t0"), slot("t1"), A.min)
+        scan(("wu", 1, C, 4), four(0), four(1))
+        fill(2)
+        turn(cols("urow"), cols("wu"))
+        if k == 0:
+            tree_facts()
+        else:
+            for b in range(2):
+                copy("s", cols("fo%d" % b), ps(1 + b))
+        gather("s", cols("ul"), urow, ll)
+        gather("s", cols("ur"), urow, lr)
+        for b in range(2 if k else 0, 3):
+            copy("s", cols("fo%d" % b), ps(1 + b))
+        turned("sa")
         fill()
-        tt(slot("t4"), slot("t2"), slot("t3"), A.min)
+        v0 = tt(val("v0"), plane("saT", 0), s0, A.subtract)
         fill()
-        Q0 = ts(sub("wc_", 0), slot("t4"), 256.0, A.add)
+        m = tt(val("m1"), v0, cv, A.min)
         fill()
-        turn(T.qrow[:, 0:C], ["qrow"], T.wc_[:], ["wc_.0", "wc_.i"])
-        gather("s", row("qa"), T.qrow[:, 0:C], ["qrow"], la, lak)
-        gather("s", row("qaa"), T.qa[:], ["qa"], la, lak)
+        turned("ul")
+        m = ts(val("m2"), m, -1.0e-30, A.min)
         fill()
-        gather("v", row("ql"), T.qrow[:], ["qrow", "qrow.n"], ll, llk)
-        gather("s", row("qr"), T.qrow[:], ["qrow", "qrow.n"], lr, lrk)
-        gather("s", row("qaaa"), T.qaa[:], ["qaa"], la, lak)
+        m = tt(val("m3"), m, plane("ulT", 0), A.min)
         fill(len(todo))
-        turned("qaT", "qa")
-        turned("qlT", "ql")
-        Qa, Qaa, Qaaa, Ql, Qr = plane("qaT", 0), plane("qaaT", 0), plane("qaaaT", 0), plane("qlT", 0), plane("qrT", 0)
-        eA = tt(slot("eA"), Q0, Qa, A.is_equal)
-        xn = tt(slot("xn"), Qa, nv, A.is_equal)
-        xl = tt(slot("xl"), Qa, lv, A.is_equal)
-        xp = tt(slot("xp"), Qa, slot("pin"), A.is_equal)
-        xr = tt(slot("xr"), Qa, rv, A.is_equal)
-        eL = tt(slot("eL"), Ql, Qa, A.is_equal)
-        rn = tt(slot("rn"), xn, eA, A.mult)
-        yq = tt(slot("yq"), Qa, pv, A.subtract)
-        yl = tt(slot("yl"), xl, eL, A.mult)
-        turned("qaaT", "qaa")
-        t = tt(slot("r0"), Qa, nv, A.subtract)
-        eB = tt(slot("eB"), Qaa, Qa, A.is_equal)
-        rot = tt(slot("rot"), rn, eB, A.mult)
-        xb = tt(slot("xb"), xp, eB, A.mult)
-        turned("qrT", "qr")
-        rd = tt(slot("rd"), rot, slot("dz"), A.mult)
-        eR = tt(slot("eR"), Qr, Qa, A.is_equal)
-        xbd = tt(slot("xbd"), xb, slot("dz"), A.mult)
-        yr = tt(slot("yr"), xr, eR, A.mult)
-        rd = tt(slot("rd2"), rd, pv, A.add)
-        yy = tt(slot("yy"), yl, yr, A.add)
-        fr = tt(slot("r1"), rot, slot("cn"), A.mult)
-        Y = tt(slot("Y"), yy, eA, A.mult)
-        rs1 = tt(slot("rs1"), rot, sv, A.mult)
-        yd = tt(slot("yd"), Y, yq, A.mult)
-        turned("qaaaT", "qaaa")
-        base = tt(slot("base"), rd, yd, A.add)
-        eC = tt(slot("eC"), Qaaa, Qa, A.is_equal)
-        t = tt(slot("r2"), Y, t, A.mult)
-        cd = tt(slot("cd"), xbd, eC, A.mult)
-        fr = tt(slot("r3"), fr, nv, A.add)
-        pn = tt(sub("ba%d" % nxt, 0), base, cd, A.add)
-        rs0 = tt(slot("rs0"), rot, rs1, A.subtract)
-        turned_back("ba%d" % nxt, "rw", [0], lambda: tt(sub("wr", 0), fr, t, A.add))
-        make_list(lak2, "ba%d" % nxt, [0])
-        send(dst, "arl%d" % k, T["al%d" % k][:], la2, [lak2])
-        wait("t", "arq%d" % k, 2 * len(topo.engines(core, dst)))
+        turned("ur")
+        m = tt(val("m4"), m, plane("urT", 0), A.min)
+        er = tt(val("er"), plane("urT", 0), m, A.is_equal)
+        el = tt(val("el"), plane("ulT", 0), m, A.is_equal)
+        ec = tt(val("ec"), cv, m, A.is_equal)
+        tt(slot(3, 3), er, plane("urT", 9), A.mult)
+        tt(slot(3, 2), el, plane("ulT", 9), A.mult)
+        tt(slot(3, 1), ec, cn, A.mult)
+        tt(slot(2, 1), v0, m, A.is_equal)
+        scan(four(0, "so"), four(2), four(3), A.min)
+        B = ts(plane("lanes", LB), slot(0, 3, "so"), 256.0, A.add)
+        X = tt(plane("lanes", LX), slot(0, 3, "so"), n2, A.is_equal)
+        turn(cols("qrow"), cols("lanes"))
+        gather("s", cols("qa"), cols("qrow"), la)
+        gather("s", cols("qr", *THREE[0:2]), qrow, part(lr, 0, THREE))
+        gather("s", cols("qaa"), cols("qa"), la)
+        gather("s", cols("qr", *THREE[1:3]), qrow, part(lr, 1, THREE))
+        gather("s", cols("qaaa"), cols("qaa"), la)
+        gl = tt(val("gl"), B, lv, A.is_equal)
+        gr = tt(val("gr"), B, rv, A.is_equal)
+        gather("v", cols("ql"), qrow, ll)
+        turned("qa")
+        tt(slot(6, 3), B, pv, A.subtract)
+        yn = tt(val("yn"), B, nv, A.subtract)
+        turned("ql")
+        e01 = tt(slot(6, 2), B, plane("qaT", LB), A.is_equal)
+        i1 = tt(val("i1"), plane("qaT", LC), nv, A.is_equal)
+        tt(slot(7, 0), gl, plane("qlT", LX), A.mult)
+        r1 = tt(slot(5, 1), X, e01, A.mult)
+        tt(slot(5, 0), i1, plane("qaT", LX), A.mult)
+        gather("v", cols("qr", *THREE[2:4]), qrow, part(lr, 2, THREE))
+        turned("qaa")
+        turned("qr")
+        e12 = tt(slot(4, 2), plane("qaT", LB), plane("qaaT", LB), A.is_equal)
+        tt(slot(7, 1), gr, plane("qrT", LX), A.mult)
+        rot = tt(val("rot"), r1, e12, A.mult)
+        scan(four(2, "so"), four(6), four(7))
+        turned("qaaa")
+        tt(slot(5, 3), pv, slot(2, 3, "so"), A.add)
+        f = tt(val("r1"), rot, val("cn"), A.mult)
+        tt(slot(4, 1), plane("qaaT", LB), plane("qaaaT", LB), A.is_equal)
+        t = tt(val("r0"), slot(2, 2, "so"), yn, A.mult)
+        rp = tt(val("rp"), rot, val("pc"), A.mult)
+        scan(cols("da", 0, 112), four(4), four(5))
+        t = tt(val("r2"), t, nv, A.add)
+        dl = tt(dense("dd", 0), rp, val("side"), A.mult)
+        turn(cols("eb", 16, 144), cols("da", 0, 128))
+        tt(plane("lanes", LR), f, t, A.add)
+        tt(dense("dd", 1), rp, dl, A.subtract)
+        turn(cols("da", 128, 288), cols("eb", 0, 160))
+        turn(cols("rrep"), cols("lanes"))
+        make_list(cols(la2[0], 0, 32), cols("da", 0, 288), cols("offa", 0, 2))
+        send(dst, "arl%d" % k, T["al%d" % k][:], ap(la2), [la2])
+        wait("t", "arq%d" % k, 2 * arrivals)
         fbank = [5, 6, 7, 0]
         for b in range(4):
-            mm(fbank[b], blk("eq", b), blk("es", b), T["aq%d" % k][:], T["as%d" % k][:], ["eq%d" % b])
+            mm(fbank[b], "eq", "es", b, "aq%d" % k, "as%d" % k)
         for b in range(4):
-            op("s", lambda: S.activation(T["fp%d" % b][:], ps(fbank[b]), ACT.Copy), ["ps%d" % fbank[b]], ["fp%d" % b])
-            dma("y", "cf%d" % b, T.fq[:, C * b:C * b + C], T["fp%d" % b][:], ["fp%d" % b], ["fq%d" % b])
-        turn(T.rrep[:, 0:C], ["rrep"], T.wr[:], ["wr.0", "wr.i"])
-        rk = ["rrep", "rrep.n"]
-        gather("s", row("repl"), T.rrep[:], rk, ll, llk)
-        gather("v", row("repr_"), T.rrep[:], rk, lr, lrk)
-        if not last:
-            bl2 = sub("bl%d" % nxt, 2)
-            op("s", lambda: S.activation(bl2[0], pn[0], ACT.Copy), [pn[1]], [bl2[1]])
-        turned("replT", "repl")
-        turned("reprT", "repr_")
-        Rl, Rr = plane("replT", 0), plane("reprT", 0)
-        lnew, rnew = sub("bl%d" % nxt, 0), sub("bl%d" % nxt, 1)
-        t1 = tt(slot("l0"), pv, Rl, A.subtract)
-        t2 = tt(slot("l1"), pv, Rr, A.subtract)
-        t1 = tt(slot("l2"), rs1, t1, A.mult)
-        t2 = tt(slot("l3"), rs0, t2, A.mult)
-        tt(lnew, Rl, t1, A.add)
-        tt(rnew, Rr, t2, A.add)
-        if last:
-            quantize(T.vq[:], T.vs[:], T.vt[:], ["vt"], ["vq"])
-        wait("v", "arl%d" % k, len(topo.engines(core, dst)))
-        wait("s", "arl%d" % k, len(topo.engines(core, dst)))
-        al = T["al%d" % k]
-        for b in range(4):
-            fp, fq, kb = T["fp%d" % b], T.fq[:, C * b:C * b + C], T.kb[:, C * b:C * b + C]
-            op("v", lambda: V.tensor_tensor(kb, fp[:].indirect(al[:]), fq, A.add), ["fp%d" % b, "fq%d" % b], ["kb%d" % b])
+            fp, fq = cols("fp%d" % b), cols("fq", C * b, C * b + C)
+            copy("s", fp, ps(fbank[b]))
             if b < 3:
-                op("s", lambda: S.activation(T.zt[:, b:4 * C:4], kb.indirect(al[:]), ACT.Copy, scale=0.5), ["kb%d" % b], ["zt%d" % b])
-        op("s", lambda: S.activation(T.zt[:, 4 * H + 3:4 * C:4], kb.indirect(al[:, 14:28]), ACT.Copy, scale=0.5), ["kb3"], ["zt4"])
-        op("v", lambda: V.tensor_scalar(T.zt[:, 3:4 * H:4], kb.indirect(al[:, 0:14]), 0.5, None, A.mult), ["kb3"], ["zt3"])
-        quantize(T.zq[:], T.zs[:], T.zt[:], ["zt%d" % b for b in range(5)], ["zq"])
-        mm(1, blk("wq", 0), blk("wp", 0), T.zq[:, 0:H], T.zs[:, 0:H], ["wq", "wp", "zq"], H)
-        mm(5, blk("wq", 0), blk("wp", 0), T.zq[:, H:C], T.zs[:, H:C], ["wq", "wp", "zq"], H)
-        wbank = [1, 2, 3, 6]
-        for b in range(1, 4):
-            mm(wbank[b], blk("wq", b), blk("wp", b), T.zq[:], T.zs[:], ["wq", "wp", "zq"])
-        op("s", lambda: S.activation(T.rr0[:, 0:H], ps(1, H), ACT.Copy, scale=0.03125), ["ps1"], ["rr0.a"])
-        op("s", lambda: S.activation(T.rr0[:, H:C], ps(5, H), ACT.Copy, scale=0.03125), ["ps5"], ["rr0.b"])
-        for b in range(1, 4):
-            op("s", lambda: S.activation(T["rr%d" % b][:], ps(wbank[b]), ACT.Copy, scale=0.03125), ["ps%d" % wbank[b]], ["rr%d" % b])
-        gather("s", row("sa"), T.rr3[:], ["rr3"], la2, lak2)
-        if not last:
-            turned_back("bl%d" % nxt, "rw2", [0, 1, 2])
-            make_list("lb%d" % nxt, "bl%d" % nxt, [0, 1])
-            gather("s", row("pp"), T.rw2[:, 32:480], ["rw2"], la2, lak2)
-            gather("s", row("raa"), T.pp[:], ["pp"], la2, lak2)
+                dmas("y", "cf%d" % b, [(ap(fq), ap(fp), [fp], [fq])])
+        gather("s", cols("repl"), rrep, ll)
+        gather("v", cols("repr_"), rrep, lr)
+        turn(cols("repT", 512, 512 + C), cols("repr_"))
+        turn(cols("repT"), cols("repl"))
+        tt(cols("dt", 32, 92), ("repT", LR, 512 + C, 16), cols("dd", 0, 60), A.add)
+        if last:
+            quantize("vq", "vs", "vt", 0, 128)
+            e = tt(val("f0"), pv, nv, A.is_equal)
+            h = ts(val("f1"), nv, -1.0, A.mult, 224.0, A.add)
+            copy("s", plane("lanes", LL), lv)
+            copy("s", plane("lanes", LE), rv)
+            e = tt(val("f2"), e, h, A.mult)
+            tt(plane("lanes", LP), pv, e, A.add)
         else:
-            e = tt(slot("f0"), pn, nv, A.is_equal)
-            h = ts(slot("f1"), nv, -1.0, A.mult, 224.0, A.add)
-            e = tt(slot("f2"), e, h, A.mult)
-            tt(sub("bl1", 2), pn, e, A.add)
-            turn(T.rp2[:], ["rp2"], T.bl1[:, 0:C], ["bl1.0", "bl1.1", "bl1.2", "bl1.i"])
-            op("s", lambda: S.activation(T.trf[:], T.rp2[:], ACT.Identity, bias=T.c224[:, 0:1]), ["rp2", "c224"], ["trf"])
-            for i in range(3):
-                lane = (i + 2) % 3
-                dma("y", "st_tr", T.tr[:, C * i:C * i + C], T.trf[lane:128:16, :], ["trf"], ["tr%d" % i])
-        for b in range(3):
-            rks = ["rr0.a", "rr0.b"] if b == 0 else ["rr%d" % b]
-            op("v", lambda: V.tensor_tensor(T.xn[:, b:4 * C:4], T["rr%d" % b][:].indirect(la2), T["fo%d" % b][:], A.add),
-               rks + ["fo%d" % b, lak2], ["xn%d" % b])
-        tt((T.xn[:, 3:4 * C:4], "xn3"), row("sa"), (ps(4), "ps4"), A.add)
-        quantize(T["q%d" % (k + 1)][:], T["qs%d" % (k + 1)][:], T.xn[:], ["xn%d" % b for b in range(4)], ["q%d" % (k + 1)])
+            tree_lanes()
+            turn(cols("eb", 48, 112), cols("dt", 32, 96))
+            child_order()
+            turn(cols("dt", 160, 256), cols("eb", 32, 128))
+        turn(cols("trow"), cols("lanes"))
         if not last:
-            pv, lv, rv = pn, lnew, rnew
+            make_list(cols("lb", 0, 64), cols("dt", 0, 256), cols("offm", 2, 6))
+        wait("v", "arl%d" % k, arrivals)
+        wait("s", "arl%d" % k, arrivals)
+        al = cols("al%d" % k, 0, 28)
+        kb = [cols("kb", C * b, C * b + C) for b in range(4)]
+        gather("s", cols("kg"), cols("fp3"), al)
+        for b in (0, 1, 3, 2):
+            if b == 3:
+                tt(kb[b], cols("kg"), ps(fbank[b]), A.add)
+            else:
+                gather_add(kb[b], cols("fp%d" % b), al, cols("fq", C * b, C * b + C))
+            if b != 2:
+                gather("s", ("zt", b, 4 * C, 4), kb[b], al, 0.5)
+        gather("s", piece("zt", 1, 2), kb[2], part(al, 1, CUT), 0.5)
+        gather("v", piece("zt", 0, 2), kb[2], part(al, 0, CUT), 0.5)
+        if last:
+            copy("s", cols("trf"), cols("trow"), bias=col(8))
+            dmas("y", "st_tr", [(T.tr[:, C * i:C * i + C], T.trf[LP + i:128:16, :], [cols("trf")], []) for i in range(3)])
+        else:
+            gather("s", cols("pp"), cols("trow"), la2)
+            tree_facts()
+        wbank = [1, 2, 3, 6]
+        for h in range(2):
+            quantize("zq", "zs", "zt", CUT[h], CUT[h + 1] - CUT[h])
+            mm([1, 5][h], "wq", "wp", 0, "zq", "zs", CUT[h], CUT[h + 1] - CUT[h])
+        for b in range(1, 4):
+            mm(wbank[b], "wq", "wp", b, "zq", "zs")
+        copy("s", piece("rr0", 0), ps(1, CUT[1]), scale=0.03125)
+        fill()
+        copy("v", piece("rr0", 1), ps(5, C - CUT[1]), scale=0.03125)
+        fill(3)
+        for b in range(1, 4):
+            copy("s", cols("rr%d" % b), ps(wbank[b]), scale=0.03125)
+        gather("s", cols("xg"), cols("rr3"), la2)
+        for b in range(3):
+            gather_add(("xn", b, 4 * C, 4), cols("rr%d" % b), la2, cols("fo%d" % b))
+        for h in range(2):
+            tt(piece("xn", h, 3), piece("xg", h), ("ps", 2048 + CUT[h], 2048 + CUT[h + 1], 1), A.add)
+        for h in range(2):
+            quantize("q%d" % (k + 1), "qs%d" % (k + 1), "xn", CUT[h], CUT[h + 1] - CUT[h])
 
-    mm(5, T.vq[:], T.vs[:], T.q3[:, 0:H], T.qs3[:, 0:H], ["vq", "q3"], H)
-    mm(6, T.vq[:], T.vs[:], T.q3[:, H:C], T.qs3[:, H:C], ["vq", "q3"], H)
-    dma("y", "st_oc", T.oc[:, 0:4 * C], T.q3[:, 0:C].bitcast(dt.uint8), ["q3"], ["oc"])
-    for i in range(4):
-        dma("y", "st_osc", T.osc[4 * i:4 * i + 4, :], T.qs3[32 * i:32 * i + 4, 0:C], ["q3"], ["osc%d" % i])
-    op("v", lambda: V.tensor_copy(T.yt[:, 0:H], ps(5, H)), ["ps5"], ["yt.a"])
-    op("s", lambda: S.activation(T.yt[:, H:C], ps(6, H), ACT.Copy), ["ps6"], ["yt.b"])
-    dma("s", "st_y", T.y[:], T.yt[:], ["yt.a", "yt.b"], ["yo"])
+    for h in range(2):
+        mm(5 + h, "vq", "vs", 0, "q3", "qs3", CUT[h], CUT[h + 1] - CUT[h])
+    dmas("y", "st_oc", [(T.oc[:, 0:4 * C], T.q3[:, 0:C].bitcast(dt.uint8), [cols("q3")], [])]
+         + [(T.osc[4 * i:4 * i + 4, :], T.qs3[32 * i:32 * i + 4, 0:C], [cols("qs3")], []) for i in range(4)])
+    copy("s", piece("yt", 0), ps(5, CUT[1]))
+    copy("v", piece("yt", 1), ps(6, C - CUT[1]))
+    dmas("s", "st_y", [(T.y[:, CUT[h]:CUT[h + 1]], ap(piece("yt", h)), [piece("yt", h)], []) for h in range(2)])
     for sem in sorted(count):
         wait("g", sem, count[sem])

@@ -2,11 +2,17 @@ from concourse.mybir import dt, AluOpType, ActivationFunctionType
 
 N = 4
 C = 448
-H = 224
-CUT = [0, 256, C]
-THREE = [0, 128, 288, C]
 STEP = [1, 2, 3]
 BIGV = 3.0e29
+CUT = [0, 256, C]
+CUT_SR = [0, 224, C]
+CUT_UR = [0, 160, C]
+CUT_AA = [0, 128, C]
+CUT_RR = [0, C, C]
+CUT_Z = [0, 256, C]
+CUT_X = [0, 320, C]
+CYCLE, SAME, CROSS, LOCAL, SHORT, LONG = 0.0009, 0.15, 0.2, 2.0, 1.8, 8.0
+PASSES = 3
 
 F32, BF, U16, I32, CODE, PLANE = "float32", "bfloat16", "uint16", "int32", "float8_e4m3fn_x4", "uint8"
 SCRATCH = {"ps": ("psum", [128, 4096], F32)}
@@ -29,28 +35,28 @@ _sbuf("pidx", 8, I32)
 _sbuf("col", 16, F32)
 _sbuf("i16 i32 jt nn", 28, F32)
 _sbuf("offm", 6, U16)
+_sbuf("offa", 2, U16)
 _sbuf("ti", 96, I32)
 _sbuf("al0 al1 al2", 28, U16)
 _sbuf("la0 la1 la2 la3", 32, U16)
-_sbuf("lb", 64, U16)
-_sbuf("di dt", 256, BF)
+_sbuf("lb lc", 64, U16)
+_sbuf("di dt dc", 256, BF)
 _sbuf("da", 288, BF)
-_sbuf("offa", 2, U16)
-_sbuf("eb", 160, BF)
-_sbuf("kg", C, BF)
+_sbuf("eb", 448, BF)
 _sbuf("dd", 64, F32)
 _sbuf("qrow rrep", 464, BF)
 _sbuf("srow urow", 456, F32)
-_sbuf("lanes trow pp ppT qa qaa qaaa ql qr qaT qaaT qaaaT qlT qrT repl repr_", C, BF)
+_sbuf("wq_ wr wt trow pp ppT qa qaa qaaa qc qaT qaaT qaaaT qcT repl repr_ kg", C, BF)
 _sbuf("repT", 512 + C, BF)
-_sbuf("sa sl sr ul ur xg sT saT slT srT ulT urT trf yt rr0 rr1 rr2 rr3 wu", C, F32)
+_sbuf("sa sl sr ul ur xg xh sT saT slT srT ulT urT trf yt rr0 rr1 rr2 rr3 wu", C, F32)
 _sbuf("sc", 1024, F32)
 _sbuf("so", 3 * 112, F32)
 _sbuf("cb", 28 * 40, F32)
 _sbuf("fo0 fo1 fo2 fp0 fp1 fp2 fp3", C, BF)
 
 SEMAPHORES = (["cv", "cs", "ct", "cg", "sent"] + ["ld_" + k for k in "x0 x1 u v t w".split()]
-              + ["st_" + k for k in "y oc tr".split()] + ["cf%d" % k for k in range(4)] + ["arq%d" % k for k in range(3)] + ["arl%d" % k for k in range(3)])
+              + ["st_" + k for k in "y0 y1 oc0 oc1 sc tr".split()] + ["cf%d" % k for k in range(3)]
+              + ["arq%d" % k for k in range(3)] + ["arl%d" % k for k in range(3)])
 
 
 def rank_program(g, core, T, topo):
@@ -62,9 +68,7 @@ def rank_program(g, core, T, topo):
     V, S = g.vector, g.scalar
     queue = {"v": V, "s": S, "t": g.tensor, "g": g, "y": g.sync}
 
-    count = {}
-    seen = {k: {} for k in queue}
-    facts = {}
+    calls = []
     uses = {}
     masks = {}
 
@@ -78,67 +82,123 @@ def rank_program(g, core, T, topo):
             masks[v[1:]] = sum(1 << c for c in range(v[1], v[2], v[3]))
         return masks[v[1:]]
 
-    def wait(q, sem, val):
-        s = seen[q]
-        if s.get(sem, 0) >= val:
-            return
-        queue[q].wait_ge(T.sem[sem], val)
-        s[sem] = val
-        for k, n in facts.get((sem, val), {}).items():
-            if s.get(k, 0) < n:
-                s[k] = n
-
-    def prepare(q, reads, writes):
-        need = {}
+    def record(q, issue, sem, inc, holds, takes, reads, writes):
+        after = {}
         for v, w in [(v, False) for v in reads] + [(v, True) for v in writes]:
-            m = columns(v)
-            for cols, sem, val, uq, wrote in uses.get(v[0], []):
-                if cols & m and (wrote or ((w or v[0] == "ps") and not (uq == q and sem == "c" + q))):
-                    need[sem] = max(need.get(sem, 0), val)
-        for sem in sorted(need, key=lambda s: (s == "c" + q, s)):
-            wait(q, sem, need[sem])
-
-    def note(q, sem, val, reads, writes):
-        facts[(sem, val)] = dict(seen[q])
+            for m, i, wrote in uses.get(v[0], []):
+                if m & columns(v) and (wrote or w or v[0] == "ps"):
+                    after[i] = after.get(i, False) or wrote or w or calls[i]["q"] != q
+        me = len(calls)
+        calls.append(dict(q=q, issue=issue, sem=sem, inc=inc, holds=holds, takes=takes, after=after))
         for v in writes:
             m = columns(v)
-            uses[v[0]] = [[u[0] & ~m] + u[1:] for u in uses.get(v[0], []) if u[0] & ~m] + [[m, sem, val, q, True]]
+            uses[v[0]] = [[u[0] & ~m] + u[1:] for u in uses.get(v[0], []) if u[0] & ~m] + [[m, me, True]]
         for v in reads:
-            uses.setdefault(v[0], []).append([columns(v), sem, val, q, False])
+            uses.setdefault(v[0], []).append([columns(v), me, False])
 
-    def op(q, fn, reads, writes):
-        prepare(q, reads, writes)
-        sem = "c" + q
-        count[sem] = count.get(sem, 0) + 1
-        fn().then_inc(T.sem[sem], 1)
-        note(q, sem, count[sem], reads, writes)
+    lines = {}
 
-    def dmas(q, sem, moves):
-        for out, in_, reads, writes in moves:
-            prepare(q, reads, writes)
-            queue[q].dma_start(out, in_).then_inc(T.sem[sem], 16)
-        count[sem] = count.get(sem, 0) + 16 * len(moves)
-        for out, in_, reads, writes in moves:
-            note(q, sem, count[sem], reads, writes)
+    def in_line(name):
+        if name in lines:
+            calls[-1]["after"].setdefault(lines[name], False)
+        lines[name] = len(calls) - 1
 
-    def send(dst, rsem, out, in_, reads):
-        prepare("g", reads, [])
+    def op(q, fn, reads, writes, cycles):
+        t = max(64, cycles) * CYCLE
+        record(q, lambda: fn().then_inc(T.sem["c" + q], 1), "c" + q, 1, t, t, reads, writes)
+
+    def dmas(q, sem, moves, takes=LOCAL):
+        def issue():
+            for m in moves:
+                queue[q].dma_start(m[0], m[1]).then_inc(T.sem[sem], 16)
+        record(q, issue, sem, 16 * len(moves), 0.05 * len(moves), takes, sum([m[2] for m in moves], []), sum([m[3] for m in moves], []))
+
+    def exchange(dst, sem, moves, takes):
         rid, pid, se = topo.addr(dst)
-        g.remote_dma(out, in_, T.sem[rsem], T.sem["sent"], pid, rid, topo.mask(core, dst))
-        count["sent"] = count.get("sent", 0) + len(topo.engines(core, dst))
+        n = len(moves) * len(topo.engines(core, dst))
+
+        def issue():
+            for m in moves:
+                g.remote_dma(m[0], m[1], T.sem[sem], T.sem["sent"], pid, rid, topo.mask(core, dst))
+        mark = (sem, 0, 1, 1)
+        record("g", issue, "sent", n, 0.1, 0.1, [m[2] for m in moves], [mark])
+        record(None, None, sem, n, 0.0, takes, [mark], [m[3] for m in moves])
+
+    def issue_all():
+        def gap(i, j):
+            if not calls[j]["after"][i] or calls[j]["q"] is None:
+                return 0.0
+            return SAME if calls[i]["q"] == calls[j]["q"] else CROSS
+        way = [c["takes"] for c in calls]
+        for j in reversed(range(len(calls))):
+            for i in calls[j]["after"]:
+                way[i] = max(way[i], calls[i]["takes"] + gap(i, j) + way[j])
+        before = [[] for c in calls]
+        for j, c in enumerate(calls):
+            for i in c["after"]:
+                before[i].append(j)
+
+        def place(order, back):
+            at, taken = {}, {q: [] for q in queue}
+            for j in order:
+                c = calls[j]
+                if back:
+                    t = max([at[i] + calls[i]["holds"] + gap(j, i) + c["takes"] - c["holds"] for i in before[j]] + [c["takes"] - c["holds"]])
+                else:
+                    t = max([at[i] + calls[i]["takes"] + gap(i, j) for i in c["after"]] + [0.0])
+                if c["q"] is not None:
+                    for a, b in taken[c["q"]]:
+                        if t + c["holds"] <= a + 1e-9:
+                            break
+                        t = max(t, b)
+                    taken[c["q"]] = sorted(taken[c["q"]] + [(t, t + c["holds"])])
+                at[j] = t
+            return at
+        every = range(len(calls))
+        start = place(sorted(every, key=lambda j: (-way[j], j)), False)
+        for _ in range(PASSES):
+            late = place(sorted(every, key=lambda j: (-start[j] - calls[j]["takes"], -j)), True)
+            start = place(sorted(every, key=lambda j: (-late[j] - calls[j]["holds"], j)), False)
+        count, seen, facts, mark = {}, {q: {} for q in queue}, {}, {}
+
+        def wait(q, sem, n):
+            if seen[q].get(sem, 0) < n:
+                queue[q].wait_ge(T.sem[sem], n)
+                for k, x in list(facts.get((sem, n), {}).items()) + [(sem, n)]:
+                    seen[q][k] = max(seen[q].get(k, 0), x)
+        for j in sorted(range(len(calls)), key=lambda j: (start[j], j)):
+            c = calls[j]
+            if c["q"] is not None:
+                need = {}
+                for i in c["after"]:
+                    if c["after"][i]:
+                        need[calls[i]["sem"]] = max(need.get(calls[i]["sem"], 0), mark[i])
+                for sem in sorted(need, key=lambda s: (s == "c" + c["q"], s)):
+                    wait(c["q"], sem, need[sem])
+                c["issue"]()
+            mark[j] = count[c["sem"]] = count.get(c["sem"], 0) + c["inc"]
+            facts[(c["sem"], mark[j])] = dict(seen.get(c["q"], {}))
+        for sem in sorted(count):
+            wait("g", sem, count[sem])
+
+    def size(v):
+        return len(range(v[1], v[2], v[3]))
+
+    def narrow(*views):
+        return 0.5 if all(SCRATCH[v[0]][2] in (BF, U16) for v in views) else 1.0
 
     def cols(buf, a=0, b=C):
         return buf, a, b, 1
 
-    def half(buf, h, w=1):
-        return buf, w * H * h, w * H * (h + 1), 1
-
-    def piece(buf, h, b=None):
-        a, z = CUT[h], CUT[h + 1]
+    def piece(buf, h, cut=CUT, b=None):
+        a, z = cut[h], cut[h + 1]
         return (buf, a, z, 1) if b is None else (buf, 4 * a + b, 4 * z, 4)
 
-    def ps(b, n=C):
-        return "ps", 512 * b, 512 * b + n, 1
+    def part(off, h, cut=CUT):
+        return off[0], off[1] + cut[h] // 16, off[1] + cut[h + 1] // 16, 1
+
+    def ps(b, n=C, a=0):
+        return "ps", 512 * b + a, 512 * b + a + n, 1
 
     def plane(buf, lane, at=0):
         return buf, at + lane, at + C, 16
@@ -162,379 +222,309 @@ def rank_program(g, core, T, topo):
         return buf, 112 * i, 112 * i + 112, 1
 
     def tt(out, a, b, o):
-        op("v", lambda: V.tensor_tensor(ap(out), ap(a), ap(b), o), [a, b], [out])
+        op("v", lambda: V.tensor_tensor(ap(out), ap(a), ap(b), o), [a, b], [out], size(out) * (1 if b[0] == "ps" else 2))
         return out
 
     def ts(out, a, s1, o1, s2=None, o2=None):
         more = [s for s in (s1, s2) if isinstance(s, tuple)]
         s1, s2 = [ap(s) if isinstance(s, tuple) else s for s in (s1, s2)]
-        if o2 is None:
-            op("v", lambda: V.tensor_scalar(ap(out), ap(a), s1, None, o1), [a] + more, [out])
-        else:
-            op("v", lambda: V.tensor_scalar(ap(out), ap(a), s1, s2, o1, o2), [a] + more, [out])
+        rest = (o1,) if o2 is None else (o1, o2)
+        op("v", lambda: V.tensor_scalar(ap(out), ap(a), s1, s2, *rest), [a] + more, [out], size(out) * narrow(out, a))
         return out
 
     def scan(out, d0, d1, o1=A.add):
-        op("v", lambda: V.tensor_tensor_scan(ap(out), ap(d0), ap(d1), 0.0, A.mult, o1), [d0, d1], [out])
+        op("v", lambda: V.tensor_tensor_scan(ap(out), ap(d0), ap(d1), 0.0, A.mult, o1), [d0, d1], [out], size(out))
 
     def turn(out, in_):
-        op("v", lambda: V.transpose(ap(out), ap(in_)), [in_], [out])
+        op("v", lambda: V.transpose(ap(out), ap(in_)), [in_], [out], size(out) * narrow(out))
 
     def turned(name):
         turn(cols(name + "T"), cols(name))
 
     def copy(q, out, in_, scale=1.0, bias=None):
-        if q == "v":
-            if scale == 1.0:
-                op("v", lambda: V.tensor_copy(ap(out), ap(in_)), [in_], [out])
-            else:
-                ts(out, in_, scale, A.mult)
+        if q == "v" and scale == 1.0:
+            op("v", lambda: V.tensor_copy(ap(out), ap(in_)), [in_], [out], size(out) * narrow(out, in_))
+        elif q == "v":
+            ts(out, in_, scale, A.mult)
         elif bias is None:
-            op("s", lambda: S.activation(ap(out), ap(in_), ACT.Copy, scale=scale), [in_], [out])
+            op("s", lambda: S.activation(ap(out), ap(in_), ACT.Copy, scale=scale), [in_], [out], size(out))
         else:
-            op("s", lambda: S.activation(ap(out), ap(in_), ACT.Identity, bias=ap(bias)), [in_, bias], [out])
+            op("s", lambda: S.activation(ap(out), ap(in_), ACT.Identity, bias=ap(bias)), [in_, bias], [out], size(out))
 
     def gather(q, out, win, off, scale=1.0):
+        cycles = 70 + 1.56 * size(out)
         if q == "s":
-            op("s", lambda: S.activation(ap(out), ap(win).indirect(ap(off)), ACT.Copy, scale=scale), [win, off], [out])
+            op("s", lambda: S.activation(ap(out), ap(win).indirect(ap(off)), ACT.Copy, scale=scale), [win, off], [out], cycles)
         elif scale == 1.0:
-            op("v", lambda: V.tensor_copy(ap(out), ap(win).indirect(ap(off))), [win, off], [out])
+            op("v", lambda: V.tensor_copy(ap(out), ap(win).indirect(ap(off))), [win, off], [out], cycles)
         else:
-            op("v", lambda: V.tensor_scalar(ap(out), ap(win).indirect(ap(off)), scale, None, A.mult), [win, off], [out])
+            op("v", lambda: V.tensor_scalar(ap(out), ap(win).indirect(ap(off)), scale, None, A.mult), [win, off], [out], cycles)
+
+    def shared(name, win, off, cut, line=None):
+        if cut[1]:
+            gather("v", piece(name, 0, cut), win, part(off, 0, cut))
+            if line:
+                in_line(line)
+        if cut[1] < C:
+            gather("s", piece(name, 1, cut), win, part(off, 1, cut))
 
     def gather_add(out, win, off, other):
-        op("v", lambda: V.tensor_tensor(ap(out), ap(win).indirect(ap(off)), ap(other), A.add), [win, off, other], [out])
-
-    def part(off, h, cut=(0, H, C)):
-        return off[0], off[1] + cut[h] // 16, off[1] + cut[h + 1] // 16, 1
+        op("v", lambda: V.tensor_tensor(ap(out), ap(win).indirect(ap(off)), ap(other), A.add), [win, off, other], [out], 70 + 1.8 * size(out))
 
     def memset(v, x):
-        op("v", lambda: V.memset(ap(v), x), [], [v])
+        op("v", lambda: V.memset(ap(v), x), [], [v], size(v) * narrow(v))
 
-    def mm(bank, l, ls, b, r, rs, a=0, n=C):
-        l, ls, r, rs = cols(l, 128 * b, 128 * b + 128), cols(ls, 128 * b, 128 * b + 128), cols(r, a, a + n), cols(rs, a, a + n)
-        op("t", lambda: g.tensor.matmul_mx(ap(ps(bank, n)), ap(l), ap(ls), ap(r), ap(rs), True, True), [l, ls, r, rs], [ps(bank)])
+    def mm(bank, l, ls, b, r, rs, a=0, z=C):
+        l, ls, r, rs = cols(l, 128 * b, 128 * b + 128), cols(ls, 128 * b, 128 * b + 128), cols(r, a, z), cols(rs, a, z)
+        op("t", lambda: g.tensor.matmul_mx(ap(ps(bank, z - a)), ap(l), ap(ls), ap(r), ap(rs), True, True), [l, ls, r, rs], [ps(bank)], 0.7 * (z - a + 16))
 
-    def quantize(out, scales, in_, a, n):
-        o, s, i = cols(out, a, a + n), cols(scales, a, a + n), cols(in_, 4 * a, 4 * (a + n))
-        op("v", lambda: V.quantize_mx(ap(o), ap(s), ap(i)), [i], [o, s])
+    def quantize(out, scales, a, z, in_):
+        o, s = cols(out, a, z), cols(scales, a, z)
+        op("v", lambda: V.quantize_mx(ap(o), ap(s), ap(in_)), [in_], [o, s], 15 + 1.06 * (z - a))
 
-    def swapped(buf, w, n):
-        turn(cols("eb", 16 + 32 * w, 16 + 32 * (w + n)), cols(buf, 32 * w, 32 * (w + n)))
-        turn(cols(buf, 128 + 32 * w, 160 + 32 * (w + n)), cols("eb", 32 * w, 32 + 32 * (w + n)))
+    def quantize_piece(out, scales, tile, h, cut=CUT):
+        quantize(out, scales, cut[h], cut[h + 1], cols(tile, 4 * cut[h], 4 * cut[h + 1]))
+
+    def swapped(buf, a, z, at):
+        turn(cols("eb", at + 16, at + 16 + z - a), cols(buf, a, z))
+        turn(cols(buf, 128 + a, 160 + z), cols("eb", at, at + 32 + z - a))
 
     def make_list(out, win, off):
-        op("v", lambda: V.tensor_scalar(ap(out), ap(win).indirect(ap(off)), 224.0, None, A.add), [win, off], [out])
-
-    todo = []
-
-    def later(f, *a):
-        todo.append(lambda: f(*a))
-
-    def fill(n=1):
-        for _ in range(n):
-            if todo:
-                todo.pop(0)()
+        op("v", lambda: V.tensor_scalar(ap(out), ap(win).indirect(ap(off)), 224.0, None, A.add), [win, off], [out], 60 + 1.56 * size(out))
 
     dmas("s", "ld_t", [(T.ti[:, 32 * i:32 * i + 28], T[k][:], [], [dense("ti", i)]) for i, k in enumerate(("up", "lf", "rt"))])
-    dmas("y", "ld_u", [(T.ut[:], T.u[:], [], [cols("ut", 0, 512)])])
+    dmas("y", "ld_u", [(T.ut[:], T.u[:], [], [cols("ut", 0, 512)])], LOCAL + 0.7)
     for h in range(2):
-        v = cols("xt", 4 * CUT[h], 4 * CUT[h + 1])
-        dmas("y", "ld_x%d" % h, [(ap(v), T.x[:, v[1]:v[2]], [], [v])])
-    wait("y", "ld_x1", 16)
-    dmas("y", "ld_w", [(T.wq[:, 0:512].bitcast(dt.uint8), T.wc[:], [], [cols("wq", 0, 512)]), (T.wp[:, 0:512], T.ws[:], [], [cols("wp", 0, 512)])])
-    dmas("y", "ld_v", [(T.vt[:], T.v[:], [], [cols("vt", 0, 512)])])
+        v = cols("xt", 4 * CUT_X[h], 4 * CUT_X[h + 1])
+        dmas("y", "ld_x%d" % h, [(ap(v), T.x[:, v[1]:v[2]], [], [v])], LOCAL + 0.9 + 0.6 * h)
+    dmas("y", "ld_w", [(T.wq[:, 0:512].bitcast(dt.uint8), T.wc[:], [v], [cols("wq", 0, 512)]), (T.wp[:, 0:512], T.ws[:], [], [cols("wp", 0, 512)])])
+    dmas("y", "ld_v", [(T.vt[:], T.v[:], [v], [cols("vt", 0, 512)])])
 
     ones = cols("ones", 0, 512)
     memset(ones, 1.0)
-    op("g", lambda: g.iota(T.pidx[:, 0:2], [[0, 2]], 0, 1), [], [cols("pidx", 0, 2)])
-    op("g", lambda: g.iota(T.i16[:], [[16, 28]], 0, 0, allow_small_or_imprecise_dtypes=True), [], [cols("i16", 0, 28)])
-    op("g", lambda: g.iota(T.i32[:], [[32, 14], [0, 2]], -224, 0, allow_small_or_imprecise_dtypes=True), [], [cols("i32", 0, 28)])
-    op("g", lambda: g.affine_select(T.et0[:], T.ones[:], [[-1, 512]], A.is_equal, 0.0, 0, 4), [ones], [cols("et0", 0, 512)])
-    for h in range(2):
-        copy("s", cols("sc", 512 * h, 512 * h + 512), ones, scale=0.0)
-    copy("s", cols("lanes"), cols("ones"), scale=0.0)
-    copy("s", cols("wu"), cols("ones"), scale=0.0)
+    op("g", lambda: g.iota(T.pidx[:, 0:2], [[0, 2]], 0, 1), [], [cols("pidx", 0, 2)], 160)
+    op("g", lambda: g.iota(T.i16[:], [[16, 28]], 0, 0, allow_small_or_imprecise_dtypes=True), [], [cols("i16", 0, 28)], 210)
+    op("g", lambda: g.iota(T.i32[:], [[32, 14], [0, 2]], -224, 0, allow_small_or_imprecise_dtypes=True), [], [cols("i32", 0, 28)], 210)
+    op("g", lambda: g.affine_select(T.et0[:], T.ones[:], [[-1, 512]], A.is_equal, 0.0, 0, 4), [ones], [cols("et0", 0, 512)], 1230)
     for b in range(1, 4):
         memset(cols("et%d" % b, 0, b), 0.0)
-    for b in range(1, 4):
         copy("s", cols("et%d" % b, b, 512), cols("et0", 0, 512 - b))
-    pd = cols("pidx", 0, 1)
+    for b in range(4):
+        quantize("eq", "es", 128 * b, 128 * b + 128, cols("et%d" % b, 0, 512))
+    for v in [cols("sc", 0, 512), cols("sc", 512, 1024)] + [cols(k) for k in ("wu", "wq_", "wr", "wt", "eb")]:
+        copy("s", v, cols("ones", 0, size(v)), scale=0.0)
+    for v in [cols("dt", 0, 256), cols("dc", 0, 128), cols("di", 96, 128), cols("da", 112, 128), cols("repT", C, 512),
+              cols("dd", 28, 32), cols("ti", 28, 32), cols("ti", 60, 64), cols("ti", 92, 96)]:
+        memset(v, 0 if v[0] == "ti" else 0.0)
+    for v, x in ((cols("srow", C, 456), -BIGV), (cols("urow", C, 456), BIGV), (cols("qrow", C, 464), 600.0), (cols("rrep", C, 464), 224.0),
+                 (col(8), 224.0), (col(9), -256.0), (col(13), 256.0), (slot(2, 2), 1.0), (slot(6, 3), 1.0)):
+        memset(v, x)
     for i, (sh, m) in enumerate(((0, 1), (4, 1), (0, 15), (0, 31))):
-        ts(cols("pidx", 2 + i, 3 + i), pd, sh, A.logical_shift_right, m, A.bitwise_and)
-    memset(("ti", 28, 32, 1), 0)
-    memset(("ti", 60, 64, 1), 0)
-    memset(("ti", 92, 96, 1), 0)
+        ts(cols("pidx", 2 + i, 3 + i), cols("pidx", 0, 1), sh, A.logical_shift_right, m, A.bitwise_and)
     copy("v", cols("col", 0, 4), cols("pidx", 2, 6))
-    memset(cols("dt", 0, 256), 0.0)
-    memset(cols("di", 96, 128), 0.0)
-    tt(col(4), col(0), col(1), A.not_equal)
-    ts(col(5), col(1), -30.0, A.mult, 159.0, A.add)
-    ts(col(10), col(1), -24.0, A.mult, 156.0, A.add)
-    ts(col(11), col(2), 4.0, A.mult, 3.0, A.add)
     jt = ts(cols("jt", 0, 28), cols("i16", 0, 28), col(2), A.add, -448.0, A.add)
     nv = ts(cols("nn", 0, 28), cols("i32", 0, 28), col(3), A.add)
+    tt(col(4), col(0), col(1), A.not_equal)
+    ts(col(5), col(1), -30.0, A.mult, 159.0, A.add)
     ts(col(7), col(4), col(5), A.mult, col(2), A.add)
-    ts(col(12), col(4), col(10), A.mult, col(11), A.add)
-    memset(cols("eb", 0, 160), 0.0)
-    memset(cols("da", 0, 288), 0.0)
-    memset(col(8), 224.0)
-    memset(col(9), -256.0)
     ts(cols("offm", 0, 6), cols("i16", 0, 6), col(7), A.add)
+    ts(col(10), col(1), -24.0, A.mult, 156.0, A.add)
+    ts(col(11), col(2), 4.0, A.mult, 3.0, A.add)
+    ts(col(12), col(4), col(10), A.mult, col(11), A.add)
     ts(cols("offa", 0, 2), cols("i16", 0, 2), 4.0, A.mult, col(12), A.add)
-    memset(cols("srow", C, 456), -BIGV)
-    memset(cols("urow", C, 456), BIGV)
-    memset(cols("qrow", C, 464), 600.0)
-    memset(cols("rrep", C, 464), 224.0)
-    memset(cols("repT", C, 512), 0.0)
-    memset(cols("dd", 28, 32), 0.0)
-    n2 = ts(slot(3, 0), nv, -256.0, A.add)
-    memset(slot(2, 2), 1.0)
-    memset(slot(2, 3), 1.0)
-    memset(slot(6, 1), 1.0)
+    n2 = ts(val("n2"), nv, -256.0, A.add)
+    copy("v", slot(7, 2), nv)
 
-    def quantize_constants(b):
-        o, s, i = cols("eq", 128 * b, 128 * b + 128), cols("es", 128 * b, 128 * b + 128), cols("et%d" % b, 0, 512)
-        op("v", lambda: V.quantize_mx(ap(o), ap(s), ap(i)), [i], [o, s])
-
+    quantize("uq", "us", 0, 128, cols("ut", 0, 512))
+    for h in range(2):
+        quantize_piece("q0", "qs0", "xt", h, CUT_X)
     ts(cols("di", 0, 96), cols("ti", 0, 96), -224.0, A.add)
     copy("v", cols("lb", 0, 64), cols("ti", 32, 96))
     e = ts(val("i0"), dense("di", 0), 224.0, A.is_equal)
-    quantize("uq", "us", "ut", 0, 128)
     e = tt(val("i1"), e, jt, A.mult)
-    quantize_constants(0)
     tt(dense("di", 0), dense("di", 0), e, A.add)
-    quantize_constants(1)
-    pv, lv, rv = ("da", 3, 112, 4), dense("dt", 1), dense("dt", 2)
-    turn(cols("eb", 16, 112), cols("di", 0, 96))
     ts(cols("la0", 0, 32), cols("di", 0, 32), 224.0, A.add)
-    turn(cols("di", 128, 256), cols("eb", 0, 128))
-    quantize("q0", "qs0", "xt", 0, CUT[1])
+    swapped("di", 0, 96, 0)
+    pv, lv, rv = ("da", 3, 112, 4), dense("dt", 1), dense("dt", 2)
     gather("v", cols("dt", 32, 96), cols("di", 0, 256), cols("offm", 2, 6))
     gather("v", ("da", 3, 128, 4), cols("di", 0, 256), cols("offm", 0, 2))
-    quantize("q0", "qs0", "xt", CUT[1], C - CUT[1])
 
-    LB, LX, LC, LR, LP, LL, LE = range(7)
-
-    def tree_lanes():
-        copy("s", slot(1, 2), lv, bias=col(9))
-        copy("s", plane("lanes", LL), lv)
-        copy("s", plane("lanes", LP), pv)
-
-    def tree_facts():
-        side, ppv = val("side"), plane("ppT", LP)
-        later(turned, "pp")
-        later(tt, side, plane("ppT", LL), nv, A.not_equal)
-        later(tt, ("sc", 953, 1008, 2), ppv, pv, A.subtract)
-        later(tt, ("sc", 897, 952, 2), nv, pv, A.subtract)
-        later(tt, val("d6"), side, slot(0, 2), A.mult)
-        later(ts, ("sc", 952, 1008, 2), ("sc", 953, 1008, 2), 0.0, A.is_equal)
-        later(tt, plane("lanes", LC), rv, val("d6"), A.subtract)
-        later(scan, ("sc", 449, 560, 2), cols("sc", 896, 952), cols("sc", 952, 1008))
-        later(tt, val("cn"), plane("lanes", LC), nv, A.subtract)
-        later(tt, val("pc"), pv, plane("lanes", LC), A.subtract)
-
-    def child_order():
-        tt(slot(0, 2), rv, lv, A.subtract)
-        tt(slot(0, 1), lv, rv, A.is_gt)
-
-    tree_lanes()
-    ll, lr = cols("lb", 0, 28), cols("lb", 32, 60)
+    LB, LX, LC = range(3)
+    LP, LL, LR = range(3)
+    ll, lr, lc, laa = cols("lb", 0, 28), cols("lb", 32, 60), cols("lc", 0, 28), cols("lc", 32, 60)
+    srow, urow, qrow, rrep = cols("srow", 0, 456), cols("urow", 0, 456), cols("qrow", 0, 464), cols("rrep", 0, 464)
     for k in range(3):
         last = k == 2
-        q, qs = "q%d" % k, "qs%d" % k
+        q, qs, aq, as_, al = "q%d" % k, "qs%d" % k, "aq%d" % k, "as%d" % k, cols("al%d" % k, 0, 28)
         dst = T.cores[(rank + STEP[k]) % N]
-        arrivals = len(topo.engines(core, dst))
         la, la2 = cols("la%d" % k, 0, 28), cols("la%d" % (k + 1), 0, 28)
-        send(dst, "arq%d" % k, T["aq%d" % k][:, 0:C].bitcast(dt.uint8), T[q][:, 0:C].bitcast(dt.uint8), [cols(q)])
-        send(dst, "arq%d" % k, T["as%d" % k][:, 0:C], T[qs][:, 0:C], [cols(qs)])
-        mm(0, "uq", "us", 0, q, qs, 0, CUT[1])
-        mm(7, "uq", "us", 0, q, qs, CUT[1], C - CUT[1])
-        if k == 0:
-            child_order()
-            quantize_constants(2)
-            quantize_constants(3)
-        else:
-            fill(2)
+        exchange(dst, "arq%d" % k, [(T[aq][:, 0:C].bitcast(dt.uint8), T[q][:, 0:C].bitcast(dt.uint8), cols(q), cols(aq)),
+                                    (T[as_][:, 0:C], T[qs][:, 0:C], cols(qs), cols(as_))], LONG)
+        copy("s", slot(1, 2), lv, bias=col(9))
+        apart = tt(slot(0, 2), rv, lv, A.subtract)
+        tt(slot(0, 1), lv, rv, A.is_gt)
+        down = tt(("sc", 897, 952, 2), nv, pv, A.subtract)
+        copy("s", plane("wt", LP), pv)
+        copy("v", plane("wt", LL), lv)
+        turn(cols("trow"), cols("wt"))
+        gather("s", cols("pp"), cols("trow"), la)
+        turned("pp")
+        ppv = plane("ppT", LP)
+        copy("s", dense("dc", 1), ppv)
+        side = tt(val("side"), plane("ppT", LL), nv, A.not_equal)
+        inner = tt(plane("wq_", LC), rv, tt(val("d6"), side, apart, A.mult), A.subtract)
+        to_inner = tt(val("cn"), inner, nv, A.subtract)
+        from_inner = tt(val("pc"), pv, inner, A.subtract)
+        up = tt(("sc", 953, 1008, 2), ppv, pv, A.subtract)
+        ts(("sc", 952, 1008, 2), up, 0.0, A.is_equal)
+        scan(("sc", 449, 560, 2), cols("sc", 896, 952), cols("sc", 952, 1008))
+        for h in range(2):
+            mm(7 * h, "uq", "us", 0, q, qs, CUT_X[h], CUT_X[h + 1])
+            copy("sv"[h], piece("srow", h, CUT_X), ps(7 * h, CUT_X[h + 1] - CUT_X[h]))
         for b in range(4):
             mm(1 + b, "eq", "es", b, q, qs)
-        srow, urow, qrow, rrep = cols("srow", 0, 456), cols("urow", 0, 456), cols("qrow", 0, 464), cols("rrep", 0, 464)
-        copy("s", piece("srow", 0), ps(0, CUT[1]))
-        copy("v", piece("srow", 1), ps(7, C - CUT[1]))
+        for b in range(2):
+            copy("s", cols("fo%d" % b), ps(1 + b))
+        copy("s", piece("fo2", 0, CUT_X), ps(3, CUT_X[1]))
         gather("s", cols("sl"), srow, ll)
-        gather("s", half("sr", 1), srow, part(lr, 1))
-        if k == 0:
-            turn(cols("trow"), cols("lanes"))
-        else:
-            fill()
-        gather("v", half("sr", 0), srow, part(lr, 0))
+        shared("sr", srow, lr, CUT_SR)
         gather("s", cols("sa"), srow, la)
-        if k == 0:
-            gather("s", cols("pp"), cols("trow"), la)
         turn(cols("sT"), cols("srow"))
-        turned("sl")
+        for n in ("sl", "sr"):
+            turned(n)
         s0 = plane("sT", 0)
-        turned("sr")
         vl = tt(val("vl"), s0, plane("slT", 0), A.subtract)
-        fill()
         vr = tt(val("vr"), s0, plane("srT", 0), A.subtract)
-        fill(2)
         tt(slot(1, 0), vl, vr, A.is_equal)
         tt(slot(1, 1), vl, vr, A.is_gt)
         cv, cn = tt(plane("wu", 0), vl, vr, A.min), plane("wu", 9)
-        fill()
         scan(("wu", 1, C, 4), four(0), four(1))
-        fill(2)
+        copy("s", dense("dc", 0), cn, bias=col(13))
+        swapped("dc", 0, 64, 288)
+        make_list(cols("lc", 0, 64), cols("dc", 0, 224), cols("offm", 0, 4))
         turn(cols("urow"), cols("wu"))
-        if k == 0:
-            tree_facts()
-        else:
-            for b in range(2):
-                copy("s", cols("fo%d" % b), ps(1 + b))
-        gather("s", cols("ul"), urow, ll)
-        gather("s", cols("ur"), urow, lr)
-        for b in range(2 if k else 0, 3):
-            copy("s", cols("fo%d" % b), ps(1 + b))
+        in_line("turns")
         turned("sa")
-        fill()
+        in_line("turns")
+        gather("s", cols("ul"), urow, ll)
+        shared("ur", urow, lr, CUT_UR, "turns")
+        for n in ("ul", "ur"):
+            turned(n)
         v0 = tt(val("v0"), plane("saT", 0), s0, A.subtract)
-        fill()
-        m = tt(val("m1"), v0, cv, A.min)
-        fill()
-        turned("ul")
-        m = ts(val("m2"), m, -1.0e-30, A.min)
-        fill()
-        m = tt(val("m3"), m, plane("ulT", 0), A.min)
-        fill(len(todo))
-        turned("ur")
-        m = tt(val("m4"), m, plane("urT", 0), A.min)
-        er = tt(val("er"), plane("urT", 0), m, A.is_equal)
-        el = tt(val("el"), plane("ulT", 0), m, A.is_equal)
-        ec = tt(val("ec"), cv, m, A.is_equal)
-        tt(slot(3, 3), er, plane("urT", 9), A.mult)
-        tt(slot(3, 2), el, plane("ulT", 9), A.mult)
-        tt(slot(3, 1), ec, cn, A.mult)
-        tt(slot(2, 1), v0, m, A.is_equal)
+        m = tt(val("m1"), v0, ts(val("m0"), cv, -1.0e-30, A.min), A.min)
+        t0 = tt(val("t0"), tt(val("e0"), v0, m, A.is_equal), n2, A.mult)
+        tt(slot(3, 0), t0, tt(val("t1"), tt(val("e1"), cv, m, A.is_equal), cn, A.mult), A.min)
+        ul, ur = plane("ulT", 0), plane("urT", 0)
+        tt(slot(3, 1), tt(val("e2"), ur, tt(val("m2"), m, ul, A.min), A.is_le), plane("urT", 9), A.mult)
+        tt(slot(3, 2), tt(val("e3"), ul, tt(val("m3"), m, ur, A.min), A.is_le), plane("ulT", 9), A.mult)
+        tt(slot(2, 1), m, tt(val("m4"), ul, ur, A.min), A.is_le)
         scan(four(0, "so"), four(2), four(3), A.min)
-        B = ts(plane("lanes", LB), slot(0, 3, "so"), 256.0, A.add)
-        X = tt(plane("lanes", LX), slot(0, 3, "so"), n2, A.is_equal)
-        turn(cols("qrow"), cols("lanes"))
+        first = slot(0, 2, "so")
+        B = ts(plane("wq_", LB), first, 256.0, A.add)
+        X = tt(plane("wq_", LX), first, n2, A.is_equal)
+        turn(cols("qrow"), cols("wq_"))
         gather("s", cols("qa"), cols("qrow"), la)
-        gather("s", cols("qr", *THREE[0:2]), qrow, part(lr, 0, THREE))
-        gather("s", cols("qaa"), cols("qa"), la)
-        gather("s", cols("qr", *THREE[1:3]), qrow, part(lr, 1, THREE))
-        gather("s", cols("qaaa"), cols("qaa"), la)
-        gl = tt(val("gl"), B, lv, A.is_equal)
-        gr = tt(val("gr"), B, rv, A.is_equal)
-        gather("v", cols("ql"), qrow, ll)
-        turned("qa")
-        tt(slot(6, 3), B, pv, A.subtract)
-        yn = tt(val("yn"), B, nv, A.subtract)
-        turned("ql")
-        e01 = tt(slot(6, 2), B, plane("qaT", LB), A.is_equal)
-        i1 = tt(val("i1"), plane("qaT", LC), nv, A.is_equal)
-        tt(slot(7, 0), gl, plane("qlT", LX), A.mult)
-        r1 = tt(slot(5, 1), X, e01, A.mult)
-        tt(slot(5, 0), i1, plane("qaT", LX), A.mult)
-        gather("v", cols("qr", *THREE[2:4]), qrow, part(lr, 2, THREE))
-        turned("qaa")
-        turned("qr")
+        in_line("claims")
+        gather("v", cols("qc"), qrow, lc)
+        in_line("turns")
+        shared("qaa", cols("qrow"), laa, CUT_AA, "turns")
+        in_line("claims")
+        gather("s", cols("qaaa"), cols("qa"), laa)
+        in_line("claims")
+        for n in ("qa", "qc", "qaa", "qaaa"):
+            turned(n)
+            in_line("turns")
+        e01 = tt(slot(6, 1), B, plane("qaT", LB), A.is_equal)
         e12 = tt(slot(4, 2), plane("qaT", LB), plane("qaaT", LB), A.is_equal)
-        tt(slot(7, 1), gr, plane("qrT", LX), A.mult)
-        rot = tt(val("rot"), r1, e12, A.mult)
-        scan(four(2, "so"), four(6), four(7))
-        turned("qaaa")
-        tt(slot(5, 3), pv, slot(2, 3, "so"), A.add)
-        f = tt(val("r1"), rot, val("cn"), A.mult)
         tt(slot(4, 1), plane("qaaT", LB), plane("qaaaT", LB), A.is_equal)
-        t = tt(val("r0"), slot(2, 2, "so"), yn, A.mult)
-        rp = tt(val("rp"), rot, val("pc"), A.mult)
+        tt(slot(7, 0), tt(val("gc"), first, cn, A.is_equal), plane("qcT", LX), A.mult)
+        tt(slot(6, 2), B, pv, A.subtract)
+        scan(four(2, "so"), four(6), four(7))
+        tt(slot(5, 3), slot(2, 2, "so"), down, A.subtract)
+        r1 = tt(slot(5, 1), X, e01, A.mult)
+        tt(slot(5, 0), tt(val("i1"), plane("qaT", LC), nv, A.is_equal), plane("qaT", LX), A.mult)
         scan(cols("da", 0, 112), four(4), four(5))
-        t = tt(val("r2"), t, nv, A.add)
-        dl = tt(dense("dd", 0), rp, val("side"), A.mult)
-        turn(cols("eb", 16, 144), cols("da", 0, 128))
-        tt(plane("lanes", LR), f, t, A.add)
-        tt(dense("dd", 1), rp, dl, A.subtract)
-        turn(cols("da", 128, 288), cols("eb", 0, 160))
-        turn(cols("rrep"), cols("lanes"))
+        swapped("da", 0, 128, 0)
         make_list(cols(la2[0], 0, 32), cols("da", 0, 288), cols("offa", 0, 2))
-        send(dst, "arl%d" % k, T["al%d" % k][:], ap(la2), [la2])
-        wait("t", "arq%d" % k, 2 * arrivals)
+        exchange(dst, "arl%d" % k, [(ap(al), ap(la2), la2, al)], SHORT)
+        rot = tt(val("rot"), r1, e12, A.mult)
+        tt(slot(6, 2), B, nv, A.subtract)
+        tt(slot(7, 3), rot, to_inner, A.mult)
+        scan(("wr", 0, C, 4), four(6), four(7))
+        turn(cols("rrep"), cols("wr"))
+        gather("s", cols("repl"), rrep, ll)
+        shared("repr_", rrep, lr, CUT_RR)
+        turn(cols("repT"), cols("repl"))
+        turn(cols("repT", 512, 512 + C), cols("repr_"))
+        rp = tt(val("rp"), rot, from_inner, A.mult)
+        tt(dense("dd", 1), rp, tt(dense("dd", 0), rp, side, A.mult), A.subtract)
+        tt(cols("dt", 32, 92), ("repT", 12, 512 + C, 16), cols("dd", 0, 60), A.add)
+        if last:
+            e = tt(val("f0"), pv, nv, A.is_equal)
+            e = tt(val("f2"), e, ts(val("f1"), nv, -1.0, A.mult, 224.0, A.add), A.mult)
+            tt(plane("wt", LP), pv, e, A.add)
+            copy("s", plane("wt", LL), lv)
+            copy("s", plane("wt", LR), rv)
+            turn(cols("trow"), cols("wt"))
+            copy("s", cols("trf"), cols("trow"), bias=col(8))
+            dmas("y", "st_tr", [(T.tr[:, C * i:C * i + C], T.trf[i:128:16, :], [cols("trf")], []) for i in range(3)])
+        else:
+            swapped("dt", 32, 96, 176)
+            make_list(cols("lb", 0, 64), cols("dt", 0, 256), cols("offm", 2, 6))
         fbank = [5, 6, 7, 0]
         for b in range(4):
-            mm(fbank[b], "eq", "es", b, "aq%d" % k, "as%d" % k)
-        for b in range(4):
+            mm(fbank[b], "eq", "es", b, aq, as_)
             fp, fq = cols("fp%d" % b), cols("fq", C * b, C * b + C)
             copy("s", fp, ps(fbank[b]))
             if b < 3:
-                dmas("y", "cf%d" % b, [(ap(fq), ap(fp), [fp], [fq])])
-        gather("s", cols("repl"), rrep, ll)
-        gather("v", cols("repr_"), rrep, lr)
-        turn(cols("repT", 512, 512 + C), cols("repr_"))
-        turn(cols("repT"), cols("repl"))
-        tt(cols("dt", 32, 92), ("repT", LR, 512 + C, 16), cols("dd", 0, 60), A.add)
-        if last:
-            quantize("vq", "vs", "vt", 0, 128)
-            e = tt(val("f0"), pv, nv, A.is_equal)
-            h = ts(val("f1"), nv, -1.0, A.mult, 224.0, A.add)
-            copy("s", plane("lanes", LL), lv)
-            copy("s", plane("lanes", LE), rv)
-            e = tt(val("f2"), e, h, A.mult)
-            tt(plane("lanes", LP), pv, e, A.add)
-        else:
-            tree_lanes()
-            turn(cols("eb", 48, 112), cols("dt", 32, 96))
-            child_order()
-            turn(cols("dt", 160, 256), cols("eb", 32, 128))
-        turn(cols("trow"), cols("lanes"))
-        if not last:
-            make_list(cols("lb", 0, 64), cols("dt", 0, 256), cols("offm", 2, 6))
-        wait("v", "arl%d" % k, arrivals)
-        wait("s", "arl%d" % k, arrivals)
-        al = cols("al%d" % k, 0, 28)
+                dmas("y", "cf%d" % b, [(ap(fq), ap(fp), [fp], [fq])], LOCAL + 0.6)
         kb = [cols("kb", C * b, C * b + C) for b in range(4)]
         gather("s", cols("kg"), cols("fp3"), al)
         for b in (0, 1, 3, 2):
             if b == 3:
-                tt(kb[b], cols("kg"), ps(fbank[b]), A.add)
+                tt(kb[3], cols("kg"), ps(fbank[3]), A.add)
             else:
                 gather_add(kb[b], cols("fp%d" % b), al, cols("fq", C * b, C * b + C))
-            if b != 2:
-                gather("s", ("zt", b, 4 * C, 4), kb[b], al, 0.5)
-        gather("s", piece("zt", 1, 2), kb[2], part(al, 1, CUT), 0.5)
-        gather("v", piece("zt", 0, 2), kb[2], part(al, 0, CUT), 0.5)
-        if last:
-            copy("s", cols("trf"), cols("trow"), bias=col(8))
-            dmas("y", "st_tr", [(T.tr[:, C * i:C * i + C], T.trf[LP + i:128:16, :], [cols("trf")], []) for i in range(3)])
-        else:
-            gather("s", cols("pp"), cols("trow"), la2)
-            tree_facts()
-        wbank = [1, 2, 3, 6]
+            in_line("sums")
+        for b in (0, 1, 3):
+            gather("s", ("zt", b, 4 * C, 4), kb[b], al, 0.5)
         for h in range(2):
-            quantize("zq", "zs", "zt", CUT[h], CUT[h + 1] - CUT[h])
-            mm([1, 5][h], "wq", "wp", 0, "zq", "zs", CUT[h], CUT[h + 1] - CUT[h])
-        for b in range(1, 4):
+            gather("vs"[h], piece("zt", h, CUT_Z, 2), kb[2], part(al, h, CUT_Z), 0.5)
+        wbank = [1, 2, 7, 6]
+        for h in range(2):
+            quantize_piece("zq", "zs", "zt", h)
+            mm([1, 5][h], "wq", "wp", 0, "zq", "zs", CUT[h], CUT[h + 1])
+            in_line("layer")
+            copy("sv"[h], piece("rr0", h), ps([1, 5][h], CUT[h + 1] - CUT[h]), scale=0.03125)
+        for b in (1, 2, 3):
             mm(wbank[b], "wq", "wp", b, "zq", "zs")
-        copy("s", piece("rr0", 0), ps(1, CUT[1]), scale=0.03125)
-        fill()
-        copy("v", piece("rr0", 1), ps(5, C - CUT[1]), scale=0.03125)
-        fill(3)
-        for b in range(1, 4):
+            in_line("layer")
             copy("s", cols("rr%d" % b), ps(wbank[b]), scale=0.03125)
+            in_line("claims")
+        gather("s", piece("xh", 1, CUT_X), cols("rr2"), part(la2, 1, CUT_X))
+        in_line("claims")
         gather("s", cols("xg"), cols("rr3"), la2)
-        for b in range(3):
+        in_line("claims")
+        for b in range(2):
             gather_add(("xn", b, 4 * C, 4), cols("rr%d" % b), la2, cols("fo%d" % b))
+            in_line("turns")
+        gather_add(piece("xn", 0, CUT_X, 2), cols("rr2"), part(la2, 0, CUT_X), piece("fo2", 0, CUT_X))
+        in_line("turns")
         for h in range(2):
-            tt(piece("xn", h, 3), piece("xg", h), ("ps", 2048 + CUT[h], 2048 + CUT[h + 1], 1), A.add)
-        for h in range(2):
-            quantize("q%d" % (k + 1), "qs%d" % (k + 1), "xn", CUT[h], CUT[h + 1] - CUT[h])
+            tt(piece("xn", h, CUT_X, 3), piece("xg", h, CUT_X), ps(4, CUT_X[h + 1] - CUT_X[h], CUT_X[h]), A.add)
+            in_line("turns")
+            if h == 0:
+                tt(piece("xn", 1, CUT_X, 2), piece("xh", 1, CUT_X), ps(3, C - CUT_X[1], CUT_X[1]), A.add)
+                in_line("turns")
+            quantize_piece("q%d" % (k + 1), "qs%d" % (k + 1), "xn", h, CUT_X)
+            in_line("turns")
 
+    quantize("vq", "vs", 0, 128, cols("vt", 0, 512))
     for h in range(2):
-        mm(5 + h, "vq", "vs", 0, "q3", "qs3", CUT[h], CUT[h + 1] - CUT[h])
-    dmas("y", "st_oc", [(T.oc[:, 0:4 * C], T.q3[:, 0:C].bitcast(dt.uint8), [cols("q3")], [])]
-         + [(T.osc[4 * i:4 * i + 4, :], T.qs3[32 * i:32 * i + 4, 0:C], [cols("qs3")], []) for i in range(4)])
-    copy("s", piece("yt", 0), ps(5, CUT[1]))
-    copy("v", piece("yt", 1), ps(6, C - CUT[1]))
-    dmas("s", "st_y", [(T.y[:, CUT[h]:CUT[h + 1]], ap(piece("yt", h)), [piece("yt", h)], []) for h in range(2)])
-    for sem in sorted(count):
-        wait("g", sem, count[sem])
+        a, z = CUT_X[h], CUT_X[h + 1]
+        mm(5 + h, "vq", "vs", 0, "q3", "qs3", a, z)
+        copy("sv"[h], cols("yt", a, z), ps(5 + h, z - a))
+        dmas("sy"[h], "st_y%d" % h, [(T.y[:, a:z], T.yt[:, a:z], [cols("yt", a, z)], [])], LOCAL + 0.5)
+        dmas("y", "st_oc%d" % h, [(T.oc[:, 4 * a:4 * z], T.q3[:, a:z].bitcast(dt.uint8), [cols("q3", a, z)], [])], LOCAL + 0.5)
+    dmas("y", "st_sc", [(T.osc[4 * i:4 * i + 4, :], T.qs3[32 * i:32 * i + 4, 0:C], [cols("qs3")], []) for i in range(4)])
+    issue_all()

@@ -4,14 +4,14 @@ N = 4
 C = 448
 STEP = [1, 2, 3]
 BIGV = 3.0e29
-CUT = [0, 256, C]
-CUT_SR = [0, 224, C]
+CUT = [0, 192, 320, C]
+CUT_SR = [0, 288, C]
 CUT_UR = [0, 160, C]
-CUT_AA = [0, 128, C]
+CUT_AA = [0, 192, C]
 CUT_RR = [0, C, C]
-CUT_Z = [0, 256, C]
-CUT_X = [0, 320, C]
-CYCLE, SAME, CROSS, LOCAL, SHORT, LONG = 0.0009, 0.15, 0.2, 2.0, 1.8, 8.0
+CUT_Z = [0, 320, C]
+CUT_X = [0, 192, C]
+CYCLE, SAME, CROSS, LOCAL, SHORT, LONG = 0.00087, 0.2, 0.2, 2.0, 1.6, 8.0
 PASSES = 3
 
 F32, BF, U16, I32, CODE, PLANE = "float32", "bfloat16", "uint16", "int32", "float8_e4m3fn_x4", "uint8"
@@ -48,14 +48,15 @@ _sbuf("qrow rrep", 464, BF)
 _sbuf("srow urow", 456, F32)
 _sbuf("wq_ wr wt trow pp ppT qa qaa qaaa qc qaT qaaT qaaaT qcT repl repr_ kg", C, BF)
 _sbuf("repT", 512 + C, BF)
-_sbuf("sa sl sr ul ur xg xh sT saT slT srT ulT urT trf yt rr0 rr1 rr2 rr3 wu", C, F32)
+_sbuf("sa sl sr ul ur xg xh sT saT slT srT ulT urT trf yt rr0 rr1 rr2 rr3 wu sw zf", C, F32)
 _sbuf("sc", 1024, F32)
-_sbuf("so", 3 * 112, F32)
+_sbuf("so", 4 * 112, F32)
+_sbuf("sx", 224, F32)
 _sbuf("cb", 28 * 40, F32)
 _sbuf("fo0 fo1 fo2 fp0 fp1 fp2 fp3", C, BF)
 
-SEMAPHORES = (["cv", "cs", "ct", "cg", "sent"] + ["ld_" + k for k in "x0 x1 u v t w".split()]
-              + ["st_" + k for k in "y0 y1 oc0 oc1 sc tr".split()] + ["cf%d" % k for k in range(3)]
+SEMAPHORES = (["cv", "cs", "ct", "cg", "sent"] + ["ld_" + k for k in "x0 x1 x2 u v t w z0 z1 z2".split()]
+              + ["st_" + k for k in "y0 y1 y2 oc0 oc1 oc2 sc tr".split()] + ["cf%d" % k for k in range(3)]
               + ["arq%d" % k for k in range(3)] + ["arl%d" % k for k in range(3)])
 
 
@@ -125,14 +126,16 @@ def rank_program(g, core, T, topo):
         record(None, None, sem, n, 0.0, takes, [mark], [m[3] for m in moves])
 
     def issue_all():
-        def gap(i, j):
-            if not calls[j]["after"][i] or calls[j]["q"] is None:
-                return 0.0
-            return SAME if calls[i]["q"] == calls[j]["q"] else CROSS
+        def span(i, j):
+            if calls[j]["q"] is None:
+                return calls[i]["takes"]
+            if not calls[j]["after"][i]:
+                return calls[i]["holds"]
+            return calls[i]["takes"] + (SAME if calls[i]["q"] == calls[j]["q"] else CROSS)
         way = [c["takes"] for c in calls]
         for j in reversed(range(len(calls))):
             for i in calls[j]["after"]:
-                way[i] = max(way[i], calls[i]["takes"] + gap(i, j) + way[j])
+                way[i] = max(way[i], span(i, j) + way[j])
         before = [[] for c in calls]
         for j, c in enumerate(calls):
             for i in c["after"]:
@@ -143,9 +146,9 @@ def rank_program(g, core, T, topo):
             for j in order:
                 c = calls[j]
                 if back:
-                    t = max([at[i] + calls[i]["holds"] + gap(j, i) + c["takes"] - c["holds"] for i in before[j]] + [c["takes"] - c["holds"]])
+                    t = max([at[i] + calls[i]["holds"] + span(j, i) - c["holds"] for i in before[j]] + [c["takes"] - c["holds"]])
                 else:
-                    t = max([at[i] + calls[i]["takes"] + gap(i, j) for i in c["after"]] + [0.0])
+                    t = max([at[i] + span(i, j) for i in c["after"]] + [0.0])
                 if c["q"] is not None:
                     for a, b in taken[c["q"]]:
                         if t + c["holds"] <= a + 1e-9:
@@ -157,7 +160,7 @@ def rank_program(g, core, T, topo):
         every = range(len(calls))
         start = place(sorted(every, key=lambda j: (-way[j], j)), False)
         for _ in range(PASSES):
-            late = place(sorted(every, key=lambda j: (-start[j] - calls[j]["takes"], -j)), True)
+            late = place(sorted(every, key=lambda j: (-start[j] - calls[j]["holds"], -j)), True)
             start = place(sorted(every, key=lambda j: (-late[j] - calls[j]["holds"], j)), False)
         count, seen, facts, mark = {}, {q: {} for q in queue}, {}, {}
 
@@ -232,8 +235,8 @@ def rank_program(g, core, T, topo):
         op("v", lambda: V.tensor_scalar(ap(out), ap(a), s1, s2, *rest), [a] + more, [out], size(out) * narrow(out, a))
         return out
 
-    def scan(out, d0, d1, o1=A.add):
-        op("v", lambda: V.tensor_tensor_scan(ap(out), ap(d0), ap(d1), 0.0, A.mult, o1), [d0, d1], [out], size(out))
+    def scan(out, d0, d1, o0=A.mult, o1=A.add):
+        op("v", lambda: V.tensor_tensor_scan(ap(out), ap(d0), ap(d1), 0.0, o0, o1), [d0, d1], [out], size(out))
 
     def turn(out, in_):
         op("v", lambda: V.transpose(ap(out), ap(in_)), [in_], [out], size(out) * narrow(out))
@@ -269,10 +272,13 @@ def rank_program(g, core, T, topo):
             gather("s", piece(name, 1, cut), win, part(off, 1, cut))
 
     def gather_add(out, win, off, other):
-        op("v", lambda: V.tensor_tensor(ap(out), ap(win).indirect(ap(off)), ap(other), A.add), [win, off, other], [out], 70 + 1.8 * size(out))
+        op("v", lambda: V.tensor_tensor(ap(out), ap(win).indirect(ap(off)), ap(other), A.add), [win, off, other], [out], 60 + 1.6 * size(out))
 
     def memset(v, x):
         op("v", lambda: V.memset(ap(v), x), [], [v], size(v) * narrow(v))
+
+    def iota(v, pattern, base):
+        op("g", lambda: g.iota(ap(v), pattern, base, 0, allow_small_or_imprecise_dtypes=True), [], [v], 160 + 2 * size(v))
 
     def mm(bank, l, ls, b, r, rs, a=0, z=C):
         l, ls, r, rs = cols(l, 128 * b, 128 * b + 128), cols(ls, 128 * b, 128 * b + 128), cols(r, a, z), cols(rs, a, z)
@@ -292,52 +298,66 @@ def rank_program(g, core, T, topo):
     def make_list(out, win, off):
         op("v", lambda: V.tensor_scalar(ap(out), ap(win).indirect(ap(off)), 224.0, None, A.add), [win, off], [out], 60 + 1.56 * size(out))
 
+    memset(cols("ti", 0, 96), 0)
     dmas("s", "ld_t", [(T.ti[:, 32 * i:32 * i + 28], T[k][:], [], [dense("ti", i)]) for i, k in enumerate(("up", "lf", "rt"))])
-    dmas("y", "ld_u", [(T.ut[:], T.u[:], [], [cols("ut", 0, 512)])], LOCAL + 0.7)
-    for h in range(2):
-        v = cols("xt", 4 * CUT_X[h], 4 * CUT_X[h + 1])
-        dmas("y", "ld_x%d" % h, [(ap(v), T.x[:, v[1]:v[2]], [], [v])], LOCAL + 0.9 + 0.6 * h)
-    dmas("y", "ld_w", [(T.wq[:, 0:512].bitcast(dt.uint8), T.wc[:], [v], [cols("wq", 0, 512)]), (T.wp[:, 0:512], T.ws[:], [], [cols("wp", 0, 512)])])
-    dmas("y", "ld_v", [(T.vt[:], T.v[:], [v], [cols("vt", 0, 512)])])
+    dmas("y", "ld_u", [(T.ut[:], T.u[:], [], [cols("ut", 0, 512)])], LOCAL + 0.4)
+    in_line("loads")
+    for h in range(3):
+        v = cols("xt", 4 * CUT[h], 4 * CUT[h + 1])
+        dmas("y", "ld_x%d" % h, [(ap(v), T.x[:, v[1]:v[2]], [], [v])], LOCAL + 0.8 + 0.35 * h)
+        in_line("loads")
+    last_x = v
 
     ones = cols("ones", 0, 512)
     memset(ones, 1.0)
     op("g", lambda: g.iota(T.pidx[:, 0:2], [[0, 2]], 0, 1), [], [cols("pidx", 0, 2)], 160)
-    op("g", lambda: g.iota(T.i16[:], [[16, 28]], 0, 0, allow_small_or_imprecise_dtypes=True), [], [cols("i16", 0, 28)], 210)
-    op("g", lambda: g.iota(T.i32[:], [[32, 14], [0, 2]], -224, 0, allow_small_or_imprecise_dtypes=True), [], [cols("i32", 0, 28)], 210)
+    iota(cols("i16", 0, 28), [[16, 28]], 0)
+    iota(cols("i32", 0, 28), [[32, 14], [0, 2]], -224)
+    in_line("first")
     op("g", lambda: g.affine_select(T.et0[:], T.ones[:], [[-1, 512]], A.is_equal, 0.0, 0, 4), [ones], [cols("et0", 0, 512)], 1230)
+    in_line("first")
+    for k in ("eb", "zf", "wr"):
+        copy("s", cols(k), cols("ones"), scale=0.0)
+        in_line("claims")
     for b in range(1, 4):
         memset(cols("et%d" % b, 0, b), 0.0)
         copy("s", cols("et%d" % b, b, 512), cols("et0", 0, 512 - b))
-    for b in range(4):
-        quantize("eq", "es", 128 * b, 128 * b + 128, cols("et%d" % b, 0, 512))
-    for v in [cols("sc", 0, 512), cols("sc", 512, 1024)] + [cols(k) for k in ("wu", "wq_", "wr", "wt", "eb")]:
-        copy("s", v, cols("ones", 0, size(v)), scale=0.0)
-    for v in [cols("dt", 0, 256), cols("dc", 0, 128), cols("di", 96, 128), cols("da", 112, 128), cols("repT", C, 512),
-              cols("dd", 28, 32), cols("ti", 28, 32), cols("ti", 60, 64), cols("ti", 92, 96)]:
-        memset(v, 0 if v[0] == "ti" else 0.0)
-    for v, x in ((cols("srow", C, 456), -BIGV), (cols("urow", C, 456), BIGV), (cols("qrow", C, 464), 600.0), (cols("rrep", C, 464), 224.0),
-                 (col(8), 224.0), (col(9), -256.0), (col(13), 256.0), (slot(2, 2), 1.0), (slot(6, 3), 1.0)):
-        memset(v, x)
+        in_line("claims")
+    for sem, zero, views in (("ld_z0", "zf", [cols("wu")]), ("ld_z1", "wr", [cols("wt"), cols("wq_"), cols("dc", 0, 128), cols("repT", C, 512)]),
+                             ("ld_z2", "zf", [cols("sc", C, 2 * C), cols("sc", 2 * C, 1024), cols("sw"), cols("sx", 0, 224), cols("dd", 28, 32)])):
+        dmas("y", sem, [(ap(v), T[zero][:, 0:size(v)], [cols(zero, 0, size(v)), last_x], [v]) for v in views], LOCAL + 1.5)
+    for v in (cols("di", 96, 128), cols("dt", 0, 256), cols("da", 112, 128)):
+        memset(v, 0.0)
+    memset(cols("srow", C, 456), -BIGV)
+    dmas("y", "ld_w", [(T.wq[:, 0:512].bitcast(dt.uint8), T.wc[:], [cols("wq_")], [cols("wq", 0, 512)]), (T.wp[:, 0:512], T.ws[:], [], [cols("wp", 0, 512)])])
+    dmas("y", "ld_v", [(T.vt[:], T.v[:], [cols("wq_")], [cols("vt", 0, 512)])])
+    for v, x, step in ((cols("qrow", C, 464), 600, 0), (cols("rrep", C, 464), 224, 0), (col(8), 224, 0), (cols("col", 9, 11), -256, 512),
+                       (("sw", 0, 224, 8), 4096, 0), (("sw", 4, 224, 8), 256, 0), (("sw", 228, C, 8), 4096, 0)):
+        iota(v, [[step, size(v)]], x)
     for i, (sh, m) in enumerate(((0, 1), (4, 1), (0, 15), (0, 31))):
         ts(cols("pidx", 2 + i, 3 + i), cols("pidx", 0, 1), sh, A.logical_shift_right, m, A.bitwise_and)
     copy("v", cols("col", 0, 4), cols("pidx", 2, 6))
+    ts(cols("urow", C, 456), cols("ones", 0, 8), ts(col(14), col(2), 2.0, A.is_equal, BIGV, A.mult), A.mult)
     jt = ts(cols("jt", 0, 28), cols("i16", 0, 28), col(2), A.add, -448.0, A.add)
     nv = ts(cols("nn", 0, 28), cols("i32", 0, 28), col(3), A.add)
     tt(col(4), col(0), col(1), A.not_equal)
     ts(col(5), col(1), -30.0, A.mult, 159.0, A.add)
     ts(col(7), col(4), col(5), A.mult, col(2), A.add)
     ts(cols("offm", 0, 6), cols("i16", 0, 6), col(7), A.add)
-    ts(col(10), col(1), -24.0, A.mult, 156.0, A.add)
+    ts(col(13), col(1), -24.0, A.mult, 156.0, A.add)
     ts(col(11), col(2), 4.0, A.mult, 3.0, A.add)
-    ts(col(12), col(4), col(10), A.mult, col(11), A.add)
+    ts(col(12), col(4), col(13), A.mult, col(11), A.add)
     ts(cols("offa", 0, 2), cols("i16", 0, 2), 4.0, A.mult, col(12), A.add)
     n2 = ts(val("n2"), nv, -256.0, A.add)
-    copy("v", slot(7, 2), nv)
+    copy("s", ("sx", 57, 112, 2), nv)
 
     quantize("uq", "us", 0, 128, cols("ut", 0, 512))
-    for h in range(2):
-        quantize_piece("q0", "qs0", "xt", h, CUT_X)
+    for h in range(3):
+        quantize_piece("q0", "qs0", "xt", h)
+        in_line("start")
+    for b in range(4):
+        quantize("eq", "es", 128 * b, 128 * b + 128, cols("et%d" % b, 0, 512))
+        in_line("start")
     ts(cols("di", 0, 96), cols("ti", 0, 96), -224.0, A.add)
     copy("v", cols("lb", 0, 64), cols("ti", 32, 96))
     e = ts(val("i0"), dense("di", 0), 224.0, A.is_equal)
@@ -349,7 +369,11 @@ def rank_program(g, core, T, topo):
     gather("v", cols("dt", 32, 96), cols("di", 0, 256), cols("offm", 2, 6))
     gather("v", ("da", 3, 128, 4), cols("di", 0, 256), cols("offm", 0, 2))
 
-    LB, LX, LC = range(3)
+    def better_child(buf, i):
+        scan(four(i, "so"), (buf, 0, C, 4), (buf, 1, C, 4))
+        return slot(i, 2, "so")
+
+    LB, LC = 8, 1
     LP, LL, LR = range(3)
     ll, lr, lc, laa = cols("lb", 0, 28), cols("lb", 32, 60), cols("lc", 0, 28), cols("lc", 32, 60)
     srow, urow, qrow, rrep = cols("srow", 0, 456), cols("urow", 0, 456), cols("qrow", 0, 464), cols("rrep", 0, 464)
@@ -360,10 +384,10 @@ def rank_program(g, core, T, topo):
         la, la2 = cols("la%d" % k, 0, 28), cols("la%d" % (k + 1), 0, 28)
         exchange(dst, "arq%d" % k, [(T[aq][:, 0:C].bitcast(dt.uint8), T[q][:, 0:C].bitcast(dt.uint8), cols(q), cols(aq)),
                                     (T[as_][:, 0:C], T[qs][:, 0:C], cols(qs), cols(as_))], LONG)
-        copy("s", slot(1, 2), lv, bias=col(9))
-        apart = tt(slot(0, 2), rv, lv, A.subtract)
-        tt(slot(0, 1), lv, rv, A.is_gt)
-        down = tt(("sc", 897, 952, 2), nv, pv, A.subtract)
+        copy("s", plane("wu", 9), lv, bias=col(9))
+        apart = tt(plane("wu", 8), rv, lv, A.subtract)
+        tt(plane("wu", 4), lv, rv, A.is_gt)
+        tt(("sc", 897, 952, 2), nv, pv, A.subtract)
         copy("s", plane("wt", LP), pv)
         copy("v", plane("wt", LL), lv)
         turn(cols("trow"), cols("wt"))
@@ -373,19 +397,19 @@ def rank_program(g, core, T, topo):
         copy("s", dense("dc", 1), ppv)
         side = tt(val("side"), plane("ppT", LL), nv, A.not_equal)
         inner = tt(plane("wq_", LC), rv, tt(val("d6"), side, apart, A.mult), A.subtract)
-        to_inner = tt(val("cn"), inner, nv, A.subtract)
+        tt(("sx", 1, 56, 2), inner, nv, A.subtract)
         from_inner = tt(val("pc"), pv, inner, A.subtract)
         up = tt(("sc", 953, 1008, 2), ppv, pv, A.subtract)
         ts(("sc", 952, 1008, 2), up, 0.0, A.is_equal)
         scan(("sc", 449, 560, 2), cols("sc", 896, 952), cols("sc", 952, 1008))
-        for h in range(2):
-            mm(7 * h, "uq", "us", 0, q, qs, CUT_X[h], CUT_X[h + 1])
-            copy("sv"[h], piece("srow", h, CUT_X), ps(7 * h, CUT_X[h + 1] - CUT_X[h]))
+        for h, bank in enumerate((0, 7, 5)):
+            mm(bank, "uq", "us", 0, q, qs, CUT[h], CUT[h + 1])
+            in_line("layer")
+            copy("ssv"[h], piece("srow", h), ps(bank, CUT[h + 1] - CUT[h]))
+            if h == 0:
+                in_line("claims")
         for b in range(4):
             mm(1 + b, "eq", "es", b, q, qs)
-        for b in range(2):
-            copy("s", cols("fo%d" % b), ps(1 + b))
-        copy("s", piece("fo2", 0, CUT_X), ps(3, CUT_X[1]))
         gather("s", cols("sl"), srow, ll)
         shared("sr", srow, lr, CUT_SR)
         gather("s", cols("sa"), srow, la)
@@ -395,11 +419,12 @@ def rank_program(g, core, T, topo):
         s0 = plane("sT", 0)
         vl = tt(val("vl"), s0, plane("slT", 0), A.subtract)
         vr = tt(val("vr"), s0, plane("srT", 0), A.subtract)
-        tt(slot(1, 0), vl, vr, A.is_equal)
-        tt(slot(1, 1), vl, vr, A.is_gt)
-        cv, cn = tt(plane("wu", 0), vl, vr, A.min), plane("wu", 9)
-        scan(("wu", 1, C, 4), four(0), four(1))
-        copy("s", dense("dc", 0), cn, bias=col(13))
+        tt(plane("wu", 1), vl, vr, A.is_equal)
+        tt(plane("wu", 5), vl, vr, A.is_gt)
+        cv = tt(plane("wu", 2), vl, vr, A.min)
+        cn = better_child("wu", 0)
+        child = dense("dc", 0)
+        copy("s", child, cn, bias=col(10))
         swapped("dc", 0, 64, 288)
         make_list(cols("lc", 0, 64), cols("dc", 0, 224), cols("offm", 0, 4))
         turn(cols("urow"), cols("wu"))
@@ -408,20 +433,20 @@ def rank_program(g, core, T, topo):
         in_line("turns")
         gather("s", cols("ul"), urow, ll)
         shared("ur", urow, lr, CUT_UR, "turns")
+        in_line("claims")
+        for b in range(3):
+            copy("s", cols("fo%d" % b), ps(1 + b))
+            in_line("claims")
         for n in ("ul", "ur"):
             turned(n)
         v0 = tt(val("v0"), plane("saT", 0), s0, A.subtract)
         m = tt(val("m1"), v0, ts(val("m0"), cv, -1.0e-30, A.min), A.min)
-        t0 = tt(val("t0"), tt(val("e0"), v0, m, A.is_equal), n2, A.mult)
-        tt(slot(3, 0), t0, tt(val("t1"), tt(val("e1"), cv, m, A.is_equal), cn, A.mult), A.min)
-        ul, ur = plane("ulT", 0), plane("urT", 0)
-        tt(slot(3, 1), tt(val("e2"), ur, tt(val("m2"), m, ul, A.min), A.is_le), plane("urT", 9), A.mult)
-        tt(slot(3, 2), tt(val("e3"), ul, tt(val("m3"), m, ur, A.min), A.is_le), plane("ulT", 9), A.mult)
-        tt(slot(2, 1), m, tt(val("m4"), ul, ur, A.min), A.is_le)
-        scan(four(0, "so"), four(2), four(3), A.min)
-        first = slot(0, 2, "so")
-        B = ts(plane("wq_", LB), first, 256.0, A.add)
-        X = tt(plane("wq_", LX), first, n2, A.is_equal)
+        ul, ur = plane("ulT", 2), plane("urT", 2)
+        m = tt(val("m3"), tt(val("m2"), m, ul, A.min), ur, A.min)
+        for i, (v, n) in enumerate(((v0, n2), (cv, cn), (ul, better_child("ulT", 3)), (ur, better_child("urT", 1)))):
+            tt(("sw", 224 + i, C, 8), tt(val("e%d" % i), v, m, A.is_equal), n, A.mult)
+        scan(("wq_", 0, C, 2), cols("sw", 0, 224), cols("sw", 224, C), A.add, A.min)
+        B = plane("wq_", LB)
         turn(cols("qrow"), cols("wq_"))
         gather("s", cols("qa"), cols("qrow"), la)
         in_line("claims")
@@ -437,20 +462,21 @@ def rank_program(g, core, T, topo):
         e01 = tt(slot(6, 1), B, plane("qaT", LB), A.is_equal)
         e12 = tt(slot(4, 2), plane("qaT", LB), plane("qaaT", LB), A.is_equal)
         tt(slot(4, 1), plane("qaaT", LB), plane("qaaaT", LB), A.is_equal)
-        tt(slot(7, 0), tt(val("gc"), first, cn, A.is_equal), plane("qcT", LX), A.mult)
-        tt(slot(6, 2), B, pv, A.subtract)
+        tt(slot(7, 0), B, child, A.is_equal)
+        tt(slot(6, 2), plane("qcT", LB), child, A.is_equal)
+        tt(slot(6, 3), B, pv, A.subtract)
         scan(four(2, "so"), four(6), four(7))
-        tt(slot(5, 3), slot(2, 2, "so"), down, A.subtract)
-        r1 = tt(slot(5, 1), X, e01, A.mult)
-        tt(slot(5, 0), tt(val("i1"), plane("qaT", LC), nv, A.is_equal), plane("qaT", LX), A.mult)
+        tt(slot(5, 3), slot(2, 3, "so"), pv, A.add)
+        r1 = tt(slot(5, 1), tt(val("x0"), B, nv, A.is_equal), e01, A.mult)
+        tt(slot(5, 0), tt(val("i1"), plane("qaT", LC), nv, A.is_equal), tt(val("x1"), plane("qaT", LB), pv, A.is_equal), A.mult)
         scan(cols("da", 0, 112), four(4), four(5))
         swapped("da", 0, 128, 0)
         make_list(cols(la2[0], 0, 32), cols("da", 0, 288), cols("offa", 0, 2))
         exchange(dst, "arl%d" % k, [(ap(al), ap(la2), la2, al)], SHORT)
-        rot = tt(val("rot"), r1, e12, A.mult)
-        tt(slot(6, 2), B, nv, A.subtract)
-        tt(slot(7, 3), rot, to_inner, A.mult)
-        scan(("wr", 0, C, 4), four(6), four(7))
+        rot = tt(("sx", 56, 112, 2), r1, e12, A.mult)
+        scan(("so", 225, 336, 2), cols("sx", 0, 56), cols("sx", 56, 112))
+        tt(("sx", 115, 224, 4), B, nv, A.subtract)
+        scan(("wr", 0, C, 4), cols("sx", 112, 224), four(2, "so"))
         turn(cols("rrep"), cols("wr"))
         gather("s", cols("repl"), rrep, ll)
         shared("repr_", rrep, lr, CUT_RR)
@@ -491,40 +517,34 @@ def rank_program(g, core, T, topo):
         for h in range(2):
             gather("vs"[h], piece("zt", h, CUT_Z, 2), kb[2], part(al, h, CUT_Z), 0.5)
         wbank = [1, 2, 7, 6]
-        for h in range(2):
+        for h, bank in enumerate((1, 5, 3)):
             quantize_piece("zq", "zs", "zt", h)
-            mm([1, 5][h], "wq", "wp", 0, "zq", "zs", CUT[h], CUT[h + 1])
+            mm(bank, "wq", "wp", 0, "zq", "zs", CUT[h], CUT[h + 1])
             in_line("layer")
-            copy("sv"[h], piece("rr0", h), ps([1, 5][h], CUT[h + 1] - CUT[h]), scale=0.03125)
-        for b in (1, 2, 3):
+            copy("ssv"[h], piece("rr0", h), ps(bank, CUT[h + 1] - CUT[h]), scale=0.03125)
+        for b in (1, 3, 2):
             mm(wbank[b], "wq", "wp", b, "zq", "zs")
             in_line("layer")
             copy("s", cols("rr%d" % b), ps(wbank[b]), scale=0.03125)
             in_line("claims")
-        gather("s", piece("xh", 1, CUT_X), cols("rr2"), part(la2, 1, CUT_X))
-        in_line("claims")
         gather("s", cols("xg"), cols("rr3"), la2)
         in_line("claims")
-        for b in range(2):
+        for b in range(3):
             gather_add(("xn", b, 4 * C, 4), cols("rr%d" % b), la2, cols("fo%d" % b))
             in_line("turns")
-        gather_add(piece("xn", 0, CUT_X, 2), cols("rr2"), part(la2, 0, CUT_X), piece("fo2", 0, CUT_X))
-        in_line("turns")
         for h in range(2):
             tt(piece("xn", h, CUT_X, 3), piece("xg", h, CUT_X), ps(4, CUT_X[h + 1] - CUT_X[h], CUT_X[h]), A.add)
             in_line("turns")
-            if h == 0:
-                tt(piece("xn", 1, CUT_X, 2), piece("xh", 1, CUT_X), ps(3, C - CUT_X[1], CUT_X[1]), A.add)
-                in_line("turns")
-            quantize_piece("q%d" % (k + 1), "qs%d" % (k + 1), "xn", h, CUT_X)
+        for h in range(3):
+            quantize_piece("q%d" % (k + 1), "qs%d" % (k + 1), "xn", h)
             in_line("turns")
 
     quantize("vq", "vs", 0, 128, cols("vt", 0, 512))
-    for h in range(2):
-        a, z = CUT_X[h], CUT_X[h + 1]
+    for h in range(3):
+        a, z = CUT[h], CUT[h + 1]
         mm(5 + h, "vq", "vs", 0, "q3", "qs3", a, z)
-        copy("sv"[h], cols("yt", a, z), ps(5 + h, z - a))
-        dmas("sy"[h], "st_y%d" % h, [(T.y[:, a:z], T.yt[:, a:z], [cols("yt", a, z)], [])], LOCAL + 0.5)
+        copy("svv"[h], cols("yt", a, z), ps(5 + h, z - a))
+        dmas("s", "st_y%d" % h, [(T.y[:, a:z], T.yt[:, a:z], [cols("yt", a, z)], [])], LOCAL + 0.5)
         dmas("y", "st_oc%d" % h, [(T.oc[:, 4 * a:4 * z], T.q3[:, a:z].bitcast(dt.uint8), [cols("q3", a, z)], [])], LOCAL + 0.5)
     dmas("y", "st_sc", [(T.osc[4 * i:4 * i + 4, :], T.qs3[32 * i:32 * i + 4, 0:C], [cols("qs3")], []) for i in range(4)])
     issue_all()

@@ -4,15 +4,37 @@ N = 4
 C = 448
 STEP = [1, 2, 3]
 BIGV = 3.0e29
+UNIT = 1.0 / 512
+NONE = 224 * UNIT
+WIDE = 976
 CUT = [0, 192, 320, C]
-CUT_SR = [0, 288, C]
-CUT_UR = [0, 160, C]
-CUT_AA = [0, 192, C]
-CUT_RR = [0, C, C]
-CUT_Z = [0, 320, C]
-CUT_X = [0, 192, C]
-CYCLE, SAME, CROSS, LOCAL, SHORT, LONG = 0.00087, 0.2, 0.2, 2.0, 1.6, 8.0
+SHARE = {"sl": [("s", 256), ("s", C)], "sr": [("v", 256), ("s", C)], "sa": [("s", C)],
+         "ul": [("s", 224), ("s", C)], "ur": [("v", 64), ("s", 256), ("s", C)],
+         "qw": [("s", C)], "qy": [("v", C)], "qc": [("s", C)], "g2": [("s", 320), ("s", C)], "pp": [("s", 224), ("s", C)],
+         "repl": [("s", 224), ("s", C)], "repr_": [("v", 320), ("s", C)]}
+CUT_X = [0, 192, 320, C]
+CYCLE, SAME, CROSS, LOCAL, SHORT, LONG = 0.001, 0.2, 0.22, 2.0, 1.6, 8.0
 PASSES = 3
+TRIES, REACH, HEAT, SWEEPS, SPAN, AHEAD, EAGER = 2200, 10, 0.005, 2, 120, 80, 0.3
+CLOCKS = [(0.226, 0.2, 1.0, 1.5, 0.83), (0.225, 0.21, 1.0, 1.08, 0.83), (0.235, 0.21, 1.4, 1.2, 0.83), (0.16, 0.24, 1.5, 1.95, 1.09)]
+SMIN = 185
+MARCH, EASE, SLACK = False, 0.0, 0.0
+PLAN = {}
+GATHER, GADD, PRODUCT = 1.8, 1.8, 0.5
+MERGE = True
+KV = [C, C, C, 0]
+ZSHARE = [[("s", C)], [("s", C)], [("v", 192), ("v", 320), ("s", C)], [("s", C)]]
+XV, RORDER = [C, C, C, 0], (1, 3, 2)
+RCUT, RQ2, STATE = [0, C], "svss", True
+HALF, TFIX, SFIX, SMALL = True, 0, 30, "ggg"
+EARLY, FBANK = 3, [5, 6, 7, 0]
+DELAY, TI, MSCAN, VCUT = 0, 0.1, False, 256
+SOON = True
+LAST = True
+RELAY = 0
+TWIN, FORDER, TPS = "yyyy", (0, 1, 2, 3), True
+SQ = "svs"
+RQ = "svv"
 
 F32, BF, U16, I32, CODE, PLANE = "float32", "bfloat16", "uint16", "int32", "float8_e4m3fn_x4", "uint8"
 SCRATCH = {"ps": ("psum", [128, 4096], F32)}
@@ -24,8 +46,10 @@ def _sbuf(names, n, dtype):
 
 
 _sbuf("xt xn zt fq kb", 4 * C, BF)
-_sbuf("ut vt ones et0 et1 et2 et3", 512, BF)
+_sbuf("ut vt ones", 512, BF)
+_sbuf("et", 516, BF)
 _sbuf("uq vq", 128, CODE)
+_sbuf("hq0 hq1 hq2", 256, CODE)
 _sbuf("us vs", 128, PLANE)
 _sbuf("wq eq", 512, CODE)
 _sbuf("wp es", 512, PLANE)
@@ -41,28 +65,52 @@ _sbuf("al0 al1 al2", 28, U16)
 _sbuf("la0 la1 la2 la3", 32, U16)
 _sbuf("lb lc", 64, U16)
 _sbuf("di dt dc", 256, BF)
-_sbuf("da", 288, BF)
+_sbuf("da0 da1", 288, BF)
 _sbuf("eb", 448, BF)
 _sbuf("dd", 64, F32)
-_sbuf("qrow rrep", 464, BF)
-_sbuf("srow urow", 456, F32)
-_sbuf("wq_ wr wt trow pp ppT qa qaa qaaa qc qaT qaaT qaaaT qcT repl repr_ kg", C, BF)
+_sbuf("qx", WIDE, BF)
+_sbuf("wq_ rrep", 464, BF)
+_sbuf("srow", 456, F32)
+_sbuf("wu urow", 480, F32)
+_sbuf("wr wt trow pp ppT qy qw qc g2 qwT qyT qcT g2T repl repr_ kg0 kg1 kg2 kg3", C, BF)
 _sbuf("repT", 512 + C, BF)
-_sbuf("sa sl sr ul ur xg xh sT saT slT srT ulT urT trf yt rr0 rr1 rr2 rr3 wu sw zf", C, F32)
+_sbuf("sa sl sr ul ur xg2 xg3 sT saT slT srT ulT urT trf yt rr0 rr1 rr2 rr3", C, F32)
 _sbuf("sc", 1024, F32)
-_sbuf("so", 4 * 112, F32)
+_sbuf("mc mo ne so", 3 * 112, F32)
 _sbuf("sx", 224, F32)
-_sbuf("cb", 28 * 40, F32)
-_sbuf("fo0 fo1 fo2 fp0 fp1 fp2 fp3", C, BF)
+_sbuf("cb", 28 * 16, F32)
+_sbuf("fo0 fo1 fo2 fo3 fp0 fp1 fp2 fp3", C, BF)
 
-SEMAPHORES = (["cv", "cs", "ct", "cg", "sent"] + ["ld_" + k for k in "x0 x1 x2 u v t w z0 z1 z2".split()]
-              + ["st_" + k for k in "y0 y1 y2 oc0 oc1 oc2 sc tr".split()] + ["cf%d" % k for k in range(3)]
-              + ["arq%d" % k for k in range(3)] + ["arl%d" % k for k in range(3)])
+SEMAPHORES = (["cv", "cs", "ct", "cg", "sent"] + ["ld_" + k for k in "x0 x1 x2 u v t w".split()]
+              + ["st_" + k for k in "y0 y1 y2 oc0 oc1 oc2 sc tr".split()] + ["cf%d" % k for k in range(4)]
+              + ["hop%d" % k for k in range(3)] + ["arq%d" % k for k in range(3)] + ["arl%d" % k for k in range(3)])
 
 
 def rank_program(g, core, T, topo):
+    def helper(c):
+        return [h for h in topo.cores_of(c) if topo.die(h) != topo.die(c) and h not in T.cores and all(topo.may_write(h, d) for d in T.cores)][0]
+
+    def write(out, in_, dst, sem, mask):
+        rid, pid, se = topo.addr(dst)
+        g.remote_dma(out, in_, T.sem[sem], T.sem["sent"], pid, rid, mask)
+
+    def engines(mask):
+        return bin(mask).count("1")
+
+    def inward(c):
+        return topo.mask(c, helper(c)) & ~topo.mask(c, T.cores[(T.rank_of(c) + 1) % N])
+
     rank = T.rank_of(core)
     if rank is None:
+        for r, c in enumerate(T.cores):
+            if RELAY and helper(c) == core:
+                sent = 0
+                for k in range(3):
+                    dst = T.cores[(r + STEP[k]) % N]
+                    g.wait_ge(T.sem["hop%d" % k], engines(inward(c)))
+                    write(T["aq%d" % k][:, 0:RELAY].bitcast(dt.uint8), T["hq%d" % k][:, 0:RELAY].bitcast(dt.uint8), dst, "arq%d" % k, topo.mask(core, dst))
+                    sent += engines(topo.mask(core, dst))
+                g.wait_ge(T.sem["sent"], sent)
         return
     A = AluOpType
     ACT = ActivationFunctionType
@@ -107,6 +155,8 @@ def rank_program(g, core, T, topo):
     def op(q, fn, reads, writes, cycles):
         t = max(64, cycles) * CYCLE
         record(q, lambda: fn().then_inc(T.sem["c" + q], 1), "c" + q, 1, t, t, reads, writes)
+        if any(SCRATCH[v[0]][2] == U16 for v in reads):
+            calls[-1]["per"] = size(writes[0])
 
     def dmas(q, sem, moves, takes=LOCAL):
         def issue():
@@ -114,16 +164,16 @@ def rank_program(g, core, T, topo):
                 queue[q].dma_start(m[0], m[1]).then_inc(T.sem[sem], 16)
         record(q, issue, sem, 16 * len(moves), 0.05 * len(moves), takes, sum([m[2] for m in moves], []), sum([m[3] for m in moves], []))
 
-    def exchange(dst, sem, moves, takes):
-        rid, pid, se = topo.addr(dst)
-        n = len(moves) * len(topo.engines(core, dst))
+    def exchange(dst, sem, moves, lands, takes, more=0):
+        n = len(moves) * engines(topo.mask(core, dst))
 
         def issue():
             for m in moves:
-                g.remote_dma(m[0], m[1], T.sem[sem], T.sem["sent"], pid, rid, topo.mask(core, dst))
+                write(m[0], m[1], dst, sem, topo.mask(core, dst))
         mark = (sem, 0, 1, 1)
         record("g", issue, "sent", n, 0.1, 0.1, [m[2] for m in moves], [mark])
-        record(None, None, sem, n, 0.0, takes, [mark], [m[3] for m in moves])
+        in_line("twins")
+        record(None, None, sem, n + more, 0.0, takes, [mark], lands)
 
     def issue_all():
         def span(i, j):
@@ -158,10 +208,131 @@ def rank_program(g, core, T, topo):
                 at[j] = t
             return at
         every = range(len(calls))
-        start = place(sorted(every, key=lambda j: (-way[j], j)), False)
-        for _ in range(PASSES):
-            late = place(sorted(every, key=lambda j: (-start[j] - calls[j]["holds"], -j)), True)
-            start = place(sorted(every, key=lambda j: (-late[j] - calls[j]["holds"], j)), False)
+
+        def length(at):
+            return max(at[j] + calls[j]["takes"] for j in every)
+
+        def march(due):
+            at, free = {}, {q: 0.0 for q in queue}
+            left = [len(c["after"]) for c in calls]
+            ready = {j: 0.0 for j in every if not left[j]}
+            while ready:
+                t, q = min((max(r, free.get(calls[j]["q"], 0.0)), calls[j]["q"] or "") for j, r in ready.items())
+                mine = sorted((due[j], j) for j in ready if (calls[j]["q"] or "") == q)
+                soon = t + 1e9
+                for d, j in mine:
+                    if ready[j] > t + 1e-9:
+                        soon = min(soon, max(ready[j], d - due0[0]) + EASE)
+                    elif t + calls[j]["holds"] <= soon:
+                        break
+                else:
+                    free[q] = min(ready[j] for d, j in mine if ready[j] > t + 1e-9)
+                    continue
+                at[j] = t
+                if q:
+                    free[q] = t + calls[j]["holds"]
+                del ready[j]
+                for i in before[j]:
+                    left[i] -= 1
+                    if not left[i]:
+                        ready[i] = max(at[h] + span(h, i) for h in calls[i]["after"])
+            return at
+        qs = [c["q"] for c in calls]
+        paces = []
+        for same, cross, product, rate, pace in CLOCKS:
+            holds, takes = [[(c[x] + c.get("per", 0) * (rate - GATHER) * CYCLE) * (product if c["q"] == "t" else pace if c["sem"][0] == "c" and len(c["sem"]) == 2 else 1.0)
+                             for c in calls] for x in ("holds", "takes")]
+            links = [[(i, takes[i] if qs[j] is None else takes[i] + (same if qs[i] == qs[j] else cross) if w else holds[i])
+                      for i, w in c["after"].items()] for j, c in enumerate(calls)]
+            paces.append((links, holds, takes))
+
+        def clock(order, links, holds, takes):
+            at, why, free, last, end, tail = [0.0] * len(calls), [-1] * len(calls), {}, {}, 0.0, -1
+            for j in order:
+                t, w = 0.0, -1
+                for i, d in links[j]:
+                    if at[i] + d > t:
+                        t, w = at[i] + d, i
+                q = qs[j]
+                if q:
+                    if free.get(q, 0.0) > t + 1e-9:
+                        t, w = free[q], last[q]
+                    free[q], last[q] = t + holds[j], j
+                at[j], why[j] = t, w
+                if t + takes[j] > end:
+                    end, tail = t + takes[j], j
+            return end, at, why, tail
+
+        def moved(order, a, b, ahead):
+            mid = order[a:b + 1]
+            group = {mid[-1] if ahead else mid[0]}
+            for j in (reversed(mid[:-1]) if ahead else mid[1:]):
+                if any(i in group for i in (before[j] if ahead else calls[j]["after"])):
+                    group.add(j)
+            if mid[0] in group and mid[-1] in group:
+                return None
+            x, y = [j for j in mid if j in group], [j for j in mid if j not in group]
+            return order[:a] + (x + y if ahead else y + x) + order[b + 1:]
+
+        def stretch(part_, ats, frees):
+            total = 0.0
+            for (links, holds, takes), at, free in zip(paces, ats, frees):
+                free, early = dict(free), 0.0
+                for j in part_:
+                    t = free.get(qs[j], 0.0)
+                    for i, d in links[j]:
+                        if at[i] + d > t:
+                            t = at[i] + d
+                    at[j] = t
+                    early += t
+                    if qs[j]:
+                        free[qs[j]] = t + holds[j]
+                total += max(at[j] + takes[j] for j in part_[-12:]) + EAGER * early / len(part_)
+            return total / len(paces)
+
+        def polish(order):
+            seed = 1
+            for sweep in range(SWEEPS):
+                for lo in range(0, len(order) - 20, SPAN // 2):
+                    ats = [clock(order, *p)[1] for p in paces]
+                    order = sorted(order, key=lambda j: sum(at[j] for at in ats))
+                    frees = []
+                    for (links, holds, takes), at in zip(paces, ats):
+                        frees.append({qs[j]: at[j] + holds[j] for j in order[:lo] if qs[j]})
+                    mid = order[lo:lo + SPAN + AHEAD]
+                    now = best = stretch(mid, ats, frees)
+                    keep = mid
+                    for n in range(TRIES):
+                        seed = (seed * 1103515245 + 12345) % 2147483648
+                        a = (seed >> 8) % min(SPAN, len(mid))
+                        mine = [i for i in range(a + 1, min(len(mid), a + 60)) if qs[mid[i]] == qs[mid[a]]]
+                        if not qs[mid[a]] or not mine:
+                            continue
+                        new = moved(mid, a, mine[(seed >> 18) % min(REACH, len(mine))], seed >> 28 & 1)
+                        if new:
+                            got = stretch(new, ats, frees)
+                            if got <= now + HEAT * (1.0 - n / TRIES) * ((seed >> 4) % 16) / 16.0:
+                                mid, now = new, got
+                                if got < best:
+                                    best, keep = got, new
+                    order = order[:lo] + keep + order[lo + SPAN + AHEAD:]
+            return clock(order, *paces[0])[1]
+        due0 = [0.0]
+        if "start" not in PLAN:
+            best = place(sorted(every, key=lambda j: (-way[j], j)), False)
+            start = best
+            for _ in range(PASSES):
+                late = place(sorted(every, key=lambda j: (-start[j] - calls[j]["holds"], -j)), True)
+                if MARCH:
+                    end = max(late[j] + calls[j]["holds"] for j in every)
+                    due0[0] = SLACK
+                    start = march([end - late[j] - calls[j]["holds"] for j in every])
+                else:
+                    start = place(sorted(every, key=lambda j: (-late[j] - calls[j]["holds"], j)), False)
+                if length(start) <= length(best) or (MARCH and _ == 0):
+                    best = start
+            PLAN["start"] = polish(sorted(every, key=lambda j: (best[j], j))) if TRIES else best
+        start = PLAN["start"]
         count, seen, facts, mark = {}, {q: {} for q in queue}, {}, {}
 
         def wait(q, sem, n):
@@ -197,14 +368,17 @@ def rank_program(g, core, T, topo):
         a, z = cut[h], cut[h + 1]
         return (buf, a, z, 1) if b is None else (buf, 4 * a + b, 4 * z, 4)
 
-    def part(off, h, cut=CUT):
-        return off[0], off[1] + cut[h] // 16, off[1] + cut[h + 1] // 16, 1
+    def part(off, a, z):
+        return off[0], off[1] + a // 16, off[1] + z // 16, 1
 
     def ps(b, n=C, a=0):
         return "ps", 512 * b + a, 512 * b + a + n, 1
 
-    def plane(buf, lane, at=0):
-        return buf, at + lane, at + C, 16
+    def plane(buf, lane, end=C):
+        return buf, lane, end, 16
+
+    def lanes(buf, first):
+        return buf, first, C, 4
 
     def dense(buf, w):
         return buf, 32 * w, 32 * w + 28, 1
@@ -239,23 +413,31 @@ def rank_program(g, core, T, topo):
         op("v", lambda: V.tensor_tensor_scan(ap(out), ap(d0), ap(d1), 0.0, o0, o1), [d0, d1], [out], size(out))
 
     def turn(out, in_):
-        op("v", lambda: V.transpose(ap(out), ap(in_)), [in_], [out], size(out) * narrow(out))
+        op("v", lambda: V.transpose(ap(out), ap(in_)), [in_], [out], max(64, size(out) * narrow(out)) + TFIX)
 
-    def turned(name):
-        turn(cols(name + "T"), cols(name))
+    def halves(out, in_):
+        if not HALF:
+            return turn(cols(out), cols(in_))
+        for a in (0, C // 2):
+            turn(cols(out, a, a + C // 2), cols(in_, a, a + C // 2))
 
     def copy(q, out, in_, scale=1.0, bias=None):
         if q == "v" and scale == 1.0:
             op("v", lambda: V.tensor_copy(ap(out), ap(in_)), [in_], [out], size(out) * narrow(out, in_))
         elif q == "v":
             ts(out, in_, scale, A.mult)
+        elif q == "g":
+            op("g", lambda: g.affine_select(ap(out), ap(in_), [[0, size(out)]], A.is_equal, 0.0, 0, 0), [in_], [out], 200 + 2 * size(out))
         elif bias is None:
-            op("s", lambda: S.activation(ap(out), ap(in_), ACT.Copy, scale=scale), [in_], [out], size(out))
+            op("s", lambda: S.activation(ap(out), ap(in_), ACT.Copy, scale=scale), [in_], [out], max(SMIN, size(out)))
         else:
-            op("s", lambda: S.activation(ap(out), ap(in_), ACT.Identity, bias=ap(bias)), [in_, bias], [out], size(out))
+            op("s", lambda: S.activation(ap(out), ap(in_), ACT.Identity, bias=ap(bias), scale=scale), [in_, bias], [out], max(SMIN, size(out)))
+
+    def fill(v, x):
+        copy("s", v, cols("ones", 0, size(v)), scale=x)
 
     def gather(q, out, win, off, scale=1.0):
-        cycles = 70 + 1.56 * size(out)
+        cycles = 70 + GATHER * size(out)
         if q == "s":
             op("s", lambda: S.activation(ap(out), ap(win).indirect(ap(off)), ACT.Copy, scale=scale), [win, off], [out], cycles)
         elif scale == 1.0:
@@ -263,16 +445,17 @@ def rank_program(g, core, T, topo):
         else:
             op("v", lambda: V.tensor_scalar(ap(out), ap(win).indirect(ap(off)), scale, None, A.mult), [win, off], [out], cycles)
 
-    def shared(name, win, off, cut, line=None):
-        if cut[1]:
-            gather("v", piece(name, 0, cut), win, part(off, 0, cut))
-            if line:
+    def brought(name, win, off, out=None, at=0, line=None):
+        a = 0
+        for q, z in SHARE[name]:
+            gather(q, cols(name, a, z), win, part(off, a, z))
+            if line and q == "s":
                 in_line(line)
-        if cut[1] < C:
-            gather("s", piece(name, 1, cut), win, part(off, 1, cut))
+            turn(cols(out or name + "T", at + a, at + z), cols(name, a, z))
+            a = z
 
     def gather_add(out, win, off, other):
-        op("v", lambda: V.tensor_tensor(ap(out), ap(win).indirect(ap(off)), ap(other), A.add), [win, off, other], [out], 60 + 1.6 * size(out))
+        op("v", lambda: V.tensor_tensor(ap(out), ap(win).indirect(ap(off)), ap(other), A.add), [win, off, other], [out], 60 + GADD * size(out))
 
     def memset(v, x):
         op("v", lambda: V.memset(ap(v), x), [], [v], size(v) * narrow(v))
@@ -282,7 +465,7 @@ def rank_program(g, core, T, topo):
 
     def mm(bank, l, ls, b, r, rs, a=0, z=C):
         l, ls, r, rs = cols(l, 128 * b, 128 * b + 128), cols(ls, 128 * b, 128 * b + 128), cols(r, a, z), cols(rs, a, z)
-        op("t", lambda: g.tensor.matmul_mx(ap(ps(bank, z - a)), ap(l), ap(ls), ap(r), ap(rs), True, True), [l, ls, r, rs], [ps(bank)], 0.7 * (z - a + 16))
+        op("t", lambda: g.tensor.matmul_mx(ap(ps(bank, z - a)), ap(l), ap(ls), ap(r), ap(rs), True, True), [l, ls, r, rs], [ps(bank)], PRODUCT * (z - a + 16))
 
     def quantize(out, scales, a, z, in_):
         o, s = cols(out, a, z), cols(scales, a, z)
@@ -296,50 +479,55 @@ def rank_program(g, core, T, topo):
         turn(cols(buf, 128 + a, 160 + z), cols("eb", at, at + 32 + z - a))
 
     def make_list(out, win, off):
-        op("v", lambda: V.tensor_scalar(ap(out), ap(win).indirect(ap(off)), 224.0, None, A.add), [win, off], [out], 60 + 1.56 * size(out))
+        op("v", lambda: V.tensor_scalar(ap(out), ap(win).indirect(ap(off)), 512.0, 224.0, A.mult, A.add), [win, off], [out], 60 + GATHER * size(out))
 
-    memset(cols("ti", 0, 96), 0)
-    dmas("s", "ld_t", [(T.ti[:, 32 * i:32 * i + 28], T[k][:], [], [dense("ti", i)]) for i, k in enumerate(("up", "lf", "rt"))])
+    for i in range(3):
+        memset(cols("ti", 32 * i + 28, 32 * i + 32), 0)
+    dmas("s", "ld_t", [(T.ti[:, 32 * i:32 * i + 28], T[k][:], [], [dense("ti", i)]) for i, k in enumerate(("up", "lf", "rt"))], LOCAL + TI)
     dmas("y", "ld_u", [(T.ut[:], T.u[:], [], [cols("ut", 0, 512)])], LOCAL + 0.4)
     in_line("loads")
     for h in range(3):
         v = cols("xt", 4 * CUT[h], 4 * CUT[h + 1])
         dmas("y", "ld_x%d" % h, [(ap(v), T.x[:, v[1]:v[2]], [], [v])], LOCAL + 0.8 + 0.35 * h)
         in_line("loads")
-    last_x = v
+    dmas("y", "ld_w", [(T.wq[:, 0:512].bitcast(dt.uint8), T.wc[:], [v], [cols("wq", 0, 512)]),
+                       (T.wp[:, 0:512], T.ws[:], [], [cols("wp", 0, 512)])], LOCAL + 1.5)
 
     ones = cols("ones", 0, 512)
     memset(ones, 1.0)
+    in_line("start")
     op("g", lambda: g.iota(T.pidx[:, 0:2], [[0, 2]], 0, 1), [], [cols("pidx", 0, 2)], 160)
     iota(cols("i16", 0, 28), [[16, 28]], 0)
     iota(cols("i32", 0, 28), [[32, 14], [0, 2]], -224)
     in_line("first")
-    op("g", lambda: g.affine_select(T.et0[:], T.ones[:], [[-1, 512]], A.is_equal, 0.0, 0, 4), [ones], [cols("et0", 0, 512)], 1230)
+    memset(cols("et", 0, 516), 0.0)
+    in_line("start")
+    op("g", lambda: g.affine_select(T.et[:, 3:515:4], T.ones[:, 0:128], [[-1, 128]], A.is_equal, 0.0, 0, 1),
+       [cols("ones", 0, 128)], [("et", 3, 515, 4)], 460)
     in_line("first")
-    for k in ("eb", "zf", "wr"):
-        copy("s", cols(k), cols("ones"), scale=0.0)
-        in_line("claims")
-    for b in range(1, 4):
-        memset(cols("et%d" % b, 0, b), 0.0)
-        copy("s", cols("et%d" % b, b, 512), cols("et0", 0, 512 - b))
-        in_line("claims")
-    for sem, zero, views in (("ld_z0", "zf", [cols("wu")]), ("ld_z1", "wr", [cols("wt"), cols("wq_"), cols("dc", 0, 128), cols("repT", C, 512)]),
-                             ("ld_z2", "zf", [cols("sc", C, 2 * C), cols("sc", 2 * C, 1024), cols("sw"), cols("sx", 0, 224), cols("dd", 28, 32)])):
-        dmas("y", sem, [(ap(v), T[zero][:, 0:size(v)], [cols(zero, 0, size(v)), last_x], [v]) for v in views], LOCAL + 1.5)
-    for v in (cols("di", 96, 128), cols("dt", 0, 256), cols("da", 112, 128)):
+    memset(cols("eb"), 0.0)
+    for v in (cols("wu", 0, 480), cols("wr"), cols("wt"), cols("wq_", 0, 464), cols("dc", 0, 128), cols("repT", C, 512),
+              cols("sc", C, 952), cols("sx", 0, 224), cols("dd", 28, 32)):
+        fill(v, 0.0)
+    for v in (cols("di", 96, 128), cols("dt", 0, 256), cols("da1", 112, 128)):
         memset(v, 0.0)
     memset(cols("srow", C, 456), -BIGV)
-    dmas("y", "ld_w", [(T.wq[:, 0:512].bitcast(dt.uint8), T.wc[:], [cols("wq_")], [cols("wq", 0, 512)]), (T.wp[:, 0:512], T.ws[:], [], [cols("wp", 0, 512)])])
-    dmas("y", "ld_v", [(T.vt[:], T.v[:], [cols("wq_")], [cols("vt", 0, 512)])])
-    for v, x, step in ((cols("qrow", C, 464), 600, 0), (cols("rrep", C, 464), 224, 0), (col(8), 224, 0), (cols("col", 9, 11), -256, 512),
-                       (("sw", 0, 224, 8), 4096, 0), (("sw", 4, 224, 8), 256, 0), (("sw", 228, C, 8), 4096, 0)):
-        iota(v, [[step, size(v)]], x)
+    for v, x in ((cols("qx", C, WIDE), -3), (col(8), 224), (("ne", 3, 336, 4), 8)):
+        iota(v, [[0, size(v)]], x)
+        in_line("first")
+    iota(cols("sc", 0, 56), [[0, 28], [3, 2]], 0)
+    in_line("first")
+    fill(cols("rrep", C, 464), NONE)
+    fill(cols("mc", 0, 336), -BIGV)
+    fill(("wu", C + 4, 480, 4), BIGV)
+    for lane, x in ((0, -BIGV), (1, 8.0), (2, 8.0), (12, -1.0e-30)):
+        fill(plane("wu", lane, 480), x)
+    turn(cols("urow", C, 480), cols("wu", C, 480))
     for i, (sh, m) in enumerate(((0, 1), (4, 1), (0, 15), (0, 31))):
         ts(cols("pidx", 2 + i, 3 + i), cols("pidx", 0, 1), sh, A.logical_shift_right, m, A.bitwise_and)
     copy("v", cols("col", 0, 4), cols("pidx", 2, 6))
-    ts(cols("urow", C, 456), cols("ones", 0, 8), ts(col(14), col(2), 2.0, A.is_equal, BIGV, A.mult), A.mult)
-    jt = ts(cols("jt", 0, 28), cols("i16", 0, 28), col(2), A.add, -448.0, A.add)
-    nv = ts(cols("nn", 0, 28), cols("i32", 0, 28), col(3), A.add)
+    jt = ts(cols("jt", 0, 28), ts(val("i1"), cols("i16", 0, 28), col(2), A.add, -448.0, A.add), UNIT, A.mult)
+    nv = ts(cols("nn", 0, 28), cols("i32", 0, 28), col(3), A.add, UNIT, A.mult)
     tt(col(4), col(0), col(1), A.not_equal)
     ts(col(5), col(1), -30.0, A.mult, 159.0, A.add)
     ts(col(7), col(4), col(5), A.mult, col(2), A.add)
@@ -348,195 +536,263 @@ def rank_program(g, core, T, topo):
     ts(col(11), col(2), 4.0, A.mult, 3.0, A.add)
     ts(col(12), col(4), col(13), A.mult, col(11), A.add)
     ts(cols("offa", 0, 2), cols("i16", 0, 2), 4.0, A.mult, col(12), A.add)
-    n2 = ts(val("n2"), nv, -256.0, A.add)
     copy("s", ("sx", 57, 112, 2), nv)
+    copy("s", plane("wu", 14), nv)
 
+    for b in range(4):
+        quantize("eq", "es", 128 * b, 128 * b + 128, cols("et", 3 - b, 515 - b))
+        in_line("start")
     quantize("uq", "us", 0, 128, cols("ut", 0, 512))
+    in_line("start")
     for h in range(3):
         quantize_piece("q0", "qs0", "xt", h)
-        in_line("start")
-    for b in range(4):
-        quantize("eq", "es", 128 * b, 128 * b + 128, cols("et%d" % b, 0, 512))
-        in_line("start")
-    ts(cols("di", 0, 96), cols("ti", 0, 96), -224.0, A.add)
+    ts(cols("di", 0, 96), cols("ti", 0, 96), -224.0, A.add, UNIT, A.mult)
     copy("v", cols("lb", 0, 64), cols("ti", 32, 96))
-    e = ts(val("i0"), dense("di", 0), 224.0, A.is_equal)
-    e = tt(val("i1"), e, jt, A.mult)
+    e = ts(val("i0"), dense("ti", 0), 448.0, A.is_equal)
+    e = tt(val("i2"), e, jt, A.mult)
     tt(dense("di", 0), dense("di", 0), e, A.add)
-    ts(cols("la0", 0, 32), cols("di", 0, 32), 224.0, A.add)
+    ts(cols("la0", 0, 32), cols("di", 0, 32), 512.0, A.mult, 224.0, A.add)
     swapped("di", 0, 96, 0)
-    pv, lv, rv = ("da", 3, 112, 4), dense("dt", 1), dense("dt", 2)
+    lv, rv = dense("dt", 1), dense("dt", 2)
     gather("v", cols("dt", 32, 96), cols("di", 0, 256), cols("offm", 2, 6))
-    gather("v", ("da", 3, 128, 4), cols("di", 0, 256), cols("offm", 0, 2))
+    memset(cols("da0", 112, 128), 0.0)
+    gather("s", ("da0", 3, 128, 4), cols("di", 0, 256), cols("offm", 0, 2))
 
-    def better_child(buf, i):
-        scan(four(i, "so"), (buf, 0, C, 4), (buf, 1, C, 4))
-        return slot(i, 2, "so")
+    def first_of(i, buf, own, order, first, out):
+        if MSCAN:
+            scan(four(i, "mo"), lanes(buf, 0), four(i, "mc"), A.min, A.max)
+            least = slot(i, 3, "mo")
+            if i < 2:
+                copy("v", slot(i + 1, 0, "mc"), least)
+        elif i == 1:
+            least = tt(slot(1, 0, "mc"), tt(val("m1"), own, plane(buf, 4), A.min), plane(buf, 8), A.min)
+        else:
+            scan(four(i // 2, "mo"), lanes(buf, 0), four(i // 2, "mc"), A.min, A.max)
+            least = slot(i // 2, 3, "mo")
+        for j, v in zip(order, (own, plane(buf, 4), plane(buf, 8))):
+            tt(slot(i, j, "ne"), v, least, A.not_equal)
+        scan(out, lanes(buf, first), four(i, "ne"), A.add, A.min)
 
-    LB, LC = 8, 1
+    LB, LO, LC, LW = 12, 10, 1, 5
     LP, LL, LR = range(3)
     ll, lr, lc, laa = cols("lb", 0, 28), cols("lb", 32, 60), cols("lc", 0, 28), cols("lc", 32, 60)
-    srow, urow, qrow, rrep = cols("srow", 0, 456), cols("urow", 0, 456), cols("qrow", 0, 464), cols("rrep", 0, 464)
+    srow, urow, rrep = cols("srow", 0, 456), cols("urow", 0, 456), cols("rrep", 0, 464)
+
+    def grandparents(pv, la, line=None):
+        tt(("sc", 897, 952, 2), nv, pv, A.subtract)
+        copy(SMALL[-1], plane("wt", LP), pv)
+        halves("trow", "wt")
+        brought("pp", cols("trow"), la, line=line)
+        ppv = plane("ppT", LP)
+        copy(SMALL[1], dense("dc", 1), ppv)
+        up = tt(("sc", 953, 1008, 2), ppv, pv, A.subtract)
+        ts(("sc", 952, 1008, 2), up, 0.0, A.is_equal)
+        scan(("sc", 449, 560, 2), cols("sc", 896, 952), cols("sc", 952, 1008))
+
+    def unpack(aq, as_):
+        for b in FORDER:
+            mm(FBANK[b], "eq", "es", b, aq, as_)
+            copy("s", cols("fp%d" % b), ps(FBANK[b]))
+            if EARLY:
+                in_line("gap")
+            if KV[b]:
+                fp, fq = cols("fp%d" % b, 0, KV[b]), cols("fq", C * b, C * b + KV[b])
+                if TWIN[b] == "s":
+                    copy("s", fq, ps(FBANK[b], KV[b]))
+                else:
+                    dmas("y", "cf%d" % b, [(ap(fq), ap(fp), [fp], [fq])], LOCAL + 0.6)
+
     for k in range(3):
         last = k == 2
         q, qs, aq, as_, al = "q%d" % k, "qs%d" % k, "aq%d" % k, "as%d" % k, cols("al%d" % k, 0, 28)
         dst = T.cores[(rank + STEP[k]) % N]
         la, la2 = cols("la%d" % k, 0, 28), cols("la%d" % (k + 1), 0, 28)
-        exchange(dst, "arq%d" % k, [(T[aq][:, 0:C].bitcast(dt.uint8), T[q][:, 0:C].bitcast(dt.uint8), cols(q), cols(aq)),
-                                    (T[as_][:, 0:C], T[qs][:, 0:C], cols(qs), cols(as_))], LONG)
-        copy("s", plane("wu", 9), lv, bias=col(9))
-        apart = tt(plane("wu", 8), rv, lv, A.subtract)
-        tt(plane("wu", 4), lv, rv, A.is_gt)
-        tt(("sc", 897, 952, 2), nv, pv, A.subtract)
-        copy("s", plane("wt", LP), pv)
-        copy("v", plane("wt", LL), lv)
-        turn(cols("trow"), cols("wt"))
-        gather("s", cols("pp"), cols("trow"), la)
-        turned("pp")
-        ppv = plane("ppT", LP)
-        copy("s", dense("dc", 1), ppv)
-        side = tt(val("side"), plane("ppT", LL), nv, A.not_equal)
-        inner = tt(plane("wq_", LC), rv, tt(val("d6"), side, apart, A.mult), A.subtract)
-        tt(("sx", 1, 56, 2), inner, nv, A.subtract)
-        from_inner = tt(val("pc"), pv, inner, A.subtract)
-        up = tt(("sc", 953, 1008, 2), ppv, pv, A.subtract)
-        ts(("sc", 952, 1008, 2), up, 0.0, A.is_equal)
-        scan(("sc", 449, 560, 2), cols("sc", 896, 952), cols("sc", 952, 1008))
+        pv, da = ("da%d" % (k % 2), 3, 112, 4), "da%d" % (1 - k % 2)
+        def leave(more):
+            if RELAY:
+                record("g", lambda k=k, q=q: write(T["hq%d" % k][:, 0:RELAY].bitcast(dt.uint8), T[q][:, 0:RELAY].bitcast(dt.uint8), helper(core), "hop%d" % k, inward(core)),
+                       "sent", engines(inward(core)), 0.1, 0.1, [cols(q, 0, RELAY)], [])
+                for v in more:
+                    calls[-1]["after"][uses[v[0]][0][1]] = True
+                in_line("twins")
+            exchange(dst, "arq%d" % k, [(T[aq][:, RELAY:C].bitcast(dt.uint8), T[q][:, RELAY:C].bitcast(dt.uint8), cols(q, RELAY, C)),
+                                        (T[as_][:, 0:C], T[qs][:, 0:C], cols(qs))], [cols(aq), cols(as_)], LONG - (DELAY if more else 0),
+                     engines(topo.mask(helper(core), dst)) if RELAY else 0)
+        if k == 0:
+            leave([])
+        apart = tt(plane("wu", 9), lv, rv, A.subtract)
+        tt(plane("wu", 10), rv, nv, A.subtract)
+        for out, in_ in ((plane("wu", 3), lv), (plane("wu", 13), rv), (plane("wu", 6), apart), (plane("wq_", LC), lv)):
+            copy(SMALL[0] if k else "v", out, in_)
+            if SMALL[0] == "g" and k:
+                in_line("twins")
+        if k == 0 or not EARLY:
+            grandparents(pv, la)
+        if k:
+            leave([])
         for h, bank in enumerate((0, 7, 5)):
             mm(bank, "uq", "us", 0, q, qs, CUT[h], CUT[h + 1])
             in_line("layer")
-            copy("ssv"[h], piece("srow", h), ps(bank, CUT[h + 1] - CUT[h]))
-            if h == 0:
-                in_line("claims")
+            copy(SQ[h], piece("srow", h), ps(bank, CUT[h + 1] - CUT[h]))
+            turn(piece("sT", h), ps(bank, CUT[h + 1] - CUT[h]) if TPS else piece("srow", h))
         for b in range(4):
             mm(1 + b, "eq", "es", b, q, qs)
-        gather("s", cols("sl"), srow, ll)
-        shared("sr", srow, lr, CUT_SR)
-        gather("s", cols("sa"), srow, la)
-        turn(cols("sT"), cols("srow"))
-        for n in ("sl", "sr"):
-            turned(n)
+        brought("sl", srow, ll)
+        brought("sr", srow, lr)
+        brought("sa", srow, la)
+        if DELAY:
+            leave([cols("slT", 0, 224)])
         s0 = plane("sT", 0)
-        vl = tt(val("vl"), s0, plane("slT", 0), A.subtract)
-        vr = tt(val("vr"), s0, plane("srT", 0), A.subtract)
-        tt(plane("wu", 1), vl, vr, A.is_equal)
-        tt(plane("wu", 5), vl, vr, A.is_gt)
-        cv = tt(plane("wu", 2), vl, vr, A.min)
-        cn = better_child("wu", 0)
-        child = dense("dc", 0)
-        copy("s", child, cn, bias=col(10))
+        if VCUT:
+            for a, z in ((0, VCUT), (VCUT, C)):
+                tt(("wu", a + 4, z, 16), ("sT", a, z, 16), ("slT", a, z, 16), A.subtract)
+                tt(("wu", a + 8, z, 16), ("sT", a, z, 16), ("srT", a, z, 16), A.subtract)
+                turn(cols("urow", a, z), cols("wu", a, z))
+        else:
+            tt(plane("wu", 4), s0, plane("slT", 0), A.subtract)
+            tt(plane("wu", 8), s0, plane("srT", 0), A.subtract)
+            halves("urow", "wu")
+        brought("ul", urow, ll)
+        brought("ur", urow, lr)
+        for b in range(4):
+            if XV[b]:
+                copy("s", cols("fo%d" % b, 0, XV[b]), ps(1 + b, XV[b]))
+        v0 = tt(slot(0, 0, "mc"), plane("saT", 0), s0, A.subtract)
+        first_of(0, "wu", v0, (2, 0, 1), 2, four(0, "so"))
+        child = tt(dense("dc", 0), slot(0, 1, "so"), rv, A.add)
+        tt(plane("wq_", LW + LB - LO), slot(0, 1, "so"), apart, A.is_equal)
         swapped("dc", 0, 64, 288)
         make_list(cols("lc", 0, 64), cols("dc", 0, 224), cols("offm", 0, 4))
-        turn(cols("urow"), cols("wu"))
-        in_line("turns")
-        turned("sa")
-        in_line("turns")
-        gather("s", cols("ul"), urow, ll)
-        shared("ur", urow, lr, CUT_UR, "turns")
-        in_line("claims")
-        for b in range(3):
-            copy("s", cols("fo%d" % b), ps(1 + b))
-            in_line("claims")
-        for n in ("ul", "ur"):
-            turned(n)
-        v0 = tt(val("v0"), plane("saT", 0), s0, A.subtract)
-        m = tt(val("m1"), v0, ts(val("m0"), cv, -1.0e-30, A.min), A.min)
-        ul, ur = plane("ulT", 2), plane("urT", 2)
-        m = tt(val("m3"), tt(val("m2"), m, ul, A.min), ur, A.min)
-        for i, (v, n) in enumerate(((v0, n2), (cv, cn), (ul, better_child("ulT", 3)), (ur, better_child("urT", 1)))):
-            tt(("sw", 224 + i, C, 8), tt(val("e%d" % i), v, m, A.is_equal), n, A.mult)
-        scan(("wq_", 0, C, 2), cols("sw", 0, 224), cols("sw", 224, C), A.add, A.min)
+        tt(plane("ulT", 5), slot(0, 3, "so"), plane("ulT", 3), A.subtract)
+        first_of(1, "ulT", slot(0, 3, "mo"), (0, 1, 2), 1, four(1, "so"))
+        tt(plane("urT", 5), slot(1, 3, "so"), plane("urT", 3), A.subtract)
+        first_of(2, "urT", slot(1, 3, "mo") if MSCAN else slot(1, 0, "mc"), (0, 1, 2), 1, lanes("wq_", 0))
         B = plane("wq_", LB)
-        turn(cols("qrow"), cols("wq_"))
-        gather("s", cols("qa"), cols("qrow"), la)
-        in_line("claims")
-        gather("v", cols("qc"), qrow, lc)
-        in_line("turns")
-        shared("qaa", cols("qrow"), laa, CUT_AA, "turns")
-        in_line("claims")
-        gather("s", cols("qaaa"), cols("qa"), laa)
-        in_line("claims")
-        for n in ("qa", "qc", "qaa", "qaaa"):
-            turned(n)
-            in_line("turns")
-        e01 = tt(slot(6, 1), B, plane("qaT", LB), A.is_equal)
-        e12 = tt(slot(4, 2), plane("qaT", LB), plane("qaaT", LB), A.is_equal)
-        tt(slot(4, 1), plane("qaaT", LB), plane("qaaaT", LB), A.is_equal)
+        turn(cols("qx"), cols("wq_"))
+        if MERGE:
+            turn(cols("qy"), cols("wq_", LB - LO, C + LB - LO))
+            gather_add(cols("qw"), cols("qx"), la, cols("qy"))
+            turn(cols("qwT"), cols("qw"))
+            brought("qc", cols("qx", 0, WIDE), lc)
+            brought("g2", cols("qw"), laa)
+            b1, b2, b3, b4 = plane("qwT", LB), plane("g2T", LO), plane("g2T", LB), plane("g2T", LW)
+        else:
+            brought("qw", cols("qx"), la)
+            brought("qc", cols("qx", 0, WIDE), lc)
+            brought("qy", cols("qx"), laa)
+            brought("g2", cols("qw"), laa)
+            b1, b2, b3, b4 = plane("qwT", LB), plane("qyT", LB), plane("g2T", LB), plane("qyT", LW + LB - LO)
+        e01 = tt(slot(6, 1), B, b1, A.is_equal)
+        e12 = tt(slot(4, 2), b1, b2, A.is_equal)
+        tt(slot(4, 1), b2, b3, A.is_equal)
         tt(slot(7, 0), B, child, A.is_equal)
         tt(slot(6, 2), plane("qcT", LB), child, A.is_equal)
         tt(slot(6, 3), B, pv, A.subtract)
         scan(four(2, "so"), four(6), four(7))
         tt(slot(5, 3), slot(2, 3, "so"), pv, A.add)
         r1 = tt(slot(5, 1), tt(val("x0"), B, nv, A.is_equal), e01, A.mult)
-        tt(slot(5, 0), tt(val("i1"), plane("qaT", LC), nv, A.is_equal), tt(val("x1"), plane("qaT", LB), pv, A.is_equal), A.mult)
-        scan(cols("da", 0, 112), four(4), four(5))
-        swapped("da", 0, 128, 0)
-        make_list(cols(la2[0], 0, 32), cols("da", 0, 288), cols("offa", 0, 2))
-        exchange(dst, "arl%d" % k, [(ap(al), ap(la2), la2, al)], SHORT)
+        side = tt(("sc", 57, 112, 2), plane("qwT", LC), nv, A.not_equal)
+        tt(("sc", 56, 112, 2), b1, pv, A.not_equal)
+        scan(cols("sc", 112, 168), cols("sc", 0, 56), cols("sc", 56, 112))
+        tt(slot(5, 0), b4, ("sc", 113, 168, 2), A.is_equal)
+        inner = tt(val("in"), rv, tt(val("d6"), side, apart, A.mult), A.add)
+        tt(("sx", 1, 56, 2), inner, nv, A.subtract)
+        from_inner = tt(val("pc"), pv, inner, A.subtract)
+        scan(cols(da, 0, 112), four(4), four(5))
+        swapped(da, 0, 128, 0)
+        make_list(cols(la2[0], 0, 32), cols(da, 0, 288), cols("offa", 0, 2))
+        exchange(dst, "arl%d" % k, [(ap(al), ap(la2), la2)], [al], SHORT)
         rot = tt(("sx", 56, 112, 2), r1, e12, A.mult)
         scan(("so", 225, 336, 2), cols("sx", 0, 56), cols("sx", 56, 112))
         tt(("sx", 115, 224, 4), B, nv, A.subtract)
-        scan(("wr", 0, C, 4), cols("sx", 112, 224), four(2, "so"))
+        scan(lanes("wr", 0), cols("sx", 112, 224), four(2, "so"))
         turn(cols("rrep"), cols("wr"))
-        gather("s", cols("repl"), rrep, ll)
-        shared("repr_", rrep, lr, CUT_RR)
-        turn(cols("repT"), cols("repl"))
-        turn(cols("repT", 512, 512 + C), cols("repr_"))
+        if EARLY:
+            unpack(aq, as_)
+        if EARLY == 1 and not last:
+            grandparents((da, 3, 112, 4), la2, "gap")
+        brought("repl", rrep, ll, "repT", line="gap" if EARLY else None)
+        brought("repr_", rrep, lr, "repT", 512, line="gap" if EARLY else None)
+        if EARLY == 2 and not last:
+            grandparents((da, 3, 112, 4), la2, "gap")
+        if EARLY == 3 and not last:
+            grandparents((da, 3, 112, 4), la2)
         rp = tt(val("rp"), rot, from_inner, A.mult)
         tt(dense("dd", 1), rp, tt(dense("dd", 0), rp, side, A.mult), A.subtract)
         tt(cols("dt", 32, 92), ("repT", 12, 512 + C, 16), cols("dd", 0, 60), A.add)
         if last:
+            pv = (da, 3, 112, 4)
             e = tt(val("f0"), pv, nv, A.is_equal)
-            e = tt(val("f2"), e, ts(val("f1"), nv, -1.0, A.mult, 224.0, A.add), A.mult)
+            e = tt(val("f2"), e, ts(val("f1"), nv, -1.0, A.mult, NONE, A.add), A.mult)
             tt(plane("wt", LP), pv, e, A.add)
             copy("s", plane("wt", LL), lv)
             copy("s", plane("wt", LR), rv)
             turn(cols("trow"), cols("wt"))
-            copy("s", cols("trf"), cols("trow"), bias=col(8))
+            copy("s", cols("trf"), cols("trow"), scale=512.0, bias=col(8))
             dmas("y", "st_tr", [(T.tr[:, C * i:C * i + C], T.trf[i:128:16, :], [cols("trf")], []) for i in range(3)])
         else:
             swapped("dt", 32, 96, 176)
             make_list(cols("lb", 0, 64), cols("dt", 0, 256), cols("offm", 2, 6))
-        fbank = [5, 6, 7, 0]
-        for b in range(4):
-            mm(fbank[b], "eq", "es", b, aq, as_)
-            fp, fq = cols("fp%d" % b), cols("fq", C * b, C * b + C)
-            copy("s", fp, ps(fbank[b]))
-            if b < 3:
-                dmas("y", "cf%d" % b, [(ap(fq), ap(fp), [fp], [fq])], LOCAL + 0.6)
+        fbank = FBANK
+        if not EARLY:
+            unpack(aq, as_)
         kb = [cols("kb", C * b, C * b + C) for b in range(4)]
-        gather("s", cols("kg"), cols("fp3"), al)
         for b in (0, 1, 3, 2):
-            if b == 3:
-                tt(kb[3], cols("kg"), ps(fbank[3]), A.add)
-            else:
-                gather_add(kb[b], cols("fp%d" % b), al, cols("fq", C * b, C * b + C))
-            in_line("sums")
-        for b in (0, 1, 3):
-            gather("s", ("zt", b, 4 * C, 4), kb[b], al, 0.5)
-        for h in range(2):
-            gather("vs"[h], piece("zt", h, CUT_Z, 2), kb[2], part(al, h, CUT_Z), 0.5)
-        wbank = [1, 2, 7, 6]
-        for h, bank in enumerate((1, 5, 3)):
+            x = KV[b]
+            if x:
+                gather_add(cols("kb", C * b, C * b + x), cols("fp%d" % b), part(al, 0, x), cols("fq", C * b, C * b + x))
+                in_line("sums")
+            if x < C:
+                gather("s", cols("kg%d" % b, x, C), cols("fp%d" % b), part(al, x, C))
+                if EARLY:
+                    in_line("gap")
+                tt(cols("kb", C * b + x, C * b + C), cols("kg%d" % b, x, C), ps(fbank[b], C - x, x), A.add)
+                in_line("sums")
+        if k == 0:
+            dmas("y", "ld_v", [(T.vt[:], T.v[:], [cols("kb", 0, 1)], [cols("vt", 0, 512)])])
+        for b in range(4):
+            a = 0
+            for qq, z in ZSHARE[b]:
+                gather(qq, ("zt", 4 * a + b, 4 * z, 4), kb[b], part(al, a, z), 0.5)
+                a = z
+        for h, bank in enumerate((1, 5, 0)):
             quantize_piece("zq", "zs", "zt", h)
             mm(bank, "wq", "wp", 0, "zq", "zs", CUT[h], CUT[h + 1])
             in_line("layer")
-            copy("ssv"[h], piece("rr0", h), ps(bank, CUT[h + 1] - CUT[h]), scale=0.03125)
-        for b in (1, 3, 2):
-            mm(wbank[b], "wq", "wp", b, "zq", "zs")
-            in_line("layer")
-            copy("s", cols("rr%d" % b), ps(wbank[b]), scale=0.03125)
-            in_line("claims")
-        gather("s", cols("xg"), cols("rr3"), la2)
-        in_line("claims")
-        for b in range(3):
-            gather_add(("xn", b, 4 * C, 4), cols("rr%d" % b), la2, cols("fo%d" % b))
-            in_line("turns")
-        for h in range(2):
-            tt(piece("xn", h, CUT_X, 3), piece("xg", h, CUT_X), ps(4, CUT_X[h + 1] - CUT_X[h], CUT_X[h]), A.add)
-            in_line("turns")
-        for h in range(3):
-            quantize_piece("q%d" % (k + 1), "qs%d" % (k + 1), "xn", h)
+            copy(RQ[h], piece("rr0", h), ps(bank, CUT[h + 1] - CUT[h]), scale=0.03125)
+            if h == 1 and SOON:
+                mm(2, "wq", "wp", RORDER[0], "zq", "zs", 0, CUT[2])
+                in_line("layer")
+                copy("s", cols("rr%d" % RORDER[0], 0, CUT[2]), ps(2, CUT[2]), scale=0.03125)
+                in_line("state")
+        banks = [6, 7, 1, 5, 0] if SOON else [2, 6, 7, 1, 5, 0]
+        for b in RORDER:
+            for (a, z), qq in zip([(CUT[2], C)] if SOON and b == RORDER[0] else zip(RCUT, RCUT[1:]), RQ2[b]):
+                bank = banks.pop(0)
+                mm(bank, "wq", "wp", b, "zq", "zs", a, z)
+                in_line("layer")
+                copy(qq, cols("rr%d" % b, a, z), ps(bank, z - a), scale=0.03125)
+                if qq == "s" and STATE:
+                    in_line("state")
+        apiece = last and LAST
+        steps = []
+        for b in range(4):
+            cut = sorted({0, XV[b], C} | (set(CUT) if apiece and b >= 2 else set(CUT_X) if XV[b] < C else set()))
+            steps += [(a if apiece else 0, z > XV[b], b, a, z) for a, z in zip(cut, cut[1:])]
+            if XV[b] < C and not apiece:
+                gather("s", cols("xg%d" % b, XV[b], C), cols("rr%d" % b), part(la2, XV[b], C))
+                in_line("state")
+        steps += [(CUT[h + 1] + (h < 2) if apiece else C, 2, h, 0, 0) for h in range(3)]
+        for _, how, b, a, z in sorted(steps, key=lambda s: s[:2] + (((0,) + RORDER).index(s[2]) if s[1] < 2 else s[2],) + s[3:]):
+            if how == 2:
+                quantize_piece("q%d" % (k + 1), "qs%d" % (k + 1), "xn", b)
+            elif how:
+                if apiece:
+                    gather("s", cols("xg%d" % b, a, z), cols("rr%d" % b), part(la2, a, z))
+                    in_line("state")
+                tt(("xn", 4 * a + b, 4 * z, 4), cols("xg%d" % b, a, z), ps(1 + b, z - a, a), A.add)
+            else:
+                gather_add(("xn", 4 * a + b, 4 * z, 4), cols("rr%d" % b), part(la2, a, z), cols("fo%d" % b, a, z))
             in_line("turns")
 
     quantize("vq", "vs", 0, 128, cols("vt", 0, 512))

@@ -6,35 +6,29 @@ STEP = [1, 2, 3]
 BIGV = 3.0e29
 UNIT = 1.0 / 512
 NONE = 224 * UNIT
+HUGE = 2.0 ** 72
 WIDE = 976
 CUT = [0, 192, 320, C]
-SHARE = {"sl": [("s", 256), ("s", C)], "sr": [("v", 256), ("s", C)], "sa": [("s", C)],
-         "ul": [("s", 224), ("s", C)], "ur": [("v", 64), ("s", 256), ("s", C)],
-         "qw": [("s", C)], "qy": [("v", C)], "qc": [("s", C)], "g2": [("s", 320), ("s", C)], "pp": [("s", 224), ("s", C)],
-         "repl": [("s", 224), ("s", C)], "repr_": [("v", 320), ("s", C)]}
-CUT_X = [0, 192, 320, C]
-CYCLE, SAME, CROSS, LOCAL, SHORT, LONG = 0.001, 0.2, 0.22, 2.0, 1.6, 8.0
-PASSES = 3
-TRIES, REACH, HEAT, SWEEPS, SPAN, AHEAD, EAGER = 2200, 10, 0.005, 2, 120, 80, 0.3
-CLOCKS = [(0.226, 0.2, 1.0, 1.5, 0.83), (0.225, 0.21, 1.0, 1.08, 0.83), (0.235, 0.21, 1.4, 1.2, 0.83), (0.16, 0.24, 1.5, 1.95, 1.09)]
-SMIN = 185
-MARCH, EASE, SLACK = False, 0.0, 0.0
-PLAN = {}
-GATHER, GADD, PRODUCT = 1.8, 1.8, 0.5
-MERGE = True
+LCUT, RCUT = [0, 224, C], [0, 224, C]
+SHARE = {"sa": [("s", C)], "ul": [("s", 224), ("s", C)], "ur": [("s", 256), ("s", C)],
+         "qc": [("s", C)], "g2": [("s", 320), ("s", C)], "qz": [("s", C)]}
 KV = [C, C, C, 0]
 ZSHARE = [[("s", C)], [("s", C)], [("v", 192), ("v", 320), ("s", C)], [("s", C)]]
-XV, RORDER = [C, C, C, 0], (1, 3, 2)
-RCUT, RQ2, STATE = [0, C], "svss", True
-HALF, TFIX, SFIX, SMALL = True, 0, 30, "ggg"
-EARLY, FBANK = 3, [5, 6, 7, 0]
-DELAY, TI, MSCAN, VCUT = 0, 0.1, False, 256
-SOON = True
-LAST = True
-RELAY = 0
-TWIN, FORDER, TPS = "yyyy", (0, 1, 2, 3), True
-SQ = "svs"
-RQ = "svv"
+XV, RORDER = [C, C, 320, 0], (1, 3, 2)
+RQ, RQ2 = "svv", "svss"
+TWINS = "sgg"
+FSOON, FLATE = (), (0, 1, 2, 3)
+FBANK = [5, 6, 7, 0]
+CODED = "s"
+LOADS = [("t", "y", 0.1), ("u", "y", 0.3), (0, "y", 0.7), (1, "y", 1.0), (2, "y", 1.3)]
+CYCLE, SAME, CROSS, LOCAL, TWIN, SHORT, LONG, FIRST, ISSUE = 0.001, 0.2, 0.22, 2.0, 2.7, 1.05, 6.5, 0.5, 0.6
+GATHER, PRODUCT, SMIN = 1.8, 0.5, 185
+CLOCKS = [(0.226, 0.2, 1.0, 1.5, 0.83, 0.9), (0.225, 0.21, 1.2, 1.12, 0.89, 0.75), (0.22, 0.21, 1.7, 1.8, 0.87, 0.8), (0.16, 0.24, 1.5, 1.95, 1.09, 1.0)]
+WEIGHTS, LATER = (0.25, 0.35, 0.15, 0.2), (0.0, 0.45, 0.3, 0.2)
+PASSES, TRIES, REACH, HEAT, SWEEPS, SPAN, EAGER, SEED = 3, 5000, 6, 0.05, 4, 60, 0.25, 1
+AGAIN, HEAD, EARLY = 0, 150, (0.6, 0.55, 0.65, 0.65)
+FREE, WHOLE, COOL = ("layer", "start"), False, 0.6
+PLAN = {}
 
 F32, BF, U16, I32, CODE, PLANE = "float32", "bfloat16", "uint16", "int32", "float8_e4m3fn_x4", "uint8"
 SCRATCH = {"ps": ("psum", [128, 4096], F32)}
@@ -48,69 +42,45 @@ def _sbuf(names, n, dtype):
 _sbuf("xt xn zt fq kb", 4 * C, BF)
 _sbuf("ut vt ones", 512, BF)
 _sbuf("et", 516, BF)
-_sbuf("uq vq", 128, CODE)
-_sbuf("hq0 hq1 hq2", 256, CODE)
-_sbuf("us vs", 128, PLANE)
+_sbuf("u0 uq vq", 128, CODE)
+_sbuf("s0 us vs", 128, PLANE)
 _sbuf("wq eq", 512, CODE)
 _sbuf("wp es", 512, PLANE)
 _sbuf("zq q0 q1 q2 q3 aq0 aq1 aq2", C, CODE)
 _sbuf("zs qs0 qs1 qs2 qs3 as0 as1 as2", C, PLANE)
 _sbuf("pidx", 8, I32)
-_sbuf("col", 16, F32)
-_sbuf("i16 i32 jt nn", 28, F32)
-_sbuf("offm", 6, U16)
+_sbuf("col", 32, F32)
+_sbuf("lane", 48, F32)
+_sbuf("i16 i32 nn", 28, F32)
+_sbuf("offm offu", 8, U16)
 _sbuf("offa", 2, U16)
 _sbuf("ti", 96, I32)
 _sbuf("al0 al1 al2", 28, U16)
-_sbuf("la0 la1 la2 la3", 32, U16)
+_sbuf("la0 la1 la2 la3 lw", 32, U16)
 _sbuf("lb lc", 64, U16)
-_sbuf("di dt dc", 256, BF)
-_sbuf("da0 da1", 288, BF)
-_sbuf("eb", 448, BF)
-_sbuf("dd", 64, F32)
-_sbuf("qx", WIDE, BF)
-_sbuf("wq_ rrep", 464, BF)
-_sbuf("srow", 456, F32)
-_sbuf("wu urow", 480, F32)
-_sbuf("wr wt trow pp ppT qy qw qc g2 qwT qyT qcT g2T repl repr_ kg0 kg1 kg2 kg3", C, BF)
-_sbuf("repT", 512 + C, BF)
-_sbuf("sa sl sr ul ur xg2 xg3 sT saT slT srT ulT urT trf yt rr0 rr1 rr2 rr3", C, F32)
+_sbuf("di dt dc dw", 256, BF)
+_sbuf("da0 da1 dr", 288, BF)
+_sbuf("eb wq_", 512, BF)
+_sbuf("qw", C + WIDE, BF)
+_sbuf("w1 w2 urow", 456, F32)
+_sbuf("wt trow qy qc qz g2 qwT qcT qzT g2T kg0 kg1 kg2 kg3", C, BF)
+_sbuf("sa ul ur xg2 xg3 srow mrow lrow saT ulT urT gT trf yt rr0 rr1 rr2 rr3", C, F32)
 _sbuf("sc", 1024, F32)
-_sbuf("mc mo ne so", 3 * 112, F32)
-_sbuf("sx", 224, F32)
-_sbuf("cb", 28 * 16, F32)
+_sbuf("w0", 112, F32)
+_sbuf("st", 512, F32)
+_sbuf("mc mo ne so fin", 3 * 112, F32)
+_sbuf("dd", 672, F32)
+_sbuf("cb", 28 * 24, F32)
 _sbuf("fo0 fo1 fo2 fo3 fp0 fp1 fp2 fp3", C, BF)
 
 SEMAPHORES = (["cv", "cs", "ct", "cg", "sent"] + ["ld_" + k for k in "x0 x1 x2 u v t w".split()]
               + ["st_" + k for k in "y0 y1 y2 oc0 oc1 oc2 sc tr".split()] + ["cf%d" % k for k in range(4)]
-              + ["hop%d" % k for k in range(3)] + ["arq%d" % k for k in range(3)] + ["arl%d" % k for k in range(3)])
+              + ["arq%d" % k for k in range(3)] + ["arl%d" % k for k in range(3)])
 
 
 def rank_program(g, core, T, topo):
-    def helper(c):
-        return [h for h in topo.cores_of(c) if topo.die(h) != topo.die(c) and h not in T.cores and all(topo.may_write(h, d) for d in T.cores)][0]
-
-    def write(out, in_, dst, sem, mask):
-        rid, pid, se = topo.addr(dst)
-        g.remote_dma(out, in_, T.sem[sem], T.sem["sent"], pid, rid, mask)
-
-    def engines(mask):
-        return bin(mask).count("1")
-
-    def inward(c):
-        return topo.mask(c, helper(c)) & ~topo.mask(c, T.cores[(T.rank_of(c) + 1) % N])
-
     rank = T.rank_of(core)
     if rank is None:
-        for r, c in enumerate(T.cores):
-            if RELAY and helper(c) == core:
-                sent = 0
-                for k in range(3):
-                    dst = T.cores[(r + STEP[k]) % N]
-                    g.wait_ge(T.sem["hop%d" % k], engines(inward(c)))
-                    write(T["aq%d" % k][:, 0:RELAY].bitcast(dt.uint8), T["hq%d" % k][:, 0:RELAY].bitcast(dt.uint8), dst, "arq%d" % k, topo.mask(core, dst))
-                    sent += engines(topo.mask(core, dst))
-                g.wait_ge(T.sem["sent"], sent)
         return
     A = AluOpType
     ACT = ActivationFunctionType
@@ -148,7 +118,7 @@ def rank_program(g, core, T, topo):
     lines = {}
 
     def in_line(name):
-        if name in lines:
+        if name in lines and name not in FREE:
             calls[-1]["after"].setdefault(lines[name], False)
         lines[name] = len(calls) - 1
 
@@ -164,16 +134,17 @@ def rank_program(g, core, T, topo):
                 queue[q].dma_start(m[0], m[1]).then_inc(T.sem[sem], 16)
         record(q, issue, sem, 16 * len(moves), 0.05 * len(moves), takes, sum([m[2] for m in moves], []), sum([m[3] for m in moves], []))
 
-    def exchange(dst, sem, moves, lands, takes, more=0):
-        n = len(moves) * engines(topo.mask(core, dst))
+    def exchange(dst, sem, moves, lands, takes):
+        rid, pid, se = topo.addr(dst)
+        n = len(moves) * len(topo.engines(core, dst))
 
         def issue():
             for m in moves:
-                write(m[0], m[1], dst, sem, topo.mask(core, dst))
+                g.remote_dma(m[0], m[1], T.sem[sem], T.sem["sent"], pid, rid, topo.mask(core, dst))
         mark = (sem, 0, 1, 1)
-        record("g", issue, "sent", n, 0.1, 0.1, [m[2] for m in moves], [mark])
-        in_line("twins")
-        record(None, None, sem, n + more, 0.0, takes, [mark], lands)
+        record("g", issue, "sent", n, ISSUE * len(moves), ISSUE * len(moves), [m[2] for m in moves], [mark])
+        in_line("writes")
+        record(None, None, sem, n, 0.0, takes + 0.1 - ISSUE * len(moves), [mark], lands)
 
     def issue_all():
         def span(i, j):
@@ -211,57 +182,28 @@ def rank_program(g, core, T, topo):
 
         def length(at):
             return max(at[j] + calls[j]["takes"] for j in every)
-
-        def march(due):
-            at, free = {}, {q: 0.0 for q in queue}
-            left = [len(c["after"]) for c in calls]
-            ready = {j: 0.0 for j in every if not left[j]}
-            while ready:
-                t, q = min((max(r, free.get(calls[j]["q"], 0.0)), calls[j]["q"] or "") for j, r in ready.items())
-                mine = sorted((due[j], j) for j in ready if (calls[j]["q"] or "") == q)
-                soon = t + 1e9
-                for d, j in mine:
-                    if ready[j] > t + 1e-9:
-                        soon = min(soon, max(ready[j], d - due0[0]) + EASE)
-                    elif t + calls[j]["holds"] <= soon:
-                        break
-                else:
-                    free[q] = min(ready[j] for d, j in mine if ready[j] > t + 1e-9)
-                    continue
-                at[j] = t
-                if q:
-                    free[q] = t + calls[j]["holds"]
-                del ready[j]
-                for i in before[j]:
-                    left[i] -= 1
-                    if not left[i]:
-                        ready[i] = max(at[h] + span(h, i) for h in calls[i]["after"])
-            return at
         qs = [c["q"] for c in calls]
         paces = []
-        for same, cross, product, rate, pace in CLOCKS:
-            holds, takes = [[(c[x] + c.get("per", 0) * (rate - GATHER) * CYCLE) * (product if c["q"] == "t" else pace if c["sem"][0] == "c" and len(c["sem"]) == 2 else 1.0)
-                             for c in calls] for x in ("holds", "takes")]
+        for same, cross, product, rate, pace, moves in CLOCKS + [c[:5] + (m,) for c, m in zip(CLOCKS, EARLY)]:
+            factor = [product if c["q"] == "t" else pace if len(c["sem"]) == 2 else moves if c["sem"][2] == "_" else 1.0 for c in calls]
+            holds, takes = [[(c[x] + c.get("per", 0) * (rate - GATHER) * CYCLE) * f for c, f in zip(calls, factor)] for x in ("holds", "takes")]
+            takes = [t + (LATER[len(paces) % len(CLOCKS)] if c["sem"][:3] == "arl" else 0.0) for c, t in zip(calls, takes)]
             links = [[(i, takes[i] if qs[j] is None else takes[i] + (same if qs[i] == qs[j] else cross) if w else holds[i])
                       for i, w in c["after"].items()] for j, c in enumerate(calls)]
             paces.append((links, holds, takes))
 
         def clock(order, links, holds, takes):
-            at, why, free, last, end, tail = [0.0] * len(calls), [-1] * len(calls), {}, {}, 0.0, -1
+            at, free, end = [0.0] * len(calls), {}, 0.0
             for j in order:
-                t, w = 0.0, -1
+                t = free.get(qs[j], 0.0)
                 for i, d in links[j]:
                     if at[i] + d > t:
-                        t, w = at[i] + d, i
-                q = qs[j]
-                if q:
-                    if free.get(q, 0.0) > t + 1e-9:
-                        t, w = free[q], last[q]
-                    free[q], last[q] = t + holds[j], j
-                at[j], why[j] = t, w
-                if t + takes[j] > end:
-                    end, tail = t + takes[j], j
-            return end, at, why, tail
+                        t = at[i] + d
+                if qs[j]:
+                    free[qs[j]] = t + holds[j]
+                at[j] = t
+                end = max(end, t + takes[j])
+            return end, at
 
         def moved(order, a, b, ahead):
             mid = order[a:b + 1]
@@ -274,62 +216,77 @@ def rank_program(g, core, T, topo):
             x, y = [j for j in mid if j in group], [j for j in mid if j not in group]
             return order[:a] + (x + y if ahead else y + x) + order[b + 1:]
 
-        def stretch(part_, ats, frees):
+        def tails(order, lo, links, holds, takes):
+            far, first = list(takes), {}
+            for j in reversed(order[lo:]):
+                if qs[j] in first:
+                    far[j] = max(far[j], holds[j] + far[first[qs[j]]])
+                if qs[j]:
+                    first[qs[j]] = j
+                for i, d in links[j]:
+                    if d + far[j] > far[i]:
+                        far[i] = d + far[j]
+            return far, {q: far[j] for q, j in first.items()}
+
+        eager = [EAGER]
+
+        def stretch(part_, ats, frees, fars):
             total = 0.0
-            for (links, holds, takes), at, free in zip(paces, ats, frees):
-                free, early = dict(free), 0.0
+            for (links, holds, takes), at, free, (far, first), weight in zip(paces, ats, frees, fars, WEIGHTS):
+                free, early, end = dict(free), 0.0, 0.0
                 for j in part_:
-                    t = free.get(qs[j], 0.0)
+                    q = qs[j]
+                    t = free.get(q, 0.0)
                     for i, d in links[j]:
                         if at[i] + d > t:
                             t = at[i] + d
                     at[j] = t
                     early += t
-                    if qs[j]:
-                        free[qs[j]] = t + holds[j]
-                total += max(at[j] + takes[j] for j in part_[-12:]) + EAGER * early / len(part_)
-            return total / len(paces)
+                    if t + far[j] > end:
+                        end = t + far[j]
+                    if q:
+                        free[q] = t + holds[j]
+                for q, x in first.items():
+                    end = max(end, free.get(q, 0.0) + x)
+                total += weight * (end + eager[0] * early / len(part_))
+            return total
 
         def polish(order):
-            seed = 1
-            for sweep in range(SWEEPS):
-                for lo in range(0, len(order) - 20, SPAN // 2):
+            seed, both = SEED, list(paces)
+            for sweep in range(SWEEPS + AGAIN):
+                paces[:] = both[:len(CLOCKS)] if sweep < SWEEPS else both[len(CLOCKS):]
+                heat, eager[0] = HEAT * COOL ** sweep, EAGER * COOL ** sweep
+                for lo in [0] + list(range(SPAN // 2 - sweep % 2 * (SPAN // 4), len(order) - 20 if sweep < SWEEPS else HEAD, SPAN // 2)):
                     ats = [clock(order, *p)[1] for p in paces]
                     order = sorted(order, key=lambda j: sum(at[j] for at in ats))
-                    frees = []
-                    for (links, holds, takes), at in zip(paces, ats):
-                        frees.append({qs[j]: at[j] + holds[j] for j in order[:lo] if qs[j]})
-                    mid = order[lo:lo + SPAN + AHEAD]
-                    now = best = stretch(mid, ats, frees)
+                    frees = [{qs[j]: at[j] + p[1][j] for j in order[:lo] if qs[j]} for p, at in zip(paces, ats)]
+                    fars = [tails(order, lo + SPAN, *p) for p in paces]
+                    mid = order[lo:lo + SPAN]
+                    now = best = stretch(mid, ats, frees, fars)
                     keep = mid
                     for n in range(TRIES):
                         seed = (seed * 1103515245 + 12345) % 2147483648
-                        a = (seed >> 8) % min(SPAN, len(mid))
+                        a = (seed >> 8) % len(mid)
                         mine = [i for i in range(a + 1, min(len(mid), a + 60)) if qs[mid[i]] == qs[mid[a]]]
                         if not qs[mid[a]] or not mine:
                             continue
                         new = moved(mid, a, mine[(seed >> 18) % min(REACH, len(mine))], seed >> 28 & 1)
                         if new:
-                            got = stretch(new, ats, frees)
-                            if got <= now + HEAT * (1.0 - n / TRIES) * ((seed >> 4) % 16) / 16.0:
+                            got = stretch(new, ats, frees, fars)
+                            if got <= now + heat * (1.0 - n / TRIES) * ((seed >> 4) % 16) / 16.0:
                                 mid, now = new, got
                                 if got < best:
                                     best, keep = got, new
-                    order = order[:lo] + keep + order[lo + SPAN + AHEAD:]
+                    order = order[:lo] + keep + order[lo + SPAN:]
+            PLAN["ends"] = [round(clock(order, *p)[0], 2) for p in paces]
             return clock(order, *paces[0])[1]
-        due0 = [0.0]
         if "start" not in PLAN:
             best = place(sorted(every, key=lambda j: (-way[j], j)), False)
             start = best
             for _ in range(PASSES):
                 late = place(sorted(every, key=lambda j: (-start[j] - calls[j]["holds"], -j)), True)
-                if MARCH:
-                    end = max(late[j] + calls[j]["holds"] for j in every)
-                    due0[0] = SLACK
-                    start = march([end - late[j] - calls[j]["holds"] for j in every])
-                else:
-                    start = place(sorted(every, key=lambda j: (-late[j] - calls[j]["holds"], j)), False)
-                if length(start) <= length(best) or (MARCH and _ == 0):
+                start = place(sorted(every, key=lambda j: (-late[j] - calls[j]["holds"], j)), False)
+                if length(start) <= length(best):
                     best = start
             PLAN["start"] = polish(sorted(every, key=lambda j: (best[j], j))) if TRIES else best
         start = PLAN["start"]
@@ -364,9 +321,8 @@ def rank_program(g, core, T, topo):
     def cols(buf, a=0, b=C):
         return buf, a, b, 1
 
-    def piece(buf, h, cut=CUT, b=None):
-        a, z = cut[h], cut[h + 1]
-        return (buf, a, z, 1) if b is None else (buf, 4 * a + b, 4 * z, 4)
+    def piece(buf, h):
+        return buf, CUT[h], CUT[h + 1], 1
 
     def part(off, a, z):
         return off[0], off[1] + a // 16, off[1] + z // 16, 1
@@ -374,8 +330,8 @@ def rank_program(g, core, T, topo):
     def ps(b, n=C, a=0):
         return "ps", 512 * b + a, 512 * b + a + n, 1
 
-    def plane(buf, lane, end=C):
-        return buf, lane, end, 16
+    def plane(buf, lane):
+        return buf, lane, C, 16
 
     def lanes(buf, first):
         return buf, first, C, 4
@@ -398,28 +354,31 @@ def rank_program(g, core, T, topo):
     def four(i, buf="sc"):
         return buf, 112 * i, 112 * i + 112, 1
 
+    def number(s):
+        return ap(s) if isinstance(s, tuple) else s
+
+    def views(*more):
+        return [s for s in more if isinstance(s, tuple)]
+
     def tt(out, a, b, o):
         op("v", lambda: V.tensor_tensor(ap(out), ap(a), ap(b), o), [a, b], [out], size(out) * (1 if b[0] == "ps" else 2))
         return out
 
     def ts(out, a, s1, o1, s2=None, o2=None):
-        more = [s for s in (s1, s2) if isinstance(s, tuple)]
-        s1, s2 = [ap(s) if isinstance(s, tuple) else s for s in (s1, s2)]
         rest = (o1,) if o2 is None else (o1, o2)
-        op("v", lambda: V.tensor_scalar(ap(out), ap(a), s1, s2, *rest), [a] + more, [out], size(out) * narrow(out, a))
+        op("v", lambda: V.tensor_scalar(ap(out), ap(a), number(s1), number(s2), *rest), [a] + views(s1, s2), [out], size(out) * narrow(out, a))
         return out
 
     def scan(out, d0, d1, o0=A.mult, o1=A.add):
         op("v", lambda: V.tensor_tensor_scan(ap(out), ap(d0), ap(d1), 0.0, o0, o1), [d0, d1], [out], size(out))
 
     def turn(out, in_):
-        op("v", lambda: V.transpose(ap(out), ap(in_)), [in_], [out], max(64, size(out) * narrow(out)) + TFIX)
+        op("v", lambda: V.transpose(ap(out), ap(in_)), [in_], [out], size(out) * narrow(out))
 
-    def halves(out, in_):
-        if not HALF:
-            return turn(cols(out), cols(in_))
-        for a in (0, C // 2):
-            turn(cols(out, a, a + C // 2), cols(in_, a, a + C // 2))
+    def act(out, in_, scale, bias):
+        if bias is None:
+            return S.activation(ap(out), in_, ACT.Copy, scale=number(scale))
+        return S.activation(ap(out), in_, ACT.Identity, bias=ap(bias), scale=number(scale))
 
     def copy(q, out, in_, scale=1.0, bias=None):
         if q == "v" and scale == 1.0:
@@ -428,37 +387,32 @@ def rank_program(g, core, T, topo):
             ts(out, in_, scale, A.mult)
         elif q == "g":
             op("g", lambda: g.affine_select(ap(out), ap(in_), [[0, size(out)]], A.is_equal, 0.0, 0, 0), [in_], [out], 200 + 2 * size(out))
-        elif bias is None:
-            op("s", lambda: S.activation(ap(out), ap(in_), ACT.Copy, scale=scale), [in_], [out], max(SMIN, size(out)))
         else:
-            op("s", lambda: S.activation(ap(out), ap(in_), ACT.Identity, bias=ap(bias), scale=scale), [in_, bias], [out], max(SMIN, size(out)))
+            op("s", lambda: act(out, ap(in_), scale, bias), [in_] + views(scale, bias), [out], max(SMIN, size(out)))
 
     def fill(v, x):
         copy("s", v, cols("ones", 0, size(v)), scale=x)
 
-    def gather(q, out, win, off, scale=1.0):
-        cycles = 70 + GATHER * size(out)
+    def gather(q, out, win, off, scale=1.0, bias=None):
+        reads, cycles = [win, off] + views(scale, bias), 70 + GATHER * size(out)
         if q == "s":
-            op("s", lambda: S.activation(ap(out), ap(win).indirect(ap(off)), ACT.Copy, scale=scale), [win, off], [out], cycles)
+            op("s", lambda: act(out, ap(win).indirect(ap(off)), scale, bias), reads, [out], cycles)
         elif scale == 1.0:
-            op("v", lambda: V.tensor_copy(ap(out), ap(win).indirect(ap(off))), [win, off], [out], cycles)
+            op("v", lambda: V.tensor_copy(ap(out), ap(win).indirect(ap(off))), reads, [out], cycles)
         else:
-            op("v", lambda: V.tensor_scalar(ap(out), ap(win).indirect(ap(off)), scale, None, A.mult), [win, off], [out], cycles)
+            op("v", lambda: V.tensor_scalar(ap(out), ap(win).indirect(ap(off)), number(scale), None, A.mult), reads, [out], cycles)
 
-    def brought(name, win, off, out=None, at=0, line=None):
+    def brought(name, win, off, line=None, scale=1.0, bias=None):
         a = 0
         for q, z in SHARE[name]:
-            gather(q, cols(name, a, z), win, part(off, a, z))
+            gather(q, cols(name, a, z), win, part(off, a, z), scale, bias)
             if line and q == "s":
                 in_line(line)
-            turn(cols(out or name + "T", at + a, at + z), cols(name, a, z))
+            turn(cols(name + "T", a, z), cols(name, a, z))
             a = z
 
     def gather_add(out, win, off, other):
-        op("v", lambda: V.tensor_tensor(ap(out), ap(win).indirect(ap(off)), ap(other), A.add), [win, off, other], [out], 60 + GADD * size(out))
-
-    def memset(v, x):
-        op("v", lambda: V.memset(ap(v), x), [], [v], size(v) * narrow(v))
+        op("v", lambda: V.tensor_tensor(ap(out), ap(win).indirect(ap(off)), ap(other), A.add), [win, off, other], [out], 60 + GATHER * size(out))
 
     def iota(v, pattern, base):
         op("g", lambda: g.iota(ap(v), pattern, base, 0, allow_small_or_imprecise_dtypes=True), [], [v], 160 + 2 * size(v))
@@ -471,8 +425,8 @@ def rank_program(g, core, T, topo):
         o, s = cols(out, a, z), cols(scales, a, z)
         op("v", lambda: V.quantize_mx(ap(o), ap(s), ap(in_)), [in_], [o, s], 15 + 1.06 * (z - a))
 
-    def quantize_piece(out, scales, tile, h, cut=CUT):
-        quantize(out, scales, cut[h], cut[h + 1], cols(tile, 4 * cut[h], 4 * cut[h + 1]))
+    def quantize_piece(out, scales, tile, h):
+        quantize(out, scales, CUT[h], CUT[h + 1], cols(tile, 4 * CUT[h], 4 * CUT[h + 1]))
 
     def swapped(buf, a, z, at):
         turn(cols("eb", at + 16, at + 16 + z - a), cols(buf, a, z))
@@ -481,52 +435,46 @@ def rank_program(g, core, T, topo):
     def make_list(out, win, off):
         op("v", lambda: V.tensor_scalar(ap(out), ap(win).indirect(ap(off)), 512.0, 224.0, A.mult, A.add), [win, off], [out], 60 + GATHER * size(out))
 
-    for i in range(3):
-        memset(cols("ti", 32 * i + 28, 32 * i + 32), 0)
-    dmas("s", "ld_t", [(T.ti[:, 32 * i:32 * i + 28], T[k][:], [], [dense("ti", i)]) for i, k in enumerate(("up", "lf", "rt"))], LOCAL + TI)
-    dmas("y", "ld_u", [(T.ut[:], T.u[:], [], [cols("ut", 0, 512)])], LOCAL + 0.4)
-    in_line("loads")
-    for h in range(3):
-        v = cols("xt", 4 * CUT[h], 4 * CUT[h + 1])
-        dmas("y", "ld_x%d" % h, [(ap(v), T.x[:, v[1]:v[2]], [], [v])], LOCAL + 0.8 + 0.35 * h)
-        in_line("loads")
+    for what, qq, late in LOADS:
+        if what == "t":
+            dmas(qq, "ld_t", [(T.ti[:, 32 * i:32 * i + 28], T[k][:], [], [dense("ti", i)]) for i, k in enumerate(("up", "lf", "rt"))], LOCAL + late)
+        elif what == "u":
+            dmas(qq, "ld_u", [(T.ut[:], T.u[:], [], [cols("ut", 0, 512)])], LOCAL + late)
+        else:
+            v = cols("xt", 4 * CUT[what], 4 * CUT[what + 1])
+            dmas(qq, "ld_x%d" % what, [(ap(v), T.x[:, v[1]:v[2]], [], [v])], LOCAL + late)
+        in_line("loads" + qq)
     dmas("y", "ld_w", [(T.wq[:, 0:512].bitcast(dt.uint8), T.wc[:], [v], [cols("wq", 0, 512)]),
                        (T.wp[:, 0:512], T.ws[:], [], [cols("wp", 0, 512)])], LOCAL + 1.5)
 
-    ones = cols("ones", 0, 512)
-    memset(ones, 1.0)
-    in_line("start")
+    op("v", lambda: V.memset(T.ones[:, 0:512], 1.0), [], [cols("ones", 0, 512)], 256)
     op("g", lambda: g.iota(T.pidx[:, 0:2], [[0, 2]], 0, 1), [], [cols("pidx", 0, 2)], 160)
+    for i in (1, 2):
+        op("g", lambda i=i: g.iota(T.ti[:, 32 * i + 28:32 * i + 32], [[0, 4]], 0, 0), [], [cols("ti", 32 * i + 28, 32 * i + 32)], 170)
     iota(cols("i16", 0, 28), [[16, 28]], 0)
+    iota(cols("lane", 0, 16), [[1, 16]], 0)
     iota(cols("i32", 0, 28), [[32, 14], [0, 2]], -224)
-    in_line("first")
-    memset(cols("et", 0, 516), 0.0)
-    in_line("start")
+    iota(col(8), [[0, 1]], 224)
+    iota(("ne", 3, 336, 4), [[0, 84]], 8)
+    fill(cols("et", 0, 258), 0.0)
+    fill(cols("et", 258, 516), 0.0)
     op("g", lambda: g.affine_select(T.et[:, 3:515:4], T.ones[:, 0:128], [[-1, 128]], A.is_equal, 0.0, 0, 1),
        [cols("ones", 0, 128)], [("et", 3, 515, 4)], 460)
-    in_line("first")
-    memset(cols("eb"), 0.0)
-    for v in (cols("wu", 0, 480), cols("wr"), cols("wt"), cols("wq_", 0, 464), cols("dc", 0, 128), cols("repT", C, 512),
-              cols("sc", C, 952), cols("sx", 0, 224), cols("dd", 28, 32)):
+    for v in (cols("eb", 0, 464), cols("wt"), cols("wq_", 0, 512), cols("dc", 0, 128), cols("dw", 0, 128), cols("sc", 0, 224), cols("sc", C, 952),
+              cols("fin", 0, 336), cols("dd", 0, 336), cols("dd", 336, 672), cols("da1", 112, 128)):
         fill(v, 0.0)
-    for v in (cols("di", 96, 128), cols("dt", 0, 256), cols("da1", 112, 128)):
-        memset(v, 0.0)
-    memset(cols("srow", C, 456), -BIGV)
-    for v, x in ((cols("qx", C, WIDE), -3), (col(8), 224), (("ne", 3, 336, 4), 8)):
-        iota(v, [[0, size(v)]], x)
-        in_line("first")
-    iota(cols("sc", 0, 56), [[0, 28], [3, 2]], 0)
-    in_line("first")
-    fill(cols("rrep", C, 464), NONE)
+    for v in (cols("di", 0, 160), cols("dt", 0, 160), cols("dr", 112, 128), cols("da0", 112, 128)):
+        op("v", lambda v=v: V.memset(ap(v), 0.0), [], [v], size(v) / 2)
+    fill(cols("qw", 2 * C, 2 * C + 264), -3.0)
+    fill(cols("qw", 2 * C + 264, C + WIDE), -3.0)
     fill(cols("mc", 0, 336), -BIGV)
-    fill(("wu", C + 4, 480, 4), BIGV)
-    for lane, x in ((0, -BIGV), (1, 8.0), (2, 8.0), (12, -1.0e-30)):
-        fill(plane("wu", lane, 480), x)
-    turn(cols("urow", C, 480), cols("wu", C, 480))
+    fill(cols("st"), 2 * HUGE)
+    for v, x in ((lanes("st", 2), -BIGV), (plane("st", 4), -BIGV), (plane("st", 8), -BIGV), (plane("st", 1), 10 * HUGE), (("w0", 0, 112, 4), 8.0), (col(29), 2 * HUGE)):
+        op("g", lambda v=v, x=x: g.affine_select(ap(v), ap(cols("ones", 0, size(v))), [[0, size(v)]], A.is_gt, x, 0, 0), [cols("ones", 0, size(v))], [v], 200 + 2 * size(v))
     for i, (sh, m) in enumerate(((0, 1), (4, 1), (0, 15), (0, 31))):
         ts(cols("pidx", 2 + i, 3 + i), cols("pidx", 0, 1), sh, A.logical_shift_right, m, A.bitwise_and)
     copy("v", cols("col", 0, 4), cols("pidx", 2, 6))
-    jt = ts(cols("jt", 0, 28), ts(val("i1"), cols("i16", 0, 28), col(2), A.add, -448.0, A.add), UNIT, A.mult)
+    ts(slot(0, 3), ts(val("i1"), cols("i16", 0, 28), col(2), A.add, -448.0, A.add), UNIT, A.mult)
     nv = ts(cols("nn", 0, 28), cols("i32", 0, 28), col(3), A.add, UNIT, A.mult)
     tt(col(4), col(0), col(1), A.not_equal)
     ts(col(5), col(1), -30.0, A.mult, 159.0, A.add)
@@ -536,71 +484,64 @@ def rank_program(g, core, T, topo):
     ts(col(11), col(2), 4.0, A.mult, 3.0, A.add)
     ts(col(12), col(4), col(13), A.mult, col(11), A.add)
     ts(cols("offa", 0, 2), cols("i16", 0, 2), 4.0, A.mult, col(12), A.add)
-    copy("s", ("sx", 57, 112, 2), nv)
-    copy("s", plane("wu", 14), nv)
+    ts(cols("lane", 0, 16), cols("lane", 0, 16), col(2), A.is_equal)
 
+    def on(i):
+        return "lane", i, i + 1, 1
+    B1, B2, SD, BD = [col(16 + i) for i in range(4)]
+    S1, S2 = on(16 + 4), on(16 + 8)
+    copy("s", cols("lane", 16, 32), cols("lane", 0, 16), scale=-1.0)
+    copy("s", cols("lane", 32, 48), cols("lane", 0, 16), scale=BIGV)
+    copy("s", B1, ts(col(22), on(0), on(12), A.add, col(0), A.add), scale=-2 * HUGE)
+    copy("s", col(23), on(0), scale=-BIGV)
+    copy("s", B2, on(12), scale=-1.0e-30, bias=col(23))
+    copy("s", col(27), col(0), scale=-1.0, bias=cols("ones", 0, 1))
+    copy("s", SD, col(0), scale=1 / HUGE, bias=col(27))
+    copy("s", BD, col(0), scale=-2.0)
+    copy("s", cols("w1", C, 456), cols("ones", 0, 8), scale=on(32 + 4), bias=B1)
+    copy("s", cols("w2", C, 456), cols("ones", 0, 8), scale=on(32 + 8), bias=B2)
+    copy("s", col(28), on(1), scale=8 * HUGE, bias=on(32 + 4))
+    copy("s", cols("urow", C, 456), cols("w2", C, 456), bias=col(28))
+    copy("v", cols("offu", 0, 8), cols("i16", 0, 8))
+    copy("s", ("w0", 3, 112, 4), nv)
     for b in range(4):
         quantize("eq", "es", 128 * b, 128 * b + 128, cols("et", 3 - b, 515 - b))
         in_line("start")
-    quantize("uq", "us", 0, 128, cols("ut", 0, 512))
+
+    quantize("u0", "s0", 0, 128, cols("ut", 0, 512))
     in_line("start")
+    offu = cols("offu", 0, 8)
+    op("v", lambda: V.tensor_copy(T.uq[:, 0:128].bitcast(dt.uint32), T.u0[:, 0:128].bitcast(dt.uint32).indirect(ap(offu))),
+       [cols("u0", 0, 128), offu], [cols("uq", 0, 128)], 70 + GATHER * 128)
+    op("s", lambda: S.activation(T.us[:, 0:128], T.s0[:, 0:128].indirect(ap(offu)), ACT.Copy), [cols("s0", 0, 128), offu], [cols("us", 0, 128)], 70 + GATHER * 128)
     for h in range(3):
         quantize_piece("q0", "qs0", "xt", h)
-    ts(cols("di", 0, 96), cols("ti", 0, 96), -224.0, A.add, UNIT, A.mult)
+    ts(cols("di", 32, 96), cols("ti", 32, 96), -224.0, A.add, UNIT, A.mult)
     copy("v", cols("lb", 0, 64), cols("ti", 32, 96))
-    e = ts(val("i0"), dense("ti", 0), 448.0, A.is_equal)
-    e = tt(val("i2"), e, jt, A.mult)
-    tt(dense("di", 0), dense("di", 0), e, A.add)
-    ts(cols("la0", 0, 32), cols("di", 0, 32), 512.0, A.mult, 224.0, A.add)
-    swapped("di", 0, 96, 0)
+    swapped("di", 32, 96, 176)
     lv, rv = dense("dt", 1), dense("dt", 2)
     gather("v", cols("dt", 32, 96), cols("di", 0, 256), cols("offm", 2, 6))
-    memset(cols("da0", 112, 128), 0.0)
-    gather("s", ("da0", 3, 128, 4), cols("di", 0, 256), cols("offm", 0, 2))
+    ts(slot(1, 2), dense("ti", 0), 448.0, A.is_equal)
+    ts(slot(1, 3), dense("ti", 0), -224.0, A.add, UNIT, A.mult)
+    scan(cols("dr", 0, 112), four(0), four(1))
+    ts(cols("la0", 0, 28), ("dr", 3, 112, 4), 512.0, A.mult, 224.0, A.add)
+    swapped("dr", 0, 128, 0)
+    gather("s", ("da0", 3, 128, 4), cols("dr", 0, 288), cols("offa", 0, 2))
 
-    def first_of(i, buf, own, order, first, out):
-        if MSCAN:
-            scan(four(i, "mo"), lanes(buf, 0), four(i, "mc"), A.min, A.max)
-            least = slot(i, 3, "mo")
-            if i < 2:
-                copy("v", slot(i + 1, 0, "mc"), least)
-        elif i == 1:
+    def first_of(i, buf, own, order, steps, out):
+        if i == 1:
             least = tt(slot(1, 0, "mc"), tt(val("m1"), own, plane(buf, 4), A.min), plane(buf, 8), A.min)
         else:
             scan(four(i // 2, "mo"), lanes(buf, 0), four(i // 2, "mc"), A.min, A.max)
             least = slot(i // 2, 3, "mo")
         for j, v in zip(order, (own, plane(buf, 4), plane(buf, 8))):
             tt(slot(i, j, "ne"), v, least, A.not_equal)
-        scan(out, lanes(buf, first), four(i, "ne"), A.add, A.min)
+        scan(out, steps, four(i, "ne"), A.add, A.min)
 
-    LB, LO, LC, LW = 12, 10, 1, 5
-    LP, LL, LR = range(3)
+    LB, LO, LI, LF = 12, 10, 3, 7
+    from_inner, apart, inner, B = val("pc"), ("w0", 1, 112, 4), plane("wq_", LI), plane("wq_", LB)
     ll, lr, lc, laa = cols("lb", 0, 28), cols("lb", 32, 60), cols("lc", 0, 28), cols("lc", 32, 60)
-    srow, urow, rrep = cols("srow", 0, 456), cols("urow", 0, 456), cols("rrep", 0, 464)
-
-    def grandparents(pv, la, line=None):
-        tt(("sc", 897, 952, 2), nv, pv, A.subtract)
-        copy(SMALL[-1], plane("wt", LP), pv)
-        halves("trow", "wt")
-        brought("pp", cols("trow"), la, line=line)
-        ppv = plane("ppT", LP)
-        copy(SMALL[1], dense("dc", 1), ppv)
-        up = tt(("sc", 953, 1008, 2), ppv, pv, A.subtract)
-        ts(("sc", 952, 1008, 2), up, 0.0, A.is_equal)
-        scan(("sc", 449, 560, 2), cols("sc", 896, 952), cols("sc", 952, 1008))
-
-    def unpack(aq, as_):
-        for b in FORDER:
-            mm(FBANK[b], "eq", "es", b, aq, as_)
-            copy("s", cols("fp%d" % b), ps(FBANK[b]))
-            if EARLY:
-                in_line("gap")
-            if KV[b]:
-                fp, fq = cols("fp%d" % b, 0, KV[b]), cols("fq", C * b, C * b + KV[b])
-                if TWIN[b] == "s":
-                    copy("s", fq, ps(FBANK[b], KV[b]))
-                else:
-                    dmas("y", "cf%d" % b, [(ap(fq), ap(fp), [fp], [fq])], LOCAL + 0.6)
+    urow = cols("urow", 0, 456)
 
     for k in range(3):
         last = k == 2
@@ -608,134 +549,140 @@ def rank_program(g, core, T, topo):
         dst = T.cores[(rank + STEP[k]) % N]
         la, la2 = cols("la%d" % k, 0, 28), cols("la%d" % (k + 1), 0, 28)
         pv, da = ("da%d" % (k % 2), 3, 112, 4), "da%d" % (1 - k % 2)
-        def leave(more):
-            if RELAY:
-                record("g", lambda k=k, q=q: write(T["hq%d" % k][:, 0:RELAY].bitcast(dt.uint8), T[q][:, 0:RELAY].bitcast(dt.uint8), helper(core), "hop%d" % k, inward(core)),
-                       "sent", engines(inward(core)), 0.1, 0.1, [cols(q, 0, RELAY)], [])
-                for v in more:
-                    calls[-1]["after"][uses[v[0]][0][1]] = True
-                in_line("twins")
-            exchange(dst, "arq%d" % k, [(T[aq][:, RELAY:C].bitcast(dt.uint8), T[q][:, RELAY:C].bitcast(dt.uint8), cols(q, RELAY, C)),
-                                        (T[as_][:, 0:C], T[qs][:, 0:C], cols(qs))], [cols(aq), cols(as_)], LONG - (DELAY if more else 0),
-                     engines(topo.mask(helper(core), dst)) if RELAY else 0)
-        if k == 0:
-            leave([])
-        apart = tt(plane("wu", 9), lv, rv, A.subtract)
-        tt(plane("wu", 10), rv, nv, A.subtract)
-        for out, in_ in ((plane("wu", 3), lv), (plane("wu", 13), rv), (plane("wu", 6), apart), (plane("wq_", LC), lv)):
-            copy(SMALL[0] if k else "v", out, in_)
-            if SMALL[0] == "g" and k:
-                in_line("twins")
-        if k == 0 or not EARLY:
-            grandparents(pv, la)
-        if k:
-            leave([])
-        for h, bank in enumerate((0, 7, 5)):
+        side, side2 = val("side%d" % (k % 2)), val("side%d" % (1 - k % 2))
+        tt(apart, lv, rv, A.subtract)
+        tt(("w0", 2, 112, 4), rv, nv, A.subtract)
+        tt(("sc", 897, 952, 2), nv, pv, A.subtract)
+        copy("g", ("sc", 786, 868, 3), pv)
+        copy("g", plane("wq_", LF), pv)
+        for lane, v in ((3, lv), (13, rv), (9, apart), (7, pv)):
+            if k == 0 and lane != 9:
+                win, off = (cols("dr", 0, 288), cols("offa", 0, 2)) if lane == 7 else (cols("di", 0, 256), cols("offm", 2 if lane == 3 else 4, 4 if lane == 3 else 6))
+                gather("s", ("st", lane, 512, 16), win, off, HUGE, col(29))
+            elif CODED == "s" and k:
+                copy("s", plane("st", lane), v, scale=HUGE, bias=col(29))
+            else:
+                ts(plane("st", lane), v, 2.0, A.add, HUGE, A.mult)
+        for a in (0, C // 2):
+            turn(cols("srow", a, a + C // 2), cols("st", a, a + C // 2))
+        exchange(dst, "arq%d" % k, [(T[aq][:, 0:C].bitcast(dt.uint8), T[q][:, 0:C].bitcast(dt.uint8), cols(q)),
+                                    (T[as_][:, 0:C], T[qs][:, 0:C], cols(qs))], [cols(aq), cols(as_)], LONG + (FIRST if k == 0 else 0))
+        for h, (bank, other) in enumerate(((0, 6), (7, 1), (5, 2))):
+            n = CUT[h + 1] - CUT[h]
+            mm(other, "uq", "us", 0, q, qs, CUT[h], CUT[h + 1])
+            in_line("layer")
+            copy("s", piece("w1", h), ps(other, n), scale=S1, bias=B1)
             mm(bank, "uq", "us", 0, q, qs, CUT[h], CUT[h + 1])
             in_line("layer")
-            copy(SQ[h], piece("srow", h), ps(bank, CUT[h + 1] - CUT[h]))
-            turn(piece("sT", h), ps(bank, CUT[h + 1] - CUT[h]) if TPS else piece("srow", h))
-        for b in range(4):
-            mm(1 + b, "eq", "es", b, q, qs)
-        brought("sl", srow, ll)
-        brought("sr", srow, lr)
-        brought("sa", srow, la)
-        if DELAY:
-            leave([cols("slT", 0, 224)])
-        s0 = plane("sT", 0)
-        if VCUT:
-            for a, z in ((0, VCUT), (VCUT, C)):
-                tt(("wu", a + 4, z, 16), ("sT", a, z, 16), ("slT", a, z, 16), A.subtract)
-                tt(("wu", a + 8, z, 16), ("sT", a, z, 16), ("srT", a, z, 16), A.subtract)
-                turn(cols("urow", a, z), cols("wu", a, z))
+            tt(piece("mrow", h), piece("srow", h), ps(bank, n), A.max)
+        if WHOLE:
+            mm(3, "uq", "us", 0, q, qs)
+            copy("s", cols("w2"), ps(3), scale=S2, bias=B2)
         else:
-            tt(plane("wu", 4), s0, plane("slT", 0), A.subtract)
-            tt(plane("wu", 8), s0, plane("srT", 0), A.subtract)
-            halves("urow", "wu")
-        brought("ul", urow, ll)
-        brought("ur", urow, lr)
+            for h, other in enumerate((6, 1, 2)):
+                copy("s", piece("w2", h), ps(other, CUT[h + 1] - CUT[h]), scale=S2, bias=B2)
+        for b in (3, 2, 0, 1):
+            mm(1 + b, "eq", "es", b, q, qs)
+        for a, z in zip(LCUT, LCUT[1:]):
+            gather_add(cols("lrow", a, z), cols("w1", 0, 456), part(ll, a, z), cols("mrow", a, z))
+        for a, z in zip(RCUT, RCUT[1:]):
+            gather_add(cols("urow", a, z), cols("w2", 0, 456), part(lr, a, z), cols("lrow", a, z))
+            turn(cols("gT", a, z), cols("urow", a, z))
+        brought("sa", cols("mrow"), la, scale=SD, bias=BD)
+        brought("ul", urow, ll, scale=SD)
+        brought("ur", urow, lr, scale=SD)
         for b in range(4):
             if XV[b]:
                 copy("s", cols("fo%d" % b, 0, XV[b]), ps(1 + b, XV[b]))
-        v0 = tt(slot(0, 0, "mc"), plane("saT", 0), s0, A.subtract)
-        first_of(0, "wu", v0, (2, 0, 1), 2, four(0, "so"))
+        ppv = plane("saT", 7)
+        copy("g", dense("dc", 1), ppv)
+        up = tt(("sc", 953, 1008, 2), ppv, pv, A.subtract)
+        ts(("sc", 952, 1008, 2), up, 0.0, A.is_equal)
+        scan(("sc", 449, 560, 2), cols("sc", 896, 952), cols("sc", 952, 1008))
+        if k == 0:
+            tt(side, plane("saT", 3), nv, A.not_equal)
+        tt(inner, rv, tt(val("d6"), side, apart, A.mult), A.add)
+        tt(from_inner, pv, inner, A.subtract)
+        v0 = tt(slot(0, 0, "mc"), plane("saT", 2), plane("gT", 2), A.subtract)
+        first_of(0, "gT", v0, (2, 0, 1), cols("w0", 0, 112), four(0, "so"))
         child = tt(dense("dc", 0), slot(0, 1, "so"), rv, A.add)
-        tt(plane("wq_", LW + LB - LO), slot(0, 1, "so"), apart, A.is_equal)
         swapped("dc", 0, 64, 288)
         make_list(cols("lc", 0, 64), cols("dc", 0, 224), cols("offm", 0, 4))
         tt(plane("ulT", 5), slot(0, 3, "so"), plane("ulT", 3), A.subtract)
-        first_of(1, "ulT", slot(0, 3, "mo"), (0, 1, 2), 1, four(1, "so"))
+        first_of(1, "ulT", slot(0, 3, "mo"), (0, 1, 2), lanes("ulT", 1), four(1, "so"))
         tt(plane("urT", 5), slot(1, 3, "so"), plane("urT", 3), A.subtract)
-        first_of(2, "urT", slot(1, 3, "mo") if MSCAN else slot(1, 0, "mc"), (0, 1, 2), 1, lanes("wq_", 0))
-        B = plane("wq_", LB)
-        turn(cols("qx"), cols("wq_"))
-        if MERGE:
-            turn(cols("qy"), cols("wq_", LB - LO, C + LB - LO))
-            gather_add(cols("qw"), cols("qx"), la, cols("qy"))
-            turn(cols("qwT"), cols("qw"))
-            brought("qc", cols("qx", 0, WIDE), lc)
-            brought("g2", cols("qw"), laa)
-            b1, b2, b3, b4 = plane("qwT", LB), plane("g2T", LO), plane("g2T", LB), plane("g2T", LW)
-        else:
-            brought("qw", cols("qx"), la)
-            brought("qc", cols("qx", 0, WIDE), lc)
-            brought("qy", cols("qx"), laa)
-            brought("g2", cols("qw"), laa)
-            b1, b2, b3, b4 = plane("qwT", LB), plane("qyT", LB), plane("g2T", LB), plane("qyT", LW + LB - LO)
-        e01 = tt(slot(6, 1), B, b1, A.is_equal)
+        first_of(2, "urT", slot(1, 0, "mc"), (0, 1, 2), lanes("urT", 1), lanes("wq_", 0))
+        turn(cols("qw", C, 2 * C), cols("wq_"))
+        turn(cols("qy"), cols("wq_", LB - LO, C + LB - LO))
+        turn(cols("eb", 400, 432), ("wq_", LB, 512, 16))
+        copy("g", dense("dw", 0), B)
+        turn(cols("dw", 128, 192), cols("eb", 384, 448))
+        make_list(cols("lw", 0, 32), cols("dw", 0, 192), cols("offm", 0, 2))
+        gather_add(cols("qw"), cols("qw", C, 2 * C), la, cols("qy"))
+        turn(cols("qwT"), cols("qw"))
+        brought("qc", cols("qw", C, C + WIDE), lc)
+        brought("g2", cols("qw"), laa, line="gap")
+
+        def unpack(b):
+            mm(FBANK[b], "eq", "es", b, aq, as_)
+            copy("s", cols("fp%d" % b), ps(FBANK[b]))
+            in_line("gap")
+            if KV[b]:
+                fp, fq = cols("fp%d" % b, 0, KV[b]), cols("fq", C * b, C * b + KV[b])
+                if TWINS[b] == "y":
+                    dmas("y", "cf%d" % b, [(ap(fq), ap(fp), [fp], [fq])], TWIN)
+                else:
+                    copy(TWINS[b], fq, fp if TWINS[b] == "g" else ps(FBANK[b], KV[b]))
+                    in_line("writes" if TWINS[b] == "g" else "gap")
+        for b in FSOON:
+            unpack(b)
+        b1, b2, b3 = plane("qwT", LB), plane("g2T", LO), plane("g2T", LB)
+        e01 = tt(("sc", 673, 756, 3), B, b1, A.is_equal)
         e12 = tt(slot(4, 2), b1, b2, A.is_equal)
         tt(slot(4, 1), b2, b3, A.is_equal)
-        tt(slot(7, 0), B, child, A.is_equal)
-        tt(slot(6, 2), plane("qcT", LB), child, A.is_equal)
-        tt(slot(6, 3), B, pv, A.subtract)
-        scan(four(2, "so"), four(6), four(7))
-        tt(slot(5, 3), slot(2, 3, "so"), pv, A.add)
-        r1 = tt(slot(5, 1), tt(val("x0"), B, nv, A.is_equal), e01, A.mult)
-        side = tt(("sc", 57, 112, 2), plane("qwT", LC), nv, A.not_equal)
-        tt(("sc", 56, 112, 2), b1, pv, A.not_equal)
-        scan(cols("sc", 112, 168), cols("sc", 0, 56), cols("sc", 56, 112))
-        tt(slot(5, 0), b4, ("sc", 113, 168, 2), A.is_equal)
-        inner = tt(val("in"), rv, tt(val("d6"), side, apart, A.mult), A.add)
-        tt(("sx", 1, 56, 2), inner, nv, A.subtract)
-        from_inner = tt(val("pc"), pv, inner, A.subtract)
-        scan(cols(da, 0, 112), four(4), four(5))
+        tt(("sc", 784, 868, 3), tt(val("c1"), B, child, A.is_equal), tt(val("c2"), plane("qcT", LB), child, A.is_equal), A.mult)
+        tt(("sc", 674, 756, 3), B, pv, A.subtract)
+        scan(("fin", 1, 336, 4), cols("sc", 672, 756), cols("sc", 784, 868))
+        sinks = ("fin", 5, 336, 12)
+        r1 = tt(("fin", 3, 336, 12), tt(val("x0"), B, nv, A.is_equal), e01, A.mult)
+        within = tt(val("w2"), plane("qwT", LI), nv, A.is_equal)
+        tt(("fin", 0, 336, 12), tt(val("w1"), b1, pv, A.is_equal), within, A.mult)
+        scan(cols(da, 0, 112), four(4), ("fin", 0, 336, 3))
         swapped(da, 0, 128, 0)
         make_list(cols(la2[0], 0, 32), cols(da, 0, 288), cols("offa", 0, 2))
         exchange(dst, "arl%d" % k, [(ap(al), ap(la2), la2)], [al], SHORT)
-        rot = tt(("sx", 56, 112, 2), r1, e12, A.mult)
-        scan(("so", 225, 336, 2), cols("sx", 0, 56), cols("sx", 56, 112))
-        tt(("sx", 115, 224, 4), B, nv, A.subtract)
-        scan(lanes("wr", 0), cols("sx", 112, 224), four(2, "so"))
-        turn(cols("rrep"), cols("wr"))
-        if EARLY:
-            unpack(aq, as_)
-        if EARLY == 1 and not last:
-            grandparents((da, 3, 112, 4), la2, "gap")
-        brought("repl", rrep, ll, "repT", line="gap" if EARLY else None)
-        brought("repr_", rrep, lr, "repT", 512, line="gap" if EARLY else None)
-        if EARLY == 2 and not last:
-            grandparents((da, 3, 112, 4), la2, "gap")
-        if EARLY == 3 and not last:
-            grandparents((da, 3, 112, 4), la2)
-        rp = tt(val("rp"), rot, from_inner, A.mult)
-        tt(dense("dd", 1), rp, tt(dense("dd", 0), rp, side, A.mult), A.subtract)
-        tt(cols("dt", 32, 92), ("repT", 12, 512 + C, 16), cols("dd", 0, 60), A.add)
+        brought("qz", cols("qw", 0, WIDE), cols("lw", 0, 28), line="gap")
+        left = tt(val("s4"), side, tt(val("s2"), sinks, tt(val("s1"), B, inner, A.not_equal), A.mult), A.not_equal)
+        tt(("fin", 11, 336, 12), tt(val("rot"), r1, e12, A.mult), from_inner, A.mult)
+        tt(("dd", 1, 56, 2), plane("qcT", LI), B, A.subtract)
+        scan(cols("dd", 56, 112), cols("dd", 0, 56), ("fin", 5, 336, 6))
+        D = ("dd", 57, 112, 2)
+        tt(("dd", 169, 224, 2), D, tt(("dd", 113, 168, 2), D, left, A.mult), A.subtract)
+        above = plane("qzT", LF - LB + LO)
+        tt(("dd", 336, 420, 3), B, above, A.subtract)
+        tt(("dd", 421, 504, 3), plane("qzT", LO), B, A.is_equal)
+        tt(("dd", 422, 504, 3), plane("qzT", LB), B, A.is_equal)
+        scan(("dd", 504, 672, 2), cols("dd", 420, 504), cols("dd", 336, 420))
+        for i, v in enumerate((lv, rv)):
+            tt(("dd", 112 + 56 * i, 168 + 56 * i, 2), above, v, A.is_equal)
+            scan(cols("dd", 224 + 56 * i, 280 + 56 * i), ("dd", 505, 672, 3), cols("dd", 112 + 56 * i, 168 + 56 * i))
+            tt(v, v, ("dd", 225 + 56 * i, 280 + 56 * i, 2), A.add)
         if last:
             pv = (da, 3, 112, 4)
             e = tt(val("f0"), pv, nv, A.is_equal)
             e = tt(val("f2"), e, ts(val("f1"), nv, -1.0, A.mult, NONE, A.add), A.mult)
-            tt(plane("wt", LP), pv, e, A.add)
-            copy("s", plane("wt", LL), lv)
-            copy("s", plane("wt", LR), rv)
+            tt(plane("wt", 0), pv, e, A.add)
+            copy("g", plane("wt", 1), lv)
+            copy("g", plane("wt", 2), rv)
             turn(cols("trow"), cols("wt"))
             copy("s", cols("trf"), cols("trow"), scale=512.0, bias=col(8))
             dmas("y", "st_tr", [(T.tr[:, C * i:C * i + C], T.trf[i:128:16, :], [cols("trf")], []) for i in range(3)])
         else:
+            tt(side2, left, tt(val("s3"), (da, 2, 112, 4), within, A.mult), A.not_equal)
             swapped("dt", 32, 96, 176)
             make_list(cols("lb", 0, 64), cols("dt", 0, 256), cols("offm", 2, 6))
-        fbank = FBANK
-        if not EARLY:
-            unpack(aq, as_)
+        for b in FLATE:
+            unpack(b)
         kb = [cols("kb", C * b, C * b + C) for b in range(4)]
         for b in (0, 1, 3, 2):
             x = KV[b]
@@ -744,9 +691,8 @@ def rank_program(g, core, T, topo):
                 in_line("sums")
             if x < C:
                 gather("s", cols("kg%d" % b, x, C), cols("fp%d" % b), part(al, x, C))
-                if EARLY:
-                    in_line("gap")
-                tt(cols("kb", C * b + x, C * b + C), cols("kg%d" % b, x, C), ps(fbank[b], C - x, x), A.add)
+                in_line("gap")
+                tt(cols("kb", C * b + x, C * b + C), cols("kg%d" % b, x, C), ps(FBANK[b], C - x, x), A.add)
                 in_line("sums")
         if k == 0:
             dmas("y", "ld_v", [(T.vt[:], T.v[:], [cols("kb", 0, 1)], [cols("vt", 0, 512)])])
@@ -760,40 +706,38 @@ def rank_program(g, core, T, topo):
             mm(bank, "wq", "wp", 0, "zq", "zs", CUT[h], CUT[h + 1])
             in_line("layer")
             copy(RQ[h], piece("rr0", h), ps(bank, CUT[h + 1] - CUT[h]), scale=0.03125)
-            if h == 1 and SOON:
+            if h == 1:
                 mm(2, "wq", "wp", RORDER[0], "zq", "zs", 0, CUT[2])
                 in_line("layer")
                 copy("s", cols("rr%d" % RORDER[0], 0, CUT[2]), ps(2, CUT[2]), scale=0.03125)
                 in_line("state")
-        banks = [6, 7, 1, 5, 0] if SOON else [2, 6, 7, 1, 5, 0]
-        for b in RORDER:
-            for (a, z), qq in zip([(CUT[2], C)] if SOON and b == RORDER[0] else zip(RCUT, RCUT[1:]), RQ2[b]):
-                bank = banks.pop(0)
-                mm(bank, "wq", "wp", b, "zq", "zs", a, z)
-                in_line("layer")
-                copy(qq, cols("rr%d" % b, a, z), ps(bank, z - a), scale=0.03125)
-                if qq == "s" and STATE:
-                    in_line("state")
-        apiece = last and LAST
+        for b, bank in zip(RORDER, (6, 7, 1)):
+            a = CUT[2] if b == RORDER[0] else 0
+            mm(bank, "wq", "wp", b, "zq", "zs", a, C)
+            in_line("layer")
+            copy(RQ2[b], cols("rr%d" % b, a, C), ps(bank, C - a), scale=0.03125)
+            if RQ2[b] == "s":
+                in_line("state")
         steps = []
-        for b in range(4):
-            cut = sorted({0, XV[b], C} | (set(CUT) if apiece and b >= 2 else set(CUT_X) if XV[b] < C else set()))
-            steps += [(a if apiece else 0, z > XV[b], b, a, z) for a, z in zip(cut, cut[1:])]
-            if XV[b] < C and not apiece:
+        for b in (0,) + RORDER:
+            cut = sorted({0, XV[b], C} | (set(CUT) if last and b >= 2 or XV[b] < C else set()))
+            steps += [(a if last else 0, z > XV[b], b, a, z) for a, z in zip(cut, cut[1:])]
+            if XV[b] < C and not last:
                 gather("s", cols("xg%d" % b, XV[b], C), cols("rr%d" % b), part(la2, XV[b], C))
                 in_line("state")
-        steps += [(CUT[h + 1] + (h < 2) if apiece else C, 2, h, 0, 0) for h in range(3)]
+        steps += [(CUT[h + 1] + (h < 2) if last else C, 2, h, 0, 0) for h in range(3)]
         for _, how, b, a, z in sorted(steps, key=lambda s: s[:2] + (((0,) + RORDER).index(s[2]) if s[1] < 2 else s[2],) + s[3:]):
             if how == 2:
                 quantize_piece("q%d" % (k + 1), "qs%d" % (k + 1), "xn", b)
             elif how:
-                if apiece:
+                if last:
                     gather("s", cols("xg%d" % b, a, z), cols("rr%d" % b), part(la2, a, z))
                     in_line("state")
                 tt(("xn", 4 * a + b, 4 * z, 4), cols("xg%d" % b, a, z), ps(1 + b, z - a, a), A.add)
             else:
                 gather_add(("xn", 4 * a + b, 4 * z, 4), cols("rr%d" % b), part(la2, a, z), cols("fo%d" % b, a, z))
-            in_line("turns")
+            if last or not how:
+                in_line("turns")
 
     quantize("vq", "vs", 0, 128, cols("vt", 0, 512))
     for h in range(3):

from concourse.mybir import dt, AluOpType, ActivationFunctionType

N = 4
C = 448
STEP = [1, 2, 3]
BIGV = 3.0e29
UNIT = 1.0 / 512
NONE = 224 * UNIT
HUGE = 2.0 ** 72
WIDE = 976
CUT = [0, 192, 320, C]
LCUT, RCUT = [0, 224, C], [0, 224, C]
SHARE = {"sa": [("s", C)], "ul": [("s", 224), ("s", C)], "ur": [("s", 256), ("s", C)],
         "qc": [("s", C)], "g2": [("s", 320), ("s", C)], "qz": [("s", C)]}
KV = [C, C, C, 0]
ZSHARE = [[("s", C)], [("s", C)], [("v", 192), ("v", 320), ("s", C)], [("s", C)]]
XV, RORDER = [C, C, 320, 0], (1, 3, 2)
RQ, RQ2 = "svv", "svss"
TWINS = "sgg"
FSOON, FLATE = (), (0, 1, 2, 3)
FBANK = [5, 6, 7, 0]
CODED = "s"
LOADS = [("t", "y", 0.1), ("u", "y", 0.3), (0, "y", 0.7), (1, "y", 1.0), (2, "y", 1.3)]
CYCLE, SAME, CROSS, LOCAL, TWIN, SHORT, LONG, FIRST, ISSUE = 0.001, 0.2, 0.22, 2.0, 2.7, 1.05, 6.5, 0.5, 0.6
GATHER, PRODUCT, SMIN = 1.8, 0.5, 185
CLOCKS = [(0.226, 0.2, 1.0, 1.5, 0.83, 0.9), (0.225, 0.21, 1.2, 1.12, 0.89, 0.75), (0.22, 0.21, 1.7, 1.8, 0.87, 0.8), (0.16, 0.24, 1.5, 1.95, 1.09, 1.0)]
WEIGHTS, LATER = (0.25, 0.35, 0.15, 0.2), (0.0, 0.45, 0.3, 0.2)
PASSES, TRIES, REACH, HEAT, SWEEPS, SPAN, EAGER, SEED = 3, 5000, 6, 0.05, 4, 60, 0.25, 1
AGAIN, HEAD, EARLY = 0, 150, (0.6, 0.55, 0.65, 0.65)
FREE, WHOLE, COOL = ("layer", "start"), False, 0.6
PLAN = {}

F32, BF, U16, I32, CODE, PLANE = "float32", "bfloat16", "uint16", "int32", "float8_e4m3fn_x4", "uint8"
SCRATCH = {"ps": ("psum", [128, 4096], F32)}


def _sbuf(names, n, dtype):
    for k in names.split():
        SCRATCH[k] = ("sbuf", [128, n], dtype)


_sbuf("xt xn zt fq kb", 4 * C, BF)
_sbuf("ut vt ones", 512, BF)
_sbuf("et", 516, BF)
_sbuf("u0 uq vq", 128, CODE)
_sbuf("s0 us vs", 128, PLANE)
_sbuf("wq eq", 512, CODE)
_sbuf("wp es", 512, PLANE)
_sbuf("zq q0 q1 q2 q3 aq0 aq1 aq2", C, CODE)
_sbuf("zs qs0 qs1 qs2 qs3 as0 as1 as2", C, PLANE)
_sbuf("pidx", 8, I32)
_sbuf("col", 32, F32)
_sbuf("lane", 48, F32)
_sbuf("i16 i32 nn", 28, F32)
_sbuf("offm offu", 8, U16)
_sbuf("offa", 2, U16)
_sbuf("ti", 96, I32)
_sbuf("al0 al1 al2", 28, U16)
_sbuf("la0 la1 la2 la3 lw", 32, U16)
_sbuf("lb lc", 64, U16)
_sbuf("di dt dc dw", 256, BF)
_sbuf("da0 da1 dr", 288, BF)
_sbuf("eb wq_", 512, BF)
_sbuf("qw", C + WIDE, BF)
_sbuf("w1 w2 urow", 456, F32)
_sbuf("wt trow qy qc qz g2 qwT qcT qzT g2T kg0 kg1 kg2 kg3", C, BF)
_sbuf("sa ul ur xg2 xg3 srow mrow lrow saT ulT urT gT trf yt rr0 rr1 rr2 rr3", C, F32)
_sbuf("sc", 1024, F32)
_sbuf("w0", 112, F32)
_sbuf("st", 512, F32)
_sbuf("mc mo ne so fin", 3 * 112, F32)
_sbuf("dd", 672, F32)
_sbuf("cb", 28 * 24, F32)
_sbuf("fo0 fo1 fo2 fo3 fp0 fp1 fp2 fp3", C, BF)

SEMAPHORES = (["cv", "cs", "ct", "cg", "sent"] + ["ld_" + k for k in "x0 x1 x2 u v t w".split()]
              + ["st_" + k for k in "y0 y1 y2 oc0 oc1 oc2 sc tr".split()] + ["cf%d" % k for k in range(4)]
              + ["arq%d" % k for k in range(3)] + ["arl%d" % k for k in range(3)])


def rank_program(g, core, T, topo):
    rank = T.rank_of(core)
    if rank is None:
        return
    A = AluOpType
    ACT = ActivationFunctionType
    V, S = g.vector, g.scalar
    queue = {"v": V, "s": S, "t": g.tensor, "g": g, "y": g.sync}

    calls = []
    uses = {}
    masks = {}

    def ap(v):
        return T[v[0]][:, v[1]:v[2]:v[3]] if v[3] > 1 else T[v[0]][:, v[1]:v[2]]

    def columns(v):
        if v[0] == "ps":
            return 1 << (v[1] // 512)
        if v[1:] not in masks:
            masks[v[1:]] = sum(1 << c for c in range(v[1], v[2], v[3]))
        return masks[v[1:]]

    def record(q, issue, sem, inc, holds, takes, reads, writes):
        after = {}
        for v, w in [(v, False) for v in reads] + [(v, True) for v in writes]:
            for m, i, wrote in uses.get(v[0], []):
                if m & columns(v) and (wrote or w or v[0] == "ps"):
                    after[i] = after.get(i, False) or wrote or w or calls[i]["q"] != q
        me = len(calls)
        calls.append(dict(q=q, issue=issue, sem=sem, inc=inc, holds=holds, takes=takes, after=after))
        for v in writes:
            m = columns(v)
            uses[v[0]] = [[u[0] & ~m] + u[1:] for u in uses.get(v[0], []) if u[0] & ~m] + [[m, me, True]]
        for v in reads:
            uses.setdefault(v[0], []).append([columns(v), me, False])

    lines = {}

    def in_line(name):
        if name in lines and name not in FREE:
            calls[-1]["after"].setdefault(lines[name], False)
        lines[name] = len(calls) - 1

    def op(q, fn, reads, writes, cycles):
        t = max(64, cycles) * CYCLE
        record(q, lambda: fn().then_inc(T.sem["c" + q], 1), "c" + q, 1, t, t, reads, writes)
        if any(SCRATCH[v[0]][2] == U16 for v in reads):
            calls[-1]["per"] = size(writes[0])

    def dmas(q, sem, moves, takes=LOCAL):
        def issue():
            for m in moves:
                queue[q].dma_start(m[0], m[1]).then_inc(T.sem[sem], 16)
        record(q, issue, sem, 16 * len(moves), 0.05 * len(moves), takes, sum([m[2] for m in moves], []), sum([m[3] for m in moves], []))

    def exchange(dst, sem, moves, lands, takes):
        rid, pid, se = topo.addr(dst)
        n = len(moves) * len(topo.engines(core, dst))

        def issue():
            for m in moves:
                g.remote_dma(m[0], m[1], T.sem[sem], T.sem["sent"], pid, rid, topo.mask(core, dst))
        mark = (sem, 0, 1, 1)
        record("g", issue, "sent", n, ISSUE * len(moves), ISSUE * len(moves), [m[2] for m in moves], [mark])
        in_line("writes")
        record(None, None, sem, n, 0.0, takes + 0.1 - ISSUE * len(moves), [mark], lands)

    def issue_all():
        def span(i, j):
            if calls[j]["q"] is None:
                return calls[i]["takes"]
            if not calls[j]["after"][i]:
                return calls[i]["holds"]
            return calls[i]["takes"] + (SAME if calls[i]["q"] == calls[j]["q"] else CROSS)
        way = [c["takes"] for c in calls]
        for j in reversed(range(len(calls))):
            for i in calls[j]["after"]:
                way[i] = max(way[i], span(i, j) + way[j])
        before = [[] for c in calls]
        for j, c in enumerate(calls):
            for i in c["after"]:
                before[i].append(j)

        def place(order, back):
            at, taken = {}, {q: [] for q in queue}
            for j in order:
                c = calls[j]
                if back:
                    t = max([at[i] + calls[i]["holds"] + span(j, i) - c["holds"] for i in before[j]] + [c["takes"] - c["holds"]])
                else:
                    t = max([at[i] + span(i, j) for i in c["after"]] + [0.0])
                if c["q"] is not None:
                    for a, b in taken[c["q"]]:
                        if t + c["holds"] <= a + 1e-9:
                            break
                        t = max(t, b)
                    taken[c["q"]] = sorted(taken[c["q"]] + [(t, t + c["holds"])])
                at[j] = t
            return at
        every = range(len(calls))

        def length(at):
            return max(at[j] + calls[j]["takes"] for j in every)
        qs = [c["q"] for c in calls]
        paces = []
        for same, cross, product, rate, pace, moves in CLOCKS + [c[:5] + (m,) for c, m in zip(CLOCKS, EARLY)]:
            factor = [product if c["q"] == "t" else pace if len(c["sem"]) == 2 else moves if c["sem"][2] == "_" else 1.0 for c in calls]
            holds, takes = [[(c[x] + c.get("per", 0) * (rate - GATHER) * CYCLE) * f for c, f in zip(calls, factor)] for x in ("holds", "takes")]
            takes = [t + (LATER[len(paces) % len(CLOCKS)] if c["sem"][:3] == "arl" else 0.0) for c, t in zip(calls, takes)]
            links = [[(i, takes[i] if qs[j] is None else takes[i] + (same if qs[i] == qs[j] else cross) if w else holds[i])
                      for i, w in c["after"].items()] for j, c in enumerate(calls)]
            paces.append((links, holds, takes))

        def clock(order, links, holds, takes):
            at, free, end = [0.0] * len(calls), {}, 0.0
            for j in order:
                t = free.get(qs[j], 0.0)
                for i, d in links[j]:
                    if at[i] + d > t:
                        t = at[i] + d
                if qs[j]:
                    free[qs[j]] = t + holds[j]
                at[j] = t
                end = max(end, t + takes[j])
            return end, at

        def moved(order, a, b, ahead):
            mid = order[a:b + 1]
            group = {mid[-1] if ahead else mid[0]}
            for j in (reversed(mid[:-1]) if ahead else mid[1:]):
                if any(i in group for i in (before[j] if ahead else calls[j]["after"])):
                    group.add(j)
            if mid[0] in group and mid[-1] in group:
                return None
            x, y = [j for j in mid if j in group], [j for j in mid if j not in group]
            return order[:a] + (x + y if ahead else y + x) + order[b + 1:]

        def tails(order, lo, links, holds, takes):
            far, first = list(takes), {}
            for j in reversed(order[lo:]):
                if qs[j] in first:
                    far[j] = max(far[j], holds[j] + far[first[qs[j]]])
                if qs[j]:
                    first[qs[j]] = j
                for i, d in links[j]:
                    if d + far[j] > far[i]:
                        far[i] = d + far[j]
            return far, {q: far[j] for q, j in first.items()}

        eager = [EAGER]

        def stretch(part_, ats, frees, fars):
            total = 0.0
            for (links, holds, takes), at, free, (far, first), weight in zip(paces, ats, frees, fars, WEIGHTS):
                free, early, end = dict(free), 0.0, 0.0
                for j in part_:
                    q = qs[j]
                    t = free.get(q, 0.0)
                    for i, d in links[j]:
                        if at[i] + d > t:
                            t = at[i] + d
                    at[j] = t
                    early += t
                    if t + far[j] > end:
                        end = t + far[j]
                    if q:
                        free[q] = t + holds[j]
                for q, x in first.items():
                    end = max(end, free.get(q, 0.0) + x)
                total += weight * (end + eager[0] * early / len(part_))
            return total

        def polish(order):
            seed, both = SEED, list(paces)
            for sweep in range(SWEEPS + AGAIN):
                paces[:] = both[:len(CLOCKS)] if sweep < SWEEPS else both[len(CLOCKS):]
                heat, eager[0] = HEAT * COOL ** sweep, EAGER * COOL ** sweep
                for lo in [0] + list(range(SPAN // 2 - sweep % 2 * (SPAN // 4), len(order) - 20 if sweep < SWEEPS else HEAD, SPAN // 2)):
                    ats = [clock(order, *p)[1] for p in paces]
                    order = sorted(order, key=lambda j: sum(at[j] for at in ats))
                    frees = [{qs[j]: at[j] + p[1][j] for j in order[:lo] if qs[j]} for p, at in zip(paces, ats)]
                    fars = [tails(order, lo + SPAN, *p) for p in paces]
                    mid = order[lo:lo + SPAN]
                    now = best = stretch(mid, ats, frees, fars)
                    keep = mid
                    for n in range(TRIES):
                        seed = (seed * 1103515245 + 12345) % 2147483648
                        a = (seed >> 8) % len(mid)
                        mine = [i for i in range(a + 1, min(len(mid), a + 60)) if qs[mid[i]] == qs[mid[a]]]
                        if not qs[mid[a]] or not mine:
                            continue
                        new = moved(mid, a, mine[(seed >> 18) % min(REACH, len(mine))], seed >> 28 & 1)
                        if new:
                            got = stretch(new, ats, frees, fars)
                            if got <= now + heat * (1.0 - n / TRIES) * ((seed >> 4) % 16) / 16.0:
                                mid, now = new, got
                                if got < best:
                                    best, keep = got, new
                    order = order[:lo] + keep + order[lo + SPAN:]
            PLAN["ends"] = [round(clock(order, *p)[0], 2) for p in paces]
            return clock(order, *paces[0])[1]
        if "start" not in PLAN:
            best = place(sorted(every, key=lambda j: (-way[j], j)), False)
            start = best
            for _ in range(PASSES):
                late = place(sorted(every, key=lambda j: (-start[j] - calls[j]["holds"], -j)), True)
                start = place(sorted(every, key=lambda j: (-late[j] - calls[j]["holds"], j)), False)
                if length(start) <= length(best):
                    best = start
            PLAN["start"] = polish(sorted(every, key=lambda j: (best[j], j))) if TRIES else best
        start = PLAN["start"]
        count, seen, facts, mark = {}, {q: {} for q in queue}, {}, {}

        def wait(q, sem, n):
            if seen[q].get(sem, 0) < n:
                queue[q].wait_ge(T.sem[sem], n)
                for k, x in list(facts.get((sem, n), {}).items()) + [(sem, n)]:
                    seen[q][k] = max(seen[q].get(k, 0), x)
        for j in sorted(range(len(calls)), key=lambda j: (start[j], j)):
            c = calls[j]
            if c["q"] is not None:
                need = {}
                for i in c["after"]:
                    if c["after"][i]:
                        need[calls[i]["sem"]] = max(need.get(calls[i]["sem"], 0), mark[i])
                for sem in sorted(need, key=lambda s: (s == "c" + c["q"], s)):
                    wait(c["q"], sem, need[sem])
                c["issue"]()
            mark[j] = count[c["sem"]] = count.get(c["sem"], 0) + c["inc"]
            facts[(c["sem"], mark[j])] = dict(seen.get(c["q"], {}))
        for sem in sorted(count):
            wait("g", sem, count[sem])

    def size(v):
        return len(range(v[1], v[2], v[3]))

    def narrow(*views):
        return 0.5 if all(SCRATCH[v[0]][2] in (BF, U16) for v in views) else 1.0

    def cols(buf, a=0, b=C):
        return buf, a, b, 1

    def piece(buf, h):
        return buf, CUT[h], CUT[h + 1], 1

    def part(off, a, z):
        return off[0], off[1] + a // 16, off[1] + z // 16, 1

    def ps(b, n=C, a=0):
        return "ps", 512 * b + a, 512 * b + a + n, 1

    def plane(buf, lane):
        return buf, lane, C, 16

    def lanes(buf, first):
        return buf, first, C, 4

    def dense(buf, w):
        return buf, 32 * w, 32 * w + 28, 1

    def col(i):
        return "col", i, i + 1, 1

    slots = {}

    def val(name):
        i = slots.setdefault(name, len(slots))
        return "cb", 28 * i, 28 * i + 28, 1

    def slot(i, j, buf="sc"):
        return buf, 112 * i + j, 112 * i + 112, 4

    def four(i, buf="sc"):
        return buf, 112 * i, 112 * i + 112, 1

    def number(s):
        return ap(s) if isinstance(s, tuple) else s

    def views(*more):
        return [s for s in more if isinstance(s, tuple)]

    def tt(out, a, b, o):
        op("v", lambda: V.tensor_tensor(ap(out), ap(a), ap(b), o), [a, b], [out], size(out) * (1 if b[0] == "ps" else 2))
        return out

    def ts(out, a, s1, o1, s2=None, o2=None):
        rest = (o1,) if o2 is None else (o1, o2)
        op("v", lambda: V.tensor_scalar(ap(out), ap(a), number(s1), number(s2), *rest), [a] + views(s1, s2), [out], size(out) * narrow(out, a))
        return out

    def scan(out, d0, d1, o0=A.mult, o1=A.add):
        op("v", lambda: V.tensor_tensor_scan(ap(out), ap(d0), ap(d1), 0.0, o0, o1), [d0, d1], [out], size(out))

    def turn(out, in_):
        op("v", lambda: V.transpose(ap(out), ap(in_)), [in_], [out], size(out) * narrow(out))

    def act(out, in_, scale, bias):
        if bias is None:
            return S.activation(ap(out), in_, ACT.Copy, scale=number(scale))
        return S.activation(ap(out), in_, ACT.Identity, bias=ap(bias), scale=number(scale))

    def copy(q, out, in_, scale=1.0, bias=None):
        if q == "v" and scale == 1.0:
            op("v", lambda: V.tensor_copy(ap(out), ap(in_)), [in_], [out], size(out) * narrow(out, in_))
        elif q == "v":
            ts(out, in_, scale, A.mult)
        elif q == "g":
            op("g", lambda: g.affine_select(ap(out), ap(in_), [[0, size(out)]], A.is_equal, 0.0, 0, 0), [in_], [out], 200 + 2 * size(out))
        else:
            op("s", lambda: act(out, ap(in_), scale, bias), [in_] + views(scale, bias), [out], max(SMIN, size(out)))

    def fill(v, x):
        copy("s", v, cols("ones", 0, size(v)), scale=x)

    def gather(q, out, win, off, scale=1.0, bias=None):
        reads, cycles = [win, off] + views(scale, bias), 70 + GATHER * size(out)
        if q == "s":
            op("s", lambda: act(out, ap(win).indirect(ap(off)), scale, bias), reads, [out], cycles)
        elif scale == 1.0:
            op("v", lambda: V.tensor_copy(ap(out), ap(win).indirect(ap(off))), reads, [out], cycles)
        else:
            op("v", lambda: V.tensor_scalar(ap(out), ap(win).indirect(ap(off)), number(scale), None, A.mult), reads, [out], cycles)

    def brought(name, win, off, line=None, scale=1.0, bias=None):
        a = 0
        for q, z in SHARE[name]:
            gather(q, cols(name, a, z), win, part(off, a, z), scale, bias)
            if line and q == "s":
                in_line(line)
            turn(cols(name + "T", a, z), cols(name, a, z))
            a = z

    def gather_add(out, win, off, other):
        op("v", lambda: V.tensor_tensor(ap(out), ap(win).indirect(ap(off)), ap(other), A.add), [win, off, other], [out], 60 + GATHER * size(out))

    def iota(v, pattern, base):
        op("g", lambda: g.iota(ap(v), pattern, base, 0, allow_small_or_imprecise_dtypes=True), [], [v], 160 + 2 * size(v))

    def mm(bank, l, ls, b, r, rs, a=0, z=C):
        l, ls, r, rs = cols(l, 128 * b, 128 * b + 128), cols(ls, 128 * b, 128 * b + 128), cols(r, a, z), cols(rs, a, z)
        op("t", lambda: g.tensor.matmul_mx(ap(ps(bank, z - a)), ap(l), ap(ls), ap(r), ap(rs), True, True), [l, ls, r, rs], [ps(bank)], PRODUCT * (z - a + 16))

    def quantize(out, scales, a, z, in_):
        o, s = cols(out, a, z), cols(scales, a, z)
        op("v", lambda: V.quantize_mx(ap(o), ap(s), ap(in_)), [in_], [o, s], 15 + 1.06 * (z - a))

    def quantize_piece(out, scales, tile, h):
        quantize(out, scales, CUT[h], CUT[h + 1], cols(tile, 4 * CUT[h], 4 * CUT[h + 1]))

    def swapped(buf, a, z, at):
        turn(cols("eb", at + 16, at + 16 + z - a), cols(buf, a, z))
        turn(cols(buf, 128 + a, 160 + z), cols("eb", at, at + 32 + z - a))

    def make_list(out, win, off):
        op("v", lambda: V.tensor_scalar(ap(out), ap(win).indirect(ap(off)), 512.0, 224.0, A.mult, A.add), [win, off], [out], 60 + GATHER * size(out))

    for what, qq, late in LOADS:
        if what == "t":
            dmas(qq, "ld_t", [(T.ti[:, 32 * i:32 * i + 28], T[k][:], [], [dense("ti", i)]) for i, k in enumerate(("up", "lf", "rt"))], LOCAL + late)
        elif what == "u":
            dmas(qq, "ld_u", [(T.ut[:], T.u[:], [], [cols("ut", 0, 512)])], LOCAL + late)
        else:
            v = cols("xt", 4 * CUT[what], 4 * CUT[what + 1])
            dmas(qq, "ld_x%d" % what, [(ap(v), T.x[:, v[1]:v[2]], [], [v])], LOCAL + late)
        in_line("loads" + qq)
    dmas("y", "ld_w", [(T.wq[:, 0:512].bitcast(dt.uint8), T.wc[:], [v], [cols("wq", 0, 512)]),
                       (T.wp[:, 0:512], T.ws[:], [], [cols("wp", 0, 512)])], LOCAL + 1.5)

    op("v", lambda: V.memset(T.ones[:, 0:512], 1.0), [], [cols("ones", 0, 512)], 256)
    op("g", lambda: g.iota(T.pidx[:, 0:2], [[0, 2]], 0, 1), [], [cols("pidx", 0, 2)], 160)
    for i in (1, 2):
        op("g", lambda i=i: g.iota(T.ti[:, 32 * i + 28:32 * i + 32], [[0, 4]], 0, 0), [], [cols("ti", 32 * i + 28, 32 * i + 32)], 170)
    iota(cols("i16", 0, 28), [[16, 28]], 0)
    iota(cols("lane", 0, 16), [[1, 16]], 0)
    iota(cols("i32", 0, 28), [[32, 14], [0, 2]], -224)
    iota(col(8), [[0, 1]], 224)
    iota(("ne", 3, 336, 4), [[0, 84]], 8)
    fill(cols("et", 0, 258), 0.0)
    fill(cols("et", 258, 516), 0.0)
    op("g", lambda: g.affine_select(T.et[:, 3:515:4], T.ones[:, 0:128], [[-1, 128]], A.is_equal, 0.0, 0, 1),
       [cols("ones", 0, 128)], [("et", 3, 515, 4)], 460)
    for v in (cols("eb", 0, 464), cols("wt"), cols("wq_", 0, 512), cols("dc", 0, 128), cols("dw", 0, 128), cols("sc", 0, 224), cols("sc", C, 952),
              cols("fin", 0, 336), cols("dd", 0, 336), cols("dd", 336, 672), cols("da1", 112, 128)):
        fill(v, 0.0)
    for v in (cols("di", 0, 160), cols("dt", 0, 160), cols("dr", 112, 128), cols("da0", 112, 128)):
        op("v", lambda v=v: V.memset(ap(v), 0.0), [], [v], size(v) / 2)
    fill(cols("qw", 2 * C, 2 * C + 264), -3.0)
    fill(cols("qw", 2 * C + 264, C + WIDE), -3.0)
    fill(cols("mc", 0, 336), -BIGV)
    fill(cols("st"), 2 * HUGE)
    for v, x in ((lanes("st", 2), -BIGV), (plane("st", 4), -BIGV), (plane("st", 8), -BIGV), (plane("st", 1), 10 * HUGE), (("w0", 0, 112, 4), 8.0), (col(29), 2 * HUGE)):
        op("g", lambda v=v, x=x: g.affine_select(ap(v), ap(cols("ones", 0, size(v))), [[0, size(v)]], A.is_gt, x, 0, 0), [cols("ones", 0, size(v))], [v], 200 + 2 * size(v))
    for i, (sh, m) in enumerate(((0, 1), (4, 1), (0, 15), (0, 31))):
        ts(cols("pidx", 2 + i, 3 + i), cols("pidx", 0, 1), sh, A.logical_shift_right, m, A.bitwise_and)
    copy("v", cols("col", 0, 4), cols("pidx", 2, 6))
    ts(slot(0, 3), ts(val("i1"), cols("i16", 0, 28), col(2), A.add, -448.0, A.add), UNIT, A.mult)
    nv = ts(cols("nn", 0, 28), cols("i32", 0, 28), col(3), A.add, UNIT, A.mult)
    tt(col(4), col(0), col(1), A.not_equal)
    ts(col(5), col(1), -30.0, A.mult, 159.0, A.add)
    ts(col(7), col(4), col(5), A.mult, col(2), A.add)
    ts(cols("offm", 0, 6), cols("i16", 0, 6), col(7), A.add)
    ts(col(13), col(1), -24.0, A.mult, 156.0, A.add)
    ts(col(11), col(2), 4.0, A.mult, 3.0, A.add)
    ts(col(12), col(4), col(13), A.mult, col(11), A.add)
    ts(cols("offa", 0, 2), cols("i16", 0, 2), 4.0, A.mult, col(12), A.add)
    ts(cols("lane", 0, 16), cols("lane", 0, 16), col(2), A.is_equal)

    def on(i):
        return "lane", i, i + 1, 1
    B1, B2, SD, BD = [col(16 + i) for i in range(4)]
    S1, S2 = on(16 + 4), on(16 + 8)
    copy("s", cols("lane", 16, 32), cols("lane", 0, 16), scale=-1.0)
    copy("s", cols("lane", 32, 48), cols("lane", 0, 16), scale=BIGV)
    copy("s", B1, ts(col(22), on(0), on(12), A.add, col(0), A.add), scale=-2 * HUGE)
    copy("s", col(23), on(0), scale=-BIGV)
    copy("s", B2, on(12), scale=-1.0e-30, bias=col(23))
    copy("s", col(27), col(0), scale=-1.0, bias=cols("ones", 0, 1))
    copy("s", SD, col(0), scale=1 / HUGE, bias=col(27))
    copy("s", BD, col(0), scale=-2.0)
    copy("s", cols("w1", C, 456), cols("ones", 0, 8), scale=on(32 + 4), bias=B1)
    copy("s", cols("w2", C, 456), cols("ones", 0, 8), scale=on(32 + 8), bias=B2)
    copy("s", col(28), on(1), scale=8 * HUGE, bias=on(32 + 4))
    copy("s", cols("urow", C, 456), cols("w2", C, 456), bias=col(28))
    copy("v", cols("offu", 0, 8), cols("i16", 0, 8))
    copy("s", ("w0", 3, 112, 4), nv)
    for b in range(4):
        quantize("eq", "es", 128 * b, 128 * b + 128, cols("et", 3 - b, 515 - b))
        in_line("start")

    quantize("u0", "s0", 0, 128, cols("ut", 0, 512))
    in_line("start")
    offu = cols("offu", 0, 8)
    op("v", lambda: V.tensor_copy(T.uq[:, 0:128].bitcast(dt.uint32), T.u0[:, 0:128].bitcast(dt.uint32).indirect(ap(offu))),
       [cols("u0", 0, 128), offu], [cols("uq", 0, 128)], 70 + GATHER * 128)
    op("s", lambda: S.activation(T.us[:, 0:128], T.s0[:, 0:128].indirect(ap(offu)), ACT.Copy), [cols("s0", 0, 128), offu], [cols("us", 0, 128)], 70 + GATHER * 128)
    for h in range(3):
        quantize_piece("q0", "qs0", "xt", h)
    ts(cols("di", 32, 96), cols("ti", 32, 96), -224.0, A.add, UNIT, A.mult)
    copy("v", cols("lb", 0, 64), cols("ti", 32, 96))
    swapped("di", 32, 96, 176)
    lv, rv = dense("dt", 1), dense("dt", 2)
    gather("v", cols("dt", 32, 96), cols("di", 0, 256), cols("offm", 2, 6))
    ts(slot(1, 2), dense("ti", 0), 448.0, A.is_equal)
    ts(slot(1, 3), dense("ti", 0), -224.0, A.add, UNIT, A.mult)
    scan(cols("dr", 0, 112), four(0), four(1))
    ts(cols("la0", 0, 28), ("dr", 3, 112, 4), 512.0, A.mult, 224.0, A.add)
    swapped("dr", 0, 128, 0)
    gather("s", ("da0", 3, 128, 4), cols("dr", 0, 288), cols("offa", 0, 2))

    def first_of(i, buf, own, order, steps, out):
        if i == 1:
            least = tt(slot(1, 0, "mc"), tt(val("m1"), own, plane(buf, 4), A.min), plane(buf, 8), A.min)
        else:
            scan(four(i // 2, "mo"), lanes(buf, 0), four(i // 2, "mc"), A.min, A.max)
            least = slot(i // 2, 3, "mo")
        for j, v in zip(order, (own, plane(buf, 4), plane(buf, 8))):
            tt(slot(i, j, "ne"), v, least, A.not_equal)
        scan(out, steps, four(i, "ne"), A.add, A.min)

    LB, LO, LI, LF = 12, 10, 3, 7
    from_inner, apart, inner, B = val("pc"), ("w0", 1, 112, 4), plane("wq_", LI), plane("wq_", LB)
    ll, lr, lc, laa = cols("lb", 0, 28), cols("lb", 32, 60), cols("lc", 0, 28), cols("lc", 32, 60)
    urow = cols("urow", 0, 456)

    for k in range(3):
        last = k == 2
        q, qs, aq, as_, al = "q%d" % k, "qs%d" % k, "aq%d" % k, "as%d" % k, cols("al%d" % k, 0, 28)
        dst = T.cores[(rank + STEP[k]) % N]
        la, la2 = cols("la%d" % k, 0, 28), cols("la%d" % (k + 1), 0, 28)
        pv, da = ("da%d" % (k % 2), 3, 112, 4), "da%d" % (1 - k % 2)
        side, side2 = val("side%d" % (k % 2)), val("side%d" % (1 - k % 2))
        tt(apart, lv, rv, A.subtract)
        tt(("w0", 2, 112, 4), rv, nv, A.subtract)
        tt(("sc", 897, 952, 2), nv, pv, A.subtract)
        copy("g", ("sc", 786, 868, 3), pv)
        copy("g", plane("wq_", LF), pv)
        for lane, v in ((3, lv), (13, rv), (9, apart), (7, pv)):
            if k == 0 and lane != 9:
                win, off = (cols("dr", 0, 288), cols("offa", 0, 2)) if lane == 7 else (cols("di", 0, 256), cols("offm", 2 if lane == 3 else 4, 4 if lane == 3 else 6))
                gather("s", ("st", lane, 512, 16), win, off, HUGE, col(29))
            elif CODED == "s" and k:
                copy("s", plane("st", lane), v, scale=HUGE, bias=col(29))
            else:
                ts(plane("st", lane), v, 2.0, A.add, HUGE, A.mult)
        for a in (0, C // 2):
            turn(cols("srow", a, a + C // 2), cols("st", a, a + C // 2))
        exchange(dst, "arq%d" % k, [(T[aq][:, 0:C].bitcast(dt.uint8), T[q][:, 0:C].bitcast(dt.uint8), cols(q)),
                                    (T[as_][:, 0:C], T[qs][:, 0:C], cols(qs))], [cols(aq), cols(as_)], LONG + (FIRST if k == 0 else 0))
        for h, (bank, other) in enumerate(((0, 6), (7, 1), (5, 2))):
            n = CUT[h + 1] - CUT[h]
            mm(other, "uq", "us", 0, q, qs, CUT[h], CUT[h + 1])
            in_line("layer")
            copy("s", piece("w1", h), ps(other, n), scale=S1, bias=B1)
            mm(bank, "uq", "us", 0, q, qs, CUT[h], CUT[h + 1])
            in_line("layer")
            tt(piece("mrow", h), piece("srow", h), ps(bank, n), A.max)
        if WHOLE:
            mm(3, "uq", "us", 0, q, qs)
            copy("s", cols("w2"), ps(3), scale=S2, bias=B2)
        else:
            for h, other in enumerate((6, 1, 2)):
                copy("s", piece("w2", h), ps(other, CUT[h + 1] - CUT[h]), scale=S2, bias=B2)
        for b in (3, 2, 0, 1):
            mm(1 + b, "eq", "es", b, q, qs)
        for a, z in zip(LCUT, LCUT[1:]):
            gather_add(cols("lrow", a, z), cols("w1", 0, 456), part(ll, a, z), cols("mrow", a, z))
        for a, z in zip(RCUT, RCUT[1:]):
            gather_add(cols("urow", a, z), cols("w2", 0, 456), part(lr, a, z), cols("lrow", a, z))
            turn(cols("gT", a, z), cols("urow", a, z))
        brought("sa", cols("mrow"), la, scale=SD, bias=BD)
        brought("ul", urow, ll, scale=SD)
        brought("ur", urow, lr, scale=SD)
        for b in range(4):
            if XV[b]:
                copy("s", cols("fo%d" % b, 0, XV[b]), ps(1 + b, XV[b]))
        ppv = plane("saT", 7)
        copy("g", dense("dc", 1), ppv)
        up = tt(("sc", 953, 1008, 2), ppv, pv, A.subtract)
        ts(("sc", 952, 1008, 2), up, 0.0, A.is_equal)
        scan(("sc", 449, 560, 2), cols("sc", 896, 952), cols("sc", 952, 1008))
        if k == 0:
            tt(side, plane("saT", 3), nv, A.not_equal)
        tt(inner, rv, tt(val("d6"), side, apart, A.mult), A.add)
        tt(from_inner, pv, inner, A.subtract)
        v0 = tt(slot(0, 0, "mc"), plane("saT", 2), plane("gT", 2), A.subtract)
        first_of(0, "gT", v0, (2, 0, 1), cols("w0", 0, 112), four(0, "so"))
        child = tt(dense("dc", 0), slot(0, 1, "so"), rv, A.add)
        swapped("dc", 0, 64, 288)
        make_list(cols("lc", 0, 64), cols("dc", 0, 224), cols("offm", 0, 4))
        tt(plane("ulT", 5), slot(0, 3, "so"), plane("ulT", 3), A.subtract)
        first_of(1, "ulT", slot(0, 3, "mo"), (0, 1, 2), lanes("ulT", 1), four(1, "so"))
        tt(plane("urT", 5), slot(1, 3, "so"), plane("urT", 3), A.subtract)
        first_of(2, "urT", slot(1, 0, "mc"), (0, 1, 2), lanes("urT", 1), lanes("wq_", 0))
        turn(cols("qw", C, 2 * C), cols("wq_"))
        turn(cols("qy"), cols("wq_", LB - LO, C + LB - LO))
        turn(cols("eb", 400, 432), ("wq_", LB, 512, 16))
        copy("g", dense("dw", 0), B)
        turn(cols("dw", 128, 192), cols("eb", 384, 448))
        make_list(cols("lw", 0, 32), cols("dw", 0, 192), cols("offm", 0, 2))
        gather_add(cols("qw"), cols("qw", C, 2 * C), la, cols("qy"))
        turn(cols("qwT"), cols("qw"))
        brought("qc", cols("qw", C, C + WIDE), lc)
        brought("g2", cols("qw"), laa, line="gap")

        def unpack(b):
            mm(FBANK[b], "eq", "es", b, aq, as_)
            copy("s", cols("fp%d" % b), ps(FBANK[b]))
            in_line("gap")
            if KV[b]:
                fp, fq = cols("fp%d" % b, 0, KV[b]), cols("fq", C * b, C * b + KV[b])
                if TWINS[b] == "y":
                    dmas("y", "cf%d" % b, [(ap(fq), ap(fp), [fp], [fq])], TWIN)
                else:
                    copy(TWINS[b], fq, fp if TWINS[b] == "g" else ps(FBANK[b], KV[b]))
                    in_line("writes" if TWINS[b] == "g" else "gap")
        for b in FSOON:
            unpack(b)
        b1, b2, b3 = plane("qwT", LB), plane("g2T", LO), plane("g2T", LB)
        e01 = tt(("sc", 673, 756, 3), B, b1, A.is_equal)
        e12 = tt(slot(4, 2), b1, b2, A.is_equal)
        tt(slot(4, 1), b2, b3, A.is_equal)
        tt(("sc", 784, 868, 3), tt(val("c1"), B, child, A.is_equal), tt(val("c2"), plane("qcT", LB), child, A.is_equal), A.mult)
        tt(("sc", 674, 756, 3), B, pv, A.subtract)
        scan(("fin", 1, 336, 4), cols("sc", 672, 756), cols("sc", 784, 868))
        sinks = ("fin", 5, 336, 12)
        r1 = tt(("fin", 3, 336, 12), tt(val("x0"), B, nv, A.is_equal), e01, A.mult)
        within = tt(val("w2"), plane("qwT", LI), nv, A.is_equal)
        tt(("fin", 0, 336, 12), tt(val("w1"), b1, pv, A.is_equal), within, A.mult)
        scan(cols(da, 0, 112), four(4), ("fin", 0, 336, 3))
        swapped(da, 0, 128, 0)
        make_list(cols(la2[0], 0, 32), cols(da, 0, 288), cols("offa", 0, 2))
        exchange(dst, "arl%d" % k, [(ap(al), ap(la2), la2)], [al], SHORT)
        brought("qz", cols("qw", 0, WIDE), cols("lw", 0, 28), line="gap")
        left = tt(val("s4"), side, tt(val("s2"), sinks, tt(val("s1"), B, inner, A.not_equal), A.mult), A.not_equal)
        tt(("fin", 11, 336, 12), tt(val("rot"), r1, e12, A.mult), from_inner, A.mult)
        tt(("dd", 1, 56, 2), plane("qcT", LI), B, A.subtract)
        scan(cols("dd", 56, 112), cols("dd", 0, 56), ("fin", 5, 336, 6))
        D = ("dd", 57, 112, 2)
        tt(("dd", 169, 224, 2), D, tt(("dd", 113, 168, 2), D, left, A.mult), A.subtract)
        above = plane("qzT", LF - LB + LO)
        tt(("dd", 336, 420, 3), B, above, A.subtract)
        tt(("dd", 421, 504, 3), plane("qzT", LO), B, A.is_equal)
        tt(("dd", 422, 504, 3), plane("qzT", LB), B, A.is_equal)
        scan(("dd", 504, 672, 2), cols("dd", 420, 504), cols("dd", 336, 420))
        for i, v in enumerate((lv, rv)):
            tt(("dd", 112 + 56 * i, 168 + 56 * i, 2), above, v, A.is_equal)
            scan(cols("dd", 224 + 56 * i, 280 + 56 * i), ("dd", 505, 672, 3), cols("dd", 112 + 56 * i, 168 + 56 * i))
            tt(v, v, ("dd", 225 + 56 * i, 280 + 56 * i, 2), A.add)
        if last:
            pv = (da, 3, 112, 4)
            e = tt(val("f0"), pv, nv, A.is_equal)
            e = tt(val("f2"), e, ts(val("f1"), nv, -1.0, A.mult, NONE, A.add), A.mult)
            tt(plane("wt", 0), pv, e, A.add)
            copy("g", plane("wt", 1), lv)
            copy("g", plane("wt", 2), rv)
            turn(cols("trow"), cols("wt"))
            copy("s", cols("trf"), cols("trow"), scale=512.0, bias=col(8))
            dmas("y", "st_tr", [(T.tr[:, C * i:C * i + C], T.trf[i:128:16, :], [cols("trf")], []) for i in range(3)])
        else:
            tt(side2, left, tt(val("s3"), (da, 2, 112, 4), within, A.mult), A.not_equal)
            swapped("dt", 32, 96, 176)
            make_list(cols("lb", 0, 64), cols("dt", 0, 256), cols("offm", 2, 6))
        for b in FLATE:
            unpack(b)
        kb = [cols("kb", C * b, C * b + C) for b in range(4)]
        for b in (0, 1, 3, 2):
            x = KV[b]
            if x:
                gather_add(cols("kb", C * b, C * b + x), cols("fp%d" % b), part(al, 0, x), cols("fq", C * b, C * b + x))
                in_line("sums")
            if x < C:
                gather("s", cols("kg%d" % b, x, C), cols("fp%d" % b), part(al, x, C))
                in_line("gap")
                tt(cols("kb", C * b + x, C * b + C), cols("kg%d" % b, x, C), ps(FBANK[b], C - x, x), A.add)
                in_line("sums")
        if k == 0:
            dmas("y", "ld_v", [(T.vt[:], T.v[:], [cols("kb", 0, 1)], [cols("vt", 0, 512)])])
        for b in range(4):
            a = 0
            for qq, z in ZSHARE[b]:
                gather(qq, ("zt", 4 * a + b, 4 * z, 4), kb[b], part(al, a, z), 0.5)
                a = z
        for h, bank in enumerate((1, 5, 0)):
            quantize_piece("zq", "zs", "zt", h)
            mm(bank, "wq", "wp", 0, "zq", "zs", CUT[h], CUT[h + 1])
            in_line("layer")
            copy(RQ[h], piece("rr0", h), ps(bank, CUT[h + 1] - CUT[h]), scale=0.03125)
            if h == 1:
                mm(2, "wq", "wp", RORDER[0], "zq", "zs", 0, CUT[2])
                in_line("layer")
                copy("s", cols("rr%d" % RORDER[0], 0, CUT[2]), ps(2, CUT[2]), scale=0.03125)
                in_line("state")
        for b, bank in zip(RORDER, (6, 7, 1)):
            a = CUT[2] if b == RORDER[0] else 0
            mm(bank, "wq", "wp", b, "zq", "zs", a, C)
            in_line("layer")
            copy(RQ2[b], cols("rr%d" % b, a, C), ps(bank, C - a), scale=0.03125)
            if RQ2[b] == "s":
                in_line("state")
        steps = []
        for b in (0,) + RORDER:
            cut = sorted({0, XV[b], C} | (set(CUT) if last and b >= 2 or XV[b] < C else set()))
            steps += [(a if last else 0, z > XV[b], b, a, z) for a, z in zip(cut, cut[1:])]
            if XV[b] < C and not last:
                gather("s", cols("xg%d" % b, XV[b], C), cols("rr%d" % b), part(la2, XV[b], C))
                in_line("state")
        steps += [(CUT[h + 1] + (h < 2) if last else C, 2, h, 0, 0) for h in range(3)]
        for _, how, b, a, z in sorted(steps, key=lambda s: s[:2] + (((0,) + RORDER).index(s[2]) if s[1] < 2 else s[2],) + s[3:]):
            if how == 2:
                quantize_piece("q%d" % (k + 1), "qs%d" % (k + 1), "xn", b)
            elif how:
                if last:
                    gather("s", cols("xg%d" % b, a, z), cols("rr%d" % b), part(la2, a, z))
                    in_line("state")
                tt(("xn", 4 * a + b, 4 * z, 4), cols("xg%d" % b, a, z), ps(1 + b, z - a, a), A.add)
            else:
                gather_add(("xn", 4 * a + b, 4 * z, 4), cols("rr%d" % b), part(la2, a, z), cols("fo%d" % b, a, z))
            if last or not how:
                in_line("turns")

    quantize("vq", "vs", 0, 128, cols("vt", 0, 512))
    for h in range(3):
        a, z = CUT[h], CUT[h + 1]
        mm(5 + h, "vq", "vs", 0, "q3", "qs3", a, z)
        copy("svv"[h], cols("yt", a, z), ps(5 + h, z - a))
        dmas("s", "st_y%d" % h, [(T.y[:, a:z], T.yt[:, a:z], [cols("yt", a, z)], [])], LOCAL + 0.5)
        dmas("y", "st_oc%d" % h, [(T.oc[:, 4 * a:4 * z], T.q3[:, a:z].bitcast(dt.uint8), [cols("q3", a, z)], [])], LOCAL + 0.5)
    dmas("y", "st_sc", [(T.osc[4 * i:4 * i + 4, :], T.qs3[32 * i:32 * i + 4, 0:C], [cols("qs3")], []) for i in range(4)])
    issue_all()
